import numpy as np, ml_dtypes
CORES = [5,29,101,125,133,157,229,253]
N = 8
BF = ml_dtypes.bfloat16
S, F, L, RO, A, TH, BYG = 2048, 624, 208, 3, 544, 9, 0
def whole(x, hi):
    return np.minimum(x.astype(np.int64), hi)
def parts(rng):
    a = rng.choice(np.array([0.2, 0.3, 0.4, 0.5]), (N, 8, 1, 1)).astype(np.float32)
    t = whole(256 * rng.random((N, 8, 16, S), dtype=np.float32) ** a, 255)
    t = np.where(rng.random((N, 8, 1, S)) < 0.25, 255, t)
    return t, rng.integers(0, 255, (N, 8, 16, F)), rng.integers(0, S, (N, 8, 16, F)), rng.integers(0, S, (N, 8, 16, F))
def pack(t, z, eh, ef):
    return {"tab": t.reshape(N, 128, S).astype(np.float32).astype(BF), "zf": z.reshape(N, 128, F).astype(np.float32).astype(BF),
            "eh": np.ascontiguousarray(eh.reshape(N, 128, F)).astype(np.int32), "ef": np.ascontiguousarray(ef.reshape(N, 128, F)).astype(np.int32)}
def setup_inputs(rng):
    return pack(*parts(rng))
def setup_inputs_full(rng):
    t, z, eh, ef = parts(rng)
    for g in (0, 5):
        t[:, g] = 255; eh[:, g] = rng.integers(F, S, (N, 16, F)); ef[:, g] = rng.integers(F, S, (N, 16, F))
        eh[:, g, 0] = np.argsort(rng.random((N, F)), axis=1)
    f = np.arange(F); c = F - A; see = (f >= A - c) & (f < A)
    m = np.flatnonzero(see)
    for g in (2, 7):
        p = np.argsort(rng.random((N, S // 2)), axis=1)[:, :L]
        t[:, g] = 255; eh[:, g] = rng.integers(S // 2, S - 64, (N, 16, F)); ef[:, g] = rng.integers(S // 2, S - 64, (N, 16, F))
        z[:, g] = np.where(f < L, rng.integers(160, 255, (N, 16, F)), np.where(see, rng.integers(100, 160, (N, 16, F)), rng.integers(0, 100, (N, 16, F))))
        eh[:, g, 0] = np.where(see, eh[:, g, 0], p[:, f % L])
        for r in range(N):
            q = (r + 1 + (2 + BYG * g) % (N - 1)) % N
            a, b = m[1::4], m[3::4]
            ef[r, g, rng.integers(0, 16, len(a)), a] = p[q, L - c - 1]
            ef[r, g, rng.integers(0, 16, len(b)), b] = np.max(p[q])
    return pack(t, z, eh, ef)
def setup_inputs_ties(rng):
    t, z, eh, ef = parts(rng)
    pat = np.array([0, 0, 2, 3, 5, TH - 2, TH - 2, TH - 2, TH - 1, TH - 1, TH - 1, TH - 1, TH, TH, TH, 16])
    place = np.argsort(rng.random((N, 4, 16, S), dtype=np.float32), axis=2)
    t[:, :4] = np.where(place < pat[np.arange(S) % 16], 0, 255)
    for x in (eh, ef):
        top = rng.choice(np.array([8, 12, 12, 12, 15, 16]), (N, 4, 1, F))
        x[:, :4] = 16 * rng.integers(0, S // 16, (N, 4, 16, F)) + (rng.random((N, 4, 16, F)) * top).astype(np.int64)
    v = np.array([0, 1, 127, 128, 254, 255])
    t[:, 4:] = rng.choice(v, (N, 4, 16, S), p=[0.04, 0.04, 0.1, 0.12, 0.3, 0.4]); z[:, 4:] = rng.choice(v[:5], (N, 4, 16, F))
    return pack(t, z, eh, ef)
def setup_inputs_alike(rng):
    t, z, eh, ef = parts(rng); few = np.array([0, S - 1, S // 2, 3])
    eh[:, 0] = rng.choice(few, (N, 16, F)); eh[:, 1] = rng.integers(0, S, (N, 1, F))
    t[:, 2] = 255; eh[:, 2] = rng.integers(0, S, (N, 1, 1))
    eh[:, 3] = S - 1 - rng.integers(0, 12, (N, 16, F)); ef[:, 3] = S - 1 - rng.integers(0, 12, (N, 16, F))
    ef[:, 4] = rng.choice(few, (N, 16, F))
    for x in (z, eh, ef): x[:, 5, :, 1::2] = x[:, 5, :, 0::2]
    return pack(t, z, eh, ef)
def setup_inputs_hard(rng):
    t, z, eh, ef = parts(rng)
    t[:, 0] = 0; t[rng.integers(0, N), 1] = 0; t[:, 2] = 255
    z[:, 3] = 0; t[:, 3] = np.maximum(t[:, 3], 1)
    z[:, 4] = 254; t[:, 4] = np.where(rng.random((N, 16, S)) < 0.8, 255, t[:, 4])
    return pack(t, z, eh, ef)
def setup_inputs_spread(rng):
    u = np.float32(2) ** -rng.integers(-2, 6, (N, 8, 1, S)).astype(np.float32); v = np.float32(2) ** rng.integers(-2, 5, (N, 8, 1, F)).astype(np.float32)
    t = whole(256 * rng.random((N, 8, 16, S), dtype=np.float32) ** u, 255); z = whole(255 * rng.random((N, 8, 16, F), dtype=np.float32) ** v, 254)
    e = [whole(S * rng.random((N, 8, 16, F)) ** (2.0 ** rng.integers(0, 3, (N, 8, 16, 1))), S - 1) for i in range(2)]
    return pack(t, z, e[0], e[1])
def check_inputs(d):
    bad = []
    for k, hi in (("tab", 255), ("zf", 254), ("eh", S - 1), ("ef", S - 1)):
        v = np.asarray(d[k]).astype(np.float64)
        if not (np.min(v) >= 0 and np.max(v) <= hi): bad.append("range of " + k)
        if not np.all(v == np.floor(v)): bad.append("whole numbers in " + k)
    return bad
def reference(tab, zf, eh, ef):
    t = tab.astype(np.float32).astype(np.int32).reshape(N, 8, 16, S); z = zf.astype(np.float32).astype(np.int32).reshape(N, 8, 16, F)
    home = eh.astype(np.int64).reshape(N, 8, 16, F); far = ef.astype(np.int64).reshape(N, 8, 16, F)
    d = np.zeros((N, 8, F), np.int64); oc = np.full((N, 8, S), -1, np.int64); free = np.ones((N, 8, F), bool)
    for step in range(RO):
        old = np.array(t)
        turn = (np.arange(F) + A * step) % F
        for r in range(N):
            for g in range(8):
                q = (r + 1 + (step + BYG * g) % (N - 1)) % N
                ln = turn[free[r, g][turn]][:L]
                zl = z[r, g][:, ln]
                sh = (home[r, g][:, ln] + d[r, g, ln]) & (S - 1); sf = (far[r, g][:, ln] + d[r, g, ln]) & (S - 1)
                ph = np.sum(old[r, g][:, sh] <= zl[:, None, :], axis=0); pf = np.sum(old[q, g][:, sf] <= zl[:, None, :], axis=0)
                k = np.argmax(ph, axis=0)
                worst = np.maximum(np.max(ph, axis=0), np.max(pf, axis=0)); go = worst < TH
                d[r, g, ln] += np.where(go, 0, worst)
                cl = np.flatnonzero(go)
                s, first = np.unique(sh[k, np.arange(L)][cl], return_index=True)
                w = cl[first]; was = oc[r, g, s]; was = was[was >= 0]
                d[r, g, was] += 1; free[r, g, was] = True
                t[r, g][:, s] = zl[:, w]; oc[r, g, s] = ln[w]; free[r, g, ln[w]] = False
    return {"yt": t.reshape(N, 128, S).astype(np.float32).astype(BF), "yo": oc.astype(np.float32), "yd": d.astype(np.float32)}

@@ -1,0 +1,674 @@
+import math
+from concourse.mybir import AluOpType, ActivationFunctionType
+OP = AluOpType
+AF = ActivationFunctionType
+F32, BF, I32, U16 = "float32", "bfloat16", "int32", "uint16"
+F, L, S = 624, 208, 2048
+WT = S + 3 * 256
+PEN = 32768
+OKB = 8 * PEN
+NB = 112
+LN2 = math.log(2.0)
+LAG, SLACK = 0.1, 0.05
+
+ENG = "VAPG"
+LOADS = ["ef0", "eh0", "zf0", "tab", "tc", "ef1", "eh1", "zf1"]
+MSGS = ["RQZ", "RQL", "KFR", "F2", "F3", "U2Z", "U2D", "U3Z", "U3D", "V3Z", "V3D"]
+TO = {"RQZ": 1, "RQL": 1, "KFR": -1, "F2": -2, "U2Z": -2, "U2D": -2, "F3": -3, "U3Z": -3, "U3D": -3, "V3Z": -3, "V3D": -3}
+ORDER = ["RQZ", "U3Z", "RQL", "F3", "KFR", "U3D", "V3Z", "V3D"]
+TABLES = ("F2", "F3")
+STORES = ["yt", "yo", "yd"]
+SEMAPHORES = (["q" + e for e in ENG] + ["d_" + n for n in LOADS] + ["o_" + n for n in STORES]
+              + ["a_" + n for n in MSGS] + ["l_" + n for n in MSGS])
+
+SCRATCH = {}
+PLACE = {}
+_fill = {F32: 0, BF: 0, I32: 0, U16: 0}
+
+
+def _sb(name, shape, dtype):
+    if len(shape) == 1 and shape[0] <= 48 and name not in MSGS + ["KFO", "DT0", "DT1"]:
+        PLACE[name] = ("S" + dtype, _fill[dtype], shape[0])
+        _fill[dtype] += -(-shape[0] // 16) * 16
+        return
+    SCRATCH[name] = ("sbuf", [128] + shape, dtype)
+    PLACE[name] = (name, 0, shape[0])
+
+
+for _n, _s, _d in (
+        ("HT", [WT], BF), ("F2", [WT], BF), ("F3", [WT], BF), ("TC", [S], BF), ("OC", [WT], F32),
+        ("ZF", [F], BF), ("EHI", [F], I32), ("EFI", [F], I32), ("EE", [F], F32), ("D", [F], BF), ("DF", [F], F32),
+        ("XE", [128], F32), ("DQ", [128], F32), ("I3", [13, 32], F32), ("Y3", [13, 32], F32), ("XI", [13, 16], I32),
+        ("HF", [2, L], I32), ("GA0", [512], BF), ("GA1", [512], BF), ("GA2", [512], BF),
+        ("CMH", [3328], BF), ("CMF", [3328], BF), ("ZR", [13, 256], BF),
+        ("RQZ", [L], BF), ("RQL", [L], U16), ("KFR", [16], F32), ("KFO", [16], F32),
+        ("U2Z", [L], BF), ("U2D", [16], U16), ("U3Z", [L], BF), ("U3D", [16], U16), ("V3Z", [L], BF), ("V3D", [16], U16),
+        ("HK", [L], F32), ("HS", [L], F32), ("FS", [L], F32), ("HKI", [16], I32), ("HSL", [16], I32), ("A1", [16], F32),
+        ("AP", [16], F32), ("YY", [16], F32), ("IX", [16], U16), ("D0", [16], F32), ("L1", [16], F32), ("D2", [16], F32),
+        ("WM", [16], F32), ("WI", [16], I32), ("WS", [16], I32), ("WR", [16], F32), ("WV", [16], F32), ("WN", [16], F32),
+        ("XB", [L], BF), ("B0", [L], BF), ("B1", [L], BF), ("E0", [13, 128], BF), ("E1", [6, 128], BF),
+        ("NU", [32], F32), ("UU", [32], BF), ("UC", [32], BF), ("QQ", [32], F32), ("TB", [1], F32), ("TU", [1], F32),
+        ("XM", [128], F32), ("XS", [128], F32), ("LVF", [1024], F32), ("LVW", [1024], F32), ("UF", [336], BF),
+        ("GW", [336], BF), ("BP", [336], BF), ("NB1", [L], F32), ("B2", [336], BF), ("B3", [L], F32), ("DL", [128], F32),
+        ("ND", [128], F32),
+        ("PI", [1], I32), ("PJ", [1], I32), ("PK", [1], I32), ("PM", [1], F32), ("MH0", [1], F32), ("MH1", [1], F32),
+        ("PW", [1], F32), ("PX", [1], I32), ("PY", [1], F32), ("ML", [4], F32), ("MH", [4], F32), ("MB", [2], F32),
+        ("KIO", [L], F32), ("M16", [L], F32), ("RKM", [L], F32), ("KAD", [L], F32), ("C16", [32], F32), ("FW", [32], F32),
+        ("DMF", [32], F32), ("ONB", [128], BF), ("BA", [128], BF), ("BO", [128], BF), ("NBO", [128], BF), ("NT", [128], BF),
+        ("ID", [128], BF), ("WMU", [144], BF), ("EX0", [16], F32), ("EX1", [16], F32), ("W0", [16], BF), ("W1", [16], BF),
+        ("THR", [1], F32), ("CL", [264], F32), ("CI", [264], I32), ("CJ", [264], I32), ("CB", [264], F32),
+        ("LB", [2, 256], BF), ("HB", [2, 8], F32), ("CT0", [S + 64], BF), ("CT1", [S + 64], BF),
+        ("F2V", [416], F32), ("L128", [128], F32), ("BLF", [16], F32), ("BL", [16], U16), ("ON32", [32], F32),
+):
+    _sb(_n, _s, _d)
+for _t in range(3):
+    for _n, _s, _d in (("LI", [2, L], U16), ("KA", [L], F32), ("ZL", [L], BF), ("Z16", [13, 256], BF),
+                       ("DU", [16], F32), ("DS", [16], F32), ("DT", [16], U16), ("LW", [80 + 1024], F32),
+                       ("PL", [32], U16), ("LU", [16], U16)):
+        if not (_t == 0 and _n in ("ZL", "LW", "PL", "LU")):
+            _sb("%s%d" % (_n, _t), _s, _d)
+for _d, _w in _fill.items():
+    SCRATCH["S" + _d] = ("sbuf", [128, _w], _d)
+for _n in ["PH", "PF"] + ["T%d" % i for i in range(6)]:
+    SCRATCH[_n] = ("psum", [128, 512], F32)
+    PLACE[_n] = (_n, 0, 512)
+
+
+def plan(T, topo):
+    n = len(T.cores)
+    out = {}
+    for r in range(n):
+        src = T.cores[r]
+        for m in MSGS:
+            dst = T.cores[(r + TO[m]) % n]
+            relay = None
+            if not topo.may_write(src, dst):
+                c = [x for x in topo.cores_of(src) if x != src and topo.may_write(x, dst) and topo.die(x) == topo.die(src)]
+                relay = c[0] if m == "F3" else c[-1]
+            out[(r, m)] = (src, relay, dst)
+    return out
+
+
+def engines(topo, a, b, m):
+    e = topo.engines(a, b)
+    if m in TABLES:
+        return e[:4] if len(e) == 8 else e[8:12]
+    return e[4:8]
+
+
+def bits(e):
+    return sum(1 << x for x in e)
+
+
+def land(T, m):
+    return T[m][:, 0:S] if m in TABLES else T[m][:, :]
+
+
+def relay_program(g, core, T, topo, pl):
+    todo = sorted((ORDER.index(m), m, r) for (r, m), (s, y, d) in pl.items() if y == core)
+    for _, m, r in todo:
+        s, y, d = pl[(r, m)]
+        g.wait_ge(T.sem["a_" + m], len(engines(topo, s, y, m)))
+        rid, pid = topo.addr(d, y)
+        g.remote_dma(land(T, m), land(T, m), T.sem["a_" + m], T.sem["l_" + m], pid, rid, bits(engines(topo, y, d, m)))
+    for _, m, r in todo:
+        s, y, d = pl[(r, m)]
+        g.wait_ge(T.sem["l_" + m], len(engines(topo, y, d, m)))
+
+
+def rank_program(g, core, T, topo):
+    pl = plan(T, topo)
+    rank = T.rank_of(core)
+    if rank is None:
+        return relay_program(g, core, T, topo, pl)
+    Q = {"V": g.vector, "A": g.scalar, "P": g.tensor, "G": g, "S": g.sync}
+    cnt = {}
+    know = {e: {} for e in Q}
+    know["net"] = {}
+    hist = {}
+
+    def b(name, lo=0, hi=None, step=1, p=(0, 128)):
+        name, first, width = PLACE[name]
+        hi = first + (width if hi is None else hi)
+        lo += first
+        ap = T[name][p[0]:p[1], lo:hi] if step == 1 else T[name][p[0]:p[1], lo:hi:step]
+        return (ap, name, (0, 1, lo, hi), None, -(-(hi - lo) // step))
+
+    def b3(name, c0, c1, lo, hi, p=(0, 128)):
+        return (T[name][p[0]:p[1], c0:c1, lo:hi], name, (c0, c1, lo, hi), None, (c1 - c0) * (hi - lo))
+
+    def b2(name, c, lo, hi, p=(0, 128)):
+        return (T[name][p[0]:p[1], c, lo:hi], name, (c, c + 1, lo, hi), None, hi - lo)
+
+    def ind(win, off):
+        return (win[0].indirect(off[0]), win[1], win[2], off, 16 * off[4])
+
+    def hits(x, y):
+        return x[0] < y[1] and y[0] < x[1] and x[2] < y[3] and y[2] < x[3]
+
+    def inside(x, y):
+        return x[0] >= y[0] and x[1] <= y[1] and x[2] >= y[2] and x[3] <= y[3]
+
+    def regions(ops):
+        return [(o[1], o[2], SCRATCH[o[1]][0] == "psum") for o in ops if isinstance(o, tuple)]
+
+    def offsets(ops):
+        return [o[3] for o in ops if isinstance(o, tuple) and o[3]]
+
+    def sync(e, reads, writes):
+        deps = {}
+        for w, lst in ((False, reads), (True, writes)):
+            for name, reg, psum in lst:
+                for (r2, w2, e2, sem, count, snap) in hist.get(name, []):
+                    if not (psum and e2 != e):
+                        if not (w or w2) or not hits(reg, r2):
+                            continue
+                        if e2 == e and (e == "P" or not w2) and e in ENG:
+                            continue
+                    if deps.get(sem, (0, None))[0] < count:
+                        deps[sem] = (count, snap)
+        k = know[e]
+        for sem in sorted(deps, key=lambda x: -len(deps[x][1])):
+            count, snap = deps[sem]
+            if k.get(sem, 0) < count:
+                Q[e].wait_ge(T.sem[sem], count)
+                k[sem] = count
+                for s2, v in snap.items():
+                    if k.get(s2, 0) < v:
+                        k[s2] = v
+
+    def note(e, reads, writes, sem, n):
+        cnt[sem] = cnt.get(sem, 0) + n
+        snap = dict(know[e])
+        for w, lst in ((False, reads), (True, writes)):
+            for name, reg, psum in lst:
+                keep = [x for x in hist.get(name, [])
+                        if not (inside(x[0], reg) and (w or (not x[1] and x[2] == e and x[3] == sem)))]
+                hist[name] = keep + [(reg, w, e, sem, cnt[sem], snap)]
+
+    def emit(e, f, out, ins):
+        reads, writes = regions(ins + offsets(ins + [out])), regions([out])
+        sync(e, reads, writes)
+        f(Q[e]).then_inc(T.sem["q" + e], 1)
+        note(e, reads, writes, "q" + e, 1)
+
+    nodes, seen, group = [], {}, []
+
+    def node(e, run, reads, writes, dur, lat=0.0, after=None):
+        k, before = len(nodes), {}
+        if after is not None:
+            before[after] = 1
+        for w, lst in ((False, reads), (True, writes)):
+            for name, reg, psum in lst:
+                for (r2, w2, j) in seen.get(name, []):
+                    if nodes[j][0] == e == "P" and psum:
+                        if hits(reg, r2):
+                            before.setdefault(j, 0)
+                    elif (psum and nodes[j][0] != e) or ((w or w2) and hits(reg, r2)):
+                        before[j] = max(before.get(j, 0), 1 if w2 or nodes[j][0] != e else 0)
+        for w, lst in ((False, reads), (True, writes)):
+            for name, reg, psum in lst:
+                keep = [x for x in seen.get(name, []) if not (w and inside(x[0], reg) and not psum)]
+                seen[name] = keep + [(reg, w, k)]
+        nodes.append((e, run, dur, lat, sorted(before.items())))
+        return k
+
+    def op(e, f, out, ins, after=None):
+        win = [x for x in ins if isinstance(x, tuple) and x[3]]
+        c = 0.00083 * max(x[4] for x in ins + [out] if isinstance(x, tuple))
+        if e == "G":
+            dur = 0.15 + 2 * c
+        elif out[3]:
+            dur = 0.05 + 3.5 * c
+        elif win:
+            dur = 0.06 + 1.56 * 0.00083 * out[4]
+        else:
+            two = all(SCRATCH[x[1]][2] in (BF, U16) for x in ins + [out] if isinstance(x, tuple))
+            both = len(ins) == 2 and all(isinstance(x, tuple) and x[4] == out[4] and SCRATCH[x[1]][0] == "sbuf" for x in ins)
+            dur = max(0.06, 0.05 + c * (0.5 if two else 2 if both else 1)) + (0.14 if e == "A" else 0)
+        node(e, lambda: emit(e, f, out, ins), regions(ins + offsets(ins + [out])), regions([out]), dur, 0.0, after)
+
+    def issue():
+        tail, left, free, end, succ = [0.0] * len(nodes), [len(x[4]) for x in nodes], {}, {}, [[] for _ in nodes]
+        for k, x in enumerate(nodes):
+            for j, full in x[4]:
+                succ[j].append((k, full))
+        for k in reversed(range(len(nodes))):
+            tail[k] = nodes[k][2] + max([0.0] + [tail[s] + (nodes[k][3] + LAG) * full for s, full in succ[k]])
+        ready, order = [k for k in range(len(nodes)) if not left[k]], []
+        while ready:
+            start, first = {}, {}
+            for k in ready:
+                e, run, dur, lat, before = nodes[k]
+                start[k] = max([free.get(e, 0.0)] + [end[j] - (0 if full else nodes[j][3]) + LAG * full for j, full in before])
+                first[e] = min(first.get(e, 1e9), start[k])
+            e = min(first, key=lambda x: first[x])
+            k = max((k for k in ready if nodes[k][0] == e and start[k] <= first[e] + SLACK), key=lambda k: (tail[k], -k))
+            ready.remove(k)
+            order.append(k)
+            free[e] = start[k] + nodes[k][2]
+            end[k] = free[e] + nodes[k][3]
+            for s, full in succ[k]:
+                left[s] -= 1
+                if not left[s]:
+                    ready.append(s)
+        for k in order:
+            nodes[k][1]()
+
+    def A_(o):
+        return o[0] if isinstance(o, tuple) else o
+
+    def tt(out, a, c, o):
+        op("V", lambda q: q.tensor_tensor(A_(out), A_(a), A_(c), o), out, [a, c])
+
+    def ts(out, a, s1, o1, s2=None, o2=None):
+        if o2 is None:
+            op("V", lambda q: q.tensor_scalar(A_(out), A_(a), A_(s1), None, o1), out, [a, s1])
+        else:
+            op("V", lambda q: q.tensor_scalar(A_(out), A_(a), A_(s1), A_(s2), o1, o2), out, [a, s1, s2])
+
+    def cp(out, a):
+        op("V", lambda q: q.tensor_copy(A_(out), A_(a)), out, [a])
+
+    def scan(out, d0, d1, o0, o1):
+        op("V", lambda q: q.tensor_tensor_scan(A_(out), A_(d0), A_(d1), 0.0, o0, o1), out, [d0, d1])
+
+    def ms(out, v):
+        op("V", lambda q: q.memset(A_(out), v), out, [])
+
+    def act(out, a, fn=AF.Copy, scale=1.0, bias=0.0):
+        op("A", lambda q: q.activation(A_(out), A_(a), fn, bias=A_(bias), scale=A_(scale)), out, [a, scale, bias])
+
+    tiles = {}
+
+    def mm_now(out, l, r, st, sp, tile):
+        was = tiles.get(out[1], (tile, 0))
+        if tile is not None and was[0] != tile and know["P"].get("qP", 0) < was[1]:
+            g.tensor.wait_ge(T.sem.qP, was[1])
+            know["P"]["qP"] = was[1]
+        emit("P", lambda q: q.matmul(A_(out), A_(l), A_(r), st, sp), out, [l, r])
+        tiles[out[1]] = (tile, cnt["qP"])
+
+    def mm(out, l, r, st, sp, tile=None):
+        group.append((out, l, r, st, sp, tile))
+        if sp and not group[0][0] == "open":
+            close()
+
+    def close():
+        m = [x for x in group if x[0] != "open"]
+        group.clear()
+        node("P", lambda: [mm_now(*x) for x in m], regions([x[1] for x in m] + [x[2] for x in m]), regions([x[0] for x in m]),
+             sum(0.02 + 0.00042 * max(64, x[0][4]) for x in m))
+
+    def iota(out, pat, base, cm, after=None):
+        if SCRATCH[out[1]][2] == I32:
+            op("G", lambda q: q.iota(A_(out), pat, base, cm), out, [], after)
+        else:
+            op("G", lambda q: q.iota(A_(out), pat, base, cm, allow_small_or_imprecise_dtypes=True), out, [], after)
+
+    def asel(out, a, pat, o, base, cm):
+        op("G", lambda q: q.affine_select(A_(out), A_(a), pat, o, 0.0, base, cm), out, [a])
+
+    def scat(win, width, off, n, val):
+        cp(ind(b(win, 0, width), b(off, 0, n)), val)
+
+    def load(e, out, src, name):
+        w = regions([out])
+
+        def run():
+            sync(e, [], w)
+            Q[e].dma_start(out[0], src).then_inc(T.sem["d_" + name], 16)
+            note(e, [], w, "d_" + name, 16)
+        node(e, run, [], w, 0.1, 3.4 if out[4] > 700 else 2.4)
+
+    def store(e, dst, a, name):
+        r = regions([a])
+
+        def run():
+            sync(e, r, [])
+            Q[e].dma_start(dst, a[0]).then_inc(T.sem["o_" + name], 16)
+            note(e, r, [], "o_" + name, 16)
+        node(e, run, r, [], 0.1, 5.0 if name == "yt" else 2.0)
+
+    def send(m, src):
+        s, y, d = pl[(rank, m)]
+        to = d if y is None else y
+        r = regions([src])
+        es = engines(topo, core, to, m)
+        rid, pid = topo.addr(to, core)
+
+        def run():
+            sync("G", r, [])
+            g.remote_dma(land(T, m), src[0], T.sem["a_" + m], T.sem["l_" + m], pid, rid, bits(es))
+            note("G", r, [], "l_" + m, len(es))
+        k = node("G", run, r, [], 0.1)
+        for (r_, m_), (s_, y_, d_) in pl.items():
+            if d_ == core and m_ == m:
+                w = regions([b(m, 0, S) if m in TABLES else b(m)])
+                n = len(engines(topo, s_ if y_ is None else y_, d_, m))
+                lat = (1.7 + (9.0 if m in TABLES else 0.8 if src[4] > 100 else 0.0)) * (1 if y_ is None else 2)
+                node("n" + m, lambda: note("net", [], w, "a_" + m, n), [], w, 0.0, lat, k)
+        return k
+
+    load("S", b("EFI", 0, L), T.ef[:, 0:L], "ef0")
+    load("A", b("HT", 0, S), T.tab[:, :], "tab")
+    load("S", b("EHI", 0, L), T.eh[:, 0:L], "eh0")
+    load("S", b("ZF", 0, L), T.zf[:, 0:L], "zf0")
+    load("S", b("TC"), T.tab[:, :], "tc")
+    load("S", b("EFI", L, F), T.ef[:, L:F], "ef1")
+    load("S", b("EHI", L, F), T.eh[:, L:F], "eh1")
+    load("S", b("ZF", L, F), T.zf[:, L:F], "zf1")
+
+    ms(b("ONB"), 1.0)
+    iota(b("PI"), [[0, 1]], 0, 1)
+    iota(b("KIO"), [[0, 13], [1, 16]], 0, 0)
+    asel(b("BA"), b("ONB"), [[-16, 8], [0, 16]], OP.is_ge, 0, 1)
+    asel(b("BO"), b("BA"), [[16, 8], [0, 16]], OP.is_ge, 15, -1)
+    asel(b("ID"), b("ONB"), [[-1, 128]], OP.is_equal, 0, 1)
+    iota(b("EX0", 0, 13), [[16, 13]], 0, -1)
+    iota(b("EX1", 0, 13), [[16, 13]], -NB, -1)
+    ts(b("PJ"), b("PI"), 15, OP.bitwise_and)
+    ts(b("PK"), b("PI"), 4, OP.arith_shift_right, 1, OP.bitwise_and)
+    cp(b("PM"), b("PJ"))
+    cp(b("MH1"), b("PK"))
+    ts(b("MH0"), b("MH1"), -1.0, OP.mult, 1.0, OP.add)
+    ts(b("PW"), b("PM"), -1.0, OP.mult, 11.0, OP.add)
+    act(b("PW"), b("PW"), AF.Exp, LN2)
+    for x in (0, 1):
+        ex = "EX%d" % x
+        ts(b(ex, 0, 13), b(ex, 0, 13), 60.0, OP.min, -60.0, OP.max)
+        act(b("W%d" % x, 0, 13), b(ex, 0, 13), AF.Exp, LN2)
+    ts(b("THR"), b("PW"), 2.5 / 2048.0, OP.mult)
+    ms(b("MB", 0, 1), 200.0)
+    ms(b("MB", 1, 2), -10.0)
+    ms(b("WMU"), 0.0)
+    ts(b("WMU", 15, 143, 16), b("BO", 0, 128, 16), float(PEN), OP.mult)
+    ts(b("NBO"), b("BO"), -1.0, OP.mult)
+    ts(b("KAD"), b("KIO"), -2048.0, OP.mult, 30720.0, OP.add)
+    ts(b("RKM"), b("KIO"), 0.0, OP.is_gt)
+    ts(b("M16"), b("KIO"), b("PM"), OP.is_equal)
+
+    def pack(lo, hi):
+        ts(b("EE", lo, hi), b("EFI", lo, hi), 4096.0, OP.mult)
+        tt(b("EE", lo, hi), b("EE", lo, hi), b("EHI", lo, hi), OP.add)
+
+    def lists(x, c0, c1, t):
+        n0, n1 = 16 * c0, 16 * c1
+        ts(b3("I3", c0, c1, 0, 16), x, b("MH0"), OP.mult)
+        act(b3("I3", c0, c1, 16, 32), x, scale=b("MH1"))
+        y, i3 = b3("Y3", c0, c1, 0, 32), b3("I3", c0, c1, 0, 32)
+        op("V", lambda q: q.transpose(T.Y3[:, c0:c1, :], T.I3[:, c0:c1, :]), y, [i3])
+        tt(b3("XI", c0, c1, 0, 16), b3("Y3", c0, c1, 0, 16), b3("Y3", c0, c1, 16, 32), OP.add)
+        ts(b2("HF", 0, n0, n1), b3("XI", c0, c1, 0, 16), 2047, OP.bitwise_and)
+        ts(b2("HF", 1, n0, n1), b3("XI", c0, c1, 0, 16), 12, OP.arith_shift_right, 2047, OP.bitwise_and)
+        cp(b3("LI%d" % t, 0, 2, n0, n1), b3("HF", 0, 2, n0, n1))
+
+    def half(t, x):
+        return lambda lo, hi: b2("LI%d" % t, x, lo, hi)
+
+    def keyadd(c0, c1, t):
+        n0, n1 = 16 * c0, 16 * c1
+        tt(b("KA%d" % t, n0, n1), b("KAD", n0, n1), b2("HF", 0, n0, n1), OP.add)
+
+    def expand(z, src, c0, c1, cp=cp):
+        cp(b3(z, c0, c1, 0, 16), src)
+        for w in (16, 32, 64, 128):
+            cp(b3(z, c0, c1, w, 2 * w), b3(z, c0, c1, 0, w))
+
+    bank = [0]
+
+    def bulk(win, lst, z, cm, vch, ach):
+        for c0, c1 in ach:
+            w = 256 * (c1 - c0)
+            ga, t = "GA%d" % (bank[0] % 3), "T%d" % (bank[0] % 6)
+            bank[0] += 1
+            act(b(ga, 0, w), ind(b(win, 0, S), lst(16 * c0, 16 * c1)), scale=-1.0)
+            mm(b(t, 0, w), b("ID"), b3(z, c0, c1, 0, 256), True, False)
+            mm(b(t, 0, w), b("ID"), b(ga, 0, w), False, True)
+            act(b(cm, 256 * c0, 256 * c1), b(t, 0, w), AF.Sigmoid, 400.0, b("MB", 0, 1))
+        for c0, c1 in vch:
+            for c in range(c0, c1):
+                tt(b(cm, 256 * c, 256 * c + 256), ind(b(win, 0, S), lst(16 * c, 16 * c + 16)), b2(z, c, 0, 256), OP.is_le)
+
+    def psum(cm, dst, *cuts):
+        for c0, c1 in zip(cuts, cuts[1:]):
+            for m in range(16):
+                mm(b(dst, 16 * c0, 16 * c1), b("WMU", 15 - m, 143 - m), b(cm, 256 * c0 + m, 256 * c1, 16), m == 0, m == 15)
+
+    def home_max(t):
+        tt(b("HK"), b("PH", 0, L), b("KA%d" % t), OP.add)
+        scan(b("HS"), b("RKM"), b("HK"), OP.mult, OP.max)
+        cp(b("HKI", 0, 13), b("HS", 15, L, 16))
+        ts(b("HSL", 0, 13), b("HKI", 0, 13), 2047, OP.bitwise_and)
+        ts(b("A1", 0, 13), b("HKI", 0, 13), float(9 * PEN), OP.is_ge, float(9 * PEN), OP.mult)
+        ts(b("AP", 0, 13), b("HSL", 0, 13), float(OKB), OP.add)
+        tt(b("AP", 0, 13), b("AP", 0, 13), b("A1", 0, 13), OP.max)
+
+    JOBS = []
+    for h in (0, 1):
+        for a in (h, 2 + h):
+            JOBS += [(2 * a, "T%d" % a, 0, 0), (2 * a + 1, "T%d" % a, L, 0)]
+        JOBS += [(2 * h + x, "T4", 192 * h + 96 * x, 1) for x in (0, 1)]
+        JOBS += [(4 + 2 * h + x, ("T5", "PF")[h], L * h + 96 * x, 1) for x in (0, 1)]
+
+    def decide(t, kf):
+        tt(b("YY", 0, 13), b("AP", 0, 13), kf, OP.max)
+        ts(b("IX", 0, 13), b("YY", 0, 13), float(OKB + S), OP.min, float(OKB), OP.subtract)
+        act(b("B1"), ind(b("CT1", 0, S + 16), b("IX", 0, 13)))
+        cp(b("B0"), ind(b("CT0", 0, S + 16), b("IX", 0, 13)))
+        for gg, t_, o, blk in JOBS:
+            pp, lo, n = (32 * (gg // 2), 32 * (gg // 2) + 32), (0, NB)[blk], (NB, 96)[blk]
+            bb = "B%d" % (gg % 2)
+            mm(b(t_, o, o + L - lo, p=(0, n)), b(bb, lo, lo + n, p=pp), b(bb, lo, L, p=pp), True, True, gg // 2)
+        for gg, t_, o, blk in JOBS:
+            w, pp = (L, 96)[blk], (0, (NB, 96)[blk])
+            out = b3("E%d" % blk, 0, (13, 6)[blk], 16 * gg, 16 * gg + 16, p=pp)
+            if t_ in ("T2", "T3", "PF"):
+                act(out, b(t_, o, o + w, p=pp), AF.Relu, 1.0, b("MB", 1, 2, p=pp))
+            else:
+                ts(out, b(t_, o, o + w, p=pp), 10.5, OP.is_ge)
+        ts(b("D0", 0, 13), b("YY", 0, 13), float(-OKB), OP.add)
+        group.append(("open",))
+        for c in range(13):
+            mm(b("PH", 416 + c, 417 + c), b2("E0", c, 0, 128, p=(0, NB)), b("W0", c, c + 1, p=(0, NB)), True, c < 7)
+            if c >= 7:
+                mm(b("PH", 416 + c, 417 + c), b2("E1", c - 7, 0, 128, p=(0, 96)), b("W1", c, c + 1, p=(0, 96)), False, True)
+        close()
+        tt(b("WM", 0, 13), b("HS", 15, L, 16), kf, OP.max)
+        cp(b("WI", 0, 13), b("WM", 0, 13))
+        ts(b("WS", 0, 13), b("WI", 0, 13), 15, OP.arith_shift_right)
+        ts(b("WR", 0, 13), b("WS", 0, 13), 9.0, OP.is_ge)
+        tt(b("WV", 0, 13), b("WR", 0, 13), b("WS", 0, 13), OP.mult)
+        tt(b("XB"), ind(b("WV", 0, 16), b("BL", 0, 13)), b("M16"), OP.mult)
+        mm(b("PF", L, 2 * L), b("BO"), b("XB"), True, True)
+        ts(b("L1", 0, 13), b("PH", 416, 429), b("THR"), OP.is_gt, 4096.0, OP.mult)
+        tt(b("D2", 0, 13), b("L1", 0, 13), b("D0", 0, 13), OP.max)
+        tt(b("DS%d" % t, 0, 13), b("D2", 0, 13), b("DU%d" % t, 0, 13), OP.min)
+        cp(b("DT%d" % t, 0, 13), b("DS%d" % t, 0, 13))
+
+    def ranks(n):
+        scan(b("UC", 0, n), b("ON32", 0, n), b("UU", 0, n), OP.mult, OP.add)
+        group.append(("open",))
+        mm(b("PF", 416, 416 + n), b("BO"), b("UC", 0, n), True, False)
+        mm(b("PF", 416, 416 + n), b("NT"), b("UU", 0, n), False, True)
+        mm(b("PF", 448, 449), b("BO"), b("UC", n - 1, n), True, True)
+        close()
+
+    def lanes(t, n, fill, val):
+        pls, lw, lu = "PL%d" % t, "LW%d" % t, "LU%d" % t
+        ts(b("TB"), b("PF", 448, 449), -1.0, OP.mult, float(fill), OP.add)
+        tt(b("QQ", 0, n), b("PF", 416, 416 + n), b("NU", 0, n), OP.max)
+        cp(b(pls, 0, n), b("QQ", 0, n))
+        act(b(lw, 80, 208), b("L128"), AF.Identity, 1.0, b("TB"))
+        cp(ind(b(lw, 80, 80 + 1024), b(pls, 0, n)), val)
+        tt(b("XM"), b(lw, 80, 208), b("M16", 0, 128), OP.mult)
+        scan(b("XS"), b("RKM", 0, 128), b("XM"), OP.mult, OP.add)
+        cp(b(lu, 0, 8), b("XS", 15, 128, 16))
+
+    AS, VS = [(0, 2), (2, 3)], [(3, 5)]
+    AD, VD = [(9, 11), (5, 6)], [(6, 9), (11, 13)]
+    A0, V0 = [(0, 2), (2, 3), (9, 11)], [(3, 9), (11, 13)]
+
+    def step(t, ftab, update, later):
+        lu, hl, fl, z = "LU%d" % t, half(t, 0), half(t, 1), "Z16%d" % t
+        bulk("HT", hl, z, "CMH", VS, AS)
+        act(b("DQ"), ind(b("D"), b(lu, 0, 8)), scale=4097.0)
+        act(b("ZL%d" % t, 80, L), ind(b("ZF"), b(lu, 0, 8)))
+        tt(b("XE"), ind(b("EE"), b(lu, 0, 8)), b("DQ"), OP.add)
+        lists(b("XE"), 5, 13, t)
+        update()
+        bulk(ftab, fl, z, "CMF", VS, AS)
+        psum("CMH", "PH", 0, 5)
+        expand(z, b("ZL%d" % t, 80, L), 5, 13)
+        keyadd(5, 13, t)
+        bulk("HT", hl, z, "CMH", VD, AD)
+        psum("CMF", "PF", 0, 5)
+        bulk(ftab, fl, z, "CMF", VD, AD)
+        psum("CMH", "PH", 5, 9, 13)
+        psum("CMF", "PF", 5, 9)
+        home_max(t)
+        psum("CMF", "PF", 9, 13)
+        later()
+        scan(b("FS"), b("RKM"), b("PF", 0, L), OP.mult, OP.max)
+        decide(t, b("FS", 15, L, 16))
+
+    send("RQZ", b("ZF", 0, L))
+    send("U3Z", b("ZF", 0, L))
+    send("U2Z", b("ZF", 0, L))
+    pack(0, L)
+    lists(b("EE", 0, L), 0, 13, 0)
+    asked = send("RQL", b2("LI0", 1, 0, L))
+    expand("Z160", b("ZF", 0, L), 0, 13)
+    keyadd(0, 13, 0)
+    send("F2", b("TC"))
+    send("F3", b("TC"))
+    asel(b("NT"), b("NBO"), [[-1, 128]], OP.is_ge, 0, 1)
+    iota(b("CL", 0, 256), [[1, 256]], 0, 0)
+    iota(b("CL", 256, 264), [[256, 8]], 0, 0)
+    iota(b("C16", 0, 26), [[16, 26]], 0, 0)
+    iota(b("BLF", 0, 13), [[1, 13]], 0, 0)
+    iota(b("F2V", 0, 80), [[1, 80]], 544, 0)
+    iota(b("F2V", 80, 416), [[1, 336]], 0, 0, asked)
+    bulk("HT", half(0, 0), "Z160", "CMH", V0, A0)
+    expand("ZR", b("RQZ"), 0, 13)
+    bulk("HT", lambda lo, hi: b("RQL", lo, hi), "ZR", "CMF", V0, A0)
+    psum("CMH", "PH", 0, 5, 9, 13)
+    psum("CMF", "PF", 0, 5, 9, 13)
+    cp(b("PX"), b("PW"))
+    cp(b("PY"), b("PX"))
+    ts(b("CI"), b("CL"), b("PY"), OP.mult)
+    ts(b("CJ"), b("CI"), 2048, OP.bitwise_and)
+    ts(b("CB"), b("CJ"), 1.0 / 1024.0, OP.mult, -1.0, OP.add)
+    ts(b("ML", 2, 3), b("PM"), 8.0, OP.is_lt)
+    ts(b("MH", 2, 3), b("PM"), 11.0, OP.is_lt)
+    tt(b("MH", 2, 3), b("MH", 2, 3), b("ML", 2, 3), OP.subtract)
+    for x in (0, 1):
+        tt(b("ML", x, x + 1), b("ML", 2, 3), b("MH%d" % x), OP.mult)
+        tt(b("MH", x, x + 1), b("MH", 2, 3), b("MH%d" % x), OP.mult)
+        ts(b2("LB", x, 0, 256), b("CB", 0, 256), b("ML", x, x + 1), OP.mult)
+        ts(b2("HB", x, 0, 8), b("CB", 256, 264), b("MH", x, x + 1), OP.mult)
+        ms(b("CT%d" % x, S, S + 16), 0.0)
+    ms(b("KFO"), 0.0)
+    scan(b("FS"), b("RKM"), b("PF", 0, L), OP.mult, OP.max)
+    cp(b("KFO", 0, 13), b("FS", 15, L, 16))
+    told = send("KFR", b("KFO"))
+    home_max(0)
+    iota(b("LW1", 0, 80), [[1, 80]], 544, 0, told)
+    iota(b("LW2", 0, 80), [[1, 80]], 464, 0, told)
+    iota(b("L128"), [[1, 128]], 0, 0)
+    for x in range(0, WT, 704):
+        iota(b("OC", x, x + 704), [[0, 704]], -1, 0, told)
+    for x in (0, 512):
+        iota(b("LVF", x, x + 512), [[0, 512]], x // 8, 0, told)
+        iota(b("LVW", x, x + 512), [[0, 512]], 0, 0, told)
+    for h in range(8):
+        act(b("CT1", 256 * h, 256 * h + 256), b2("LB", 1, 0, 256), AF.Identity, 1.0, b2("HB", 1, h, h + 1))
+        ts(b("CT0", 256 * h, 256 * h + 256), b2("LB", 0, 0, 256), b2("HB", 0, h, h + 1), OP.add)
+    ts(b("FW", 0, 26), b("C16", 0, 26), b("PM"), OP.add)
+    for t in range(3):
+        ts(b("DU%d" % t, 0, 13), b("FW", 0, 13), float(S + 256 * t), OP.add)
+    ts(b("DMF", 0, 26), b("FW", 0, 26), 512.0, OP.add)
+    cp(b("BL", 0, 13), b("BLF", 0, 13))
+    for n_, v_ in (("WV", 0.0), ("WN", 0.0), ("DT0", 0), ("DT1", 0), ("ON32", 1.0), ("D", 0.0), ("BP", 0.0)):
+        ms(b(n_), v_)
+    pack(L, F)
+    for t, f0 in ((1, 544), (2, 464)):
+        lists(b("EE", f0, f0 + 80), 0, 5, t)
+        keyadd(0, 5, t)
+        act(b("ZL%d" % t, 0, 80), b("ZF", f0, f0 + 80))
+        expand("Z16%d" % t, b("ZF", f0, f0 + 80), 0, 5, act)
+    decide(0, b("KFR", 0, 13))
+    send("U2D", b("DT0"))
+    send("U3D", b("DT0"))
+
+    ts(b("UU", 0, 13), b("DS0", 0, 13), float(S), OP.is_ge)
+    ranks(13)
+    ts(b("NU", 0, 13), b("DS0", 0, 13), float(S), OP.is_lt)
+    tt(b("NU", 0, 13), b("NU", 0, 13), b("DMF", 0, 13), OP.mult)
+    scat("HT", WT, "DT0", 13, b("ZF", 0, L))
+    lanes(1, 13, 208, b("F2V", 80, 288))
+    act(b("D", 0, L), b("PF", L, 2 * L))
+
+    def update1():
+        send("V3Z", b("ZL1"))
+        scat("F2", WT, "U2D", 13, b("U2Z"))
+
+    def later1():
+        scat("OC", WT, "DT0", 13, b("F2V", 80, 288))
+        scat("F3", WT, "U3D", 13, b("U3Z"))
+    step(1, "F2", update1, later1)
+    send("V3D", b("DT1"))
+
+    ts(b("WN", 0, 13), b("DS1", 0, 13), float(S), OP.is_lt, 64.0, OP.mult)
+    tt(b("XB"), ind(b("WN", 0, 16), b("BL", 0, 13)), b("M16"), OP.mult)
+    mm(b("PH", L, 2 * L), b("BO"), b("XB"), True, True)
+    act(b("LVF", 0, 128), b("PH", L + 80, 2 * L))
+    act(b("LVW", 0, 128), b("PF", L + 80, 2 * L))
+    act(b("D", 544, F), b("PF", L, L + 80))
+    ts(b("TU"), b("TB"), -1.0, OP.mult)
+    ts(b("PL1", 13, 21), b("FW", 13, 21), b("TU"), OP.add)
+    scat("OC", WT, "DT1", 13, b("LW1", 0, L))
+    tt(b("BP", 0, L), ind(b("OC"), b("DT0", 0, 13)), b("F2V", 80, 288), OP.not_equal)
+    ts(b("UF"), ind(b("LVF"), b("PL1", 0, 21)), 64.0, OP.is_lt)
+    for x in ("BP", "UF"):
+        for m in range(16):
+            mm(b("PH", 450, 471), b("WMU", 15 - m, 143 - m), b(x, m, 336, 16), x == "BP" and m == 0, x == "UF" and m == 15)
+    ts(b("UU", 0, 5), b("DS1", 0, 5), float(S), OP.is_ge)
+    scat("HT", WT, "DT1", 13, b("ZL1"))
+    act(b("GW"), ind(b("LVW"), b("PL1", 0, 21)))
+    ts(b("UU", 5, 26), b("PH", 450, 471), 1.0, OP.is_ge)
+    ranks(26)
+    ts(b("NU", 0, 26), b("UU", 0, 26), -1.0, OP.mult, 1.0, OP.add)
+    tt(b("NU", 0, 26), b("NU", 0, 26), b("DMF", 0, 26), OP.mult)
+    lanes(2, 26, 336, b("F2V"))
+    for i, x in enumerate(("D", "GW", "BP")):
+        mm(b("T5", 0, 336), b("ID"), b(x, 0, 336), i == 0, i == 2)
+    act(b("D", 0, 336), b("T5", 0, 336))
+
+    def later2():
+        ts(b("NB1"), b("BP", 0, L), -1.0, OP.mult, 1.0, OP.add)
+        act(b("DL"), ind(b("D"), b("LU2", 0, 8)))
+        ms(b("DF", 336, 464), 0.0)
+    step(2, "F3", lambda: scat("F3", WT, "V3D", 13, b("V3Z")), later2)
+
+    scat("HT", WT, "DT2", 13, b("ZL2"))
+    store("S", T.yt[:, :], b("HT", 0, S), "yt")
+    scat("OC", WT, "DT2", 13, b("LW2", 0, L))
+    store("A", T.yo[:, :], (T.OC[0:128:16, 0:S], "OC", (0, 1, 0, S), None, S), "yo")
+    tt(b("B3"), ind(b("OC"), b("DT0", 0, 13)), b("F2V", 80, 288), OP.not_equal)
+    tt(b("HK"), ind(b("OC"), b("DT1", 0, 13)), b("LW1", 0, L), OP.not_equal)
+    tt(b("BP", 0, L), b("B3"), b("NB1"), OP.mult)
+    cp(b("LVW", 0, 128), b("HK", 80, L))
+    cp(b("B2"), ind(b("LVW"), b("PL1", 0, 21)))
+    for i, x in enumerate(("D", "BP", "B2")):
+        mm(b("T4", 0, 336), b("ID"), b(x, 0, 336), i == 0, i == 2)
+    tt(b("ND"), b("DL"), b("PF", L + 80, 2 * L), OP.add)
+    cp(b("DF", 464, 544), b("PF", L, L + 80))
+    tt(b("DF", 544, F), b("D", 544, F), b("HK", 0, 80), OP.add)
+    cp(b("DF", 0, 336), b("T4", 0, 336))
+    scat("DF", F, "LU2", 8, b("ND"))
+    store("S", T.yd[:, :], (T.DF[0:128:16, 0:F], "DF", (0, 1, 0, F), None, F), "yd")
+    issue()
+    for s in SEMAPHORES:
+        if s in cnt and know["G"].get(s, 0) < cnt[s]:
+            g.wait_ge(T.sem[s], cnt[s])

@@ -1,23 +1,24 @@
-import math
 from concourse.mybir import AluOpType, ActivationFunctionType
 OP = AluOpType
 AF = ActivationFunctionType
 F32, BF, I32, U16 = "float32", "bfloat16", "int32", "uint16"
 F, L, S = 624, 208, 2048
-WT = S + 3 * 256
-PEN = 32768
+PAD = 32
+WT = S + PAD + 3 * L
+PEN = 65536
 OKB = 8 * PEN
-NB = 112
-LN2 = math.log(2.0)
-LAG, SLACK = 0.1, 0.05
+NB = 128
+BIG = 1048576.0
+LAG, SLACK = 0.08, 0.05
+KA0, KR0, KAD_ = 6, 6, 4
 
 ENG = "VAPG"
-LOADS = ["ef0", "eh0", "zf0", "tab", "tc", "ef1", "eh1", "zf1"]
+LOADS = ["ef0", "eh0", "zf0", "tab", "ef1", "eh1", "zf1", "ef2", "eh2", "zf2"]
 MSGS = ["RQZ", "RQL", "KFR", "F2", "F3", "U2Z", "U2D", "U3Z", "U3D", "V3Z", "V3D"]
 TO = {"RQZ": 1, "RQL": 1, "KFR": -1, "F2": -2, "U2Z": -2, "U2D": -2, "F3": -3, "U3Z": -3, "U3D": -3, "V3Z": -3, "V3D": -3}
-ORDER = ["RQZ", "U3Z", "RQL", "F3", "KFR", "U3D", "V3Z", "V3D"]
-TABLES = ("F2", "F3")
-STORES = ["yt", "yo", "yd"]
+SMALL = [("RQZ", "RQZ"), ("RQL", "RQL"), ("RQZ", "U2Z"), ("RQZ", "U3Z"), ("KFR", "KFR"), ("U3D", "U3D"), ("V3Z", "V3Z"), ("V3D", "V3D")]
+TABLES = [("F2", "F2"), ("F2", "F3")]
+STORES = ["yt", "yo", "yd", "ye"]
 SEMAPHORES = (["q" + e for e in ENG] + ["d_" + n for n in LOADS] + ["o_" + n for n in STORES]
               + ["a_" + n for n in MSGS] + ["l_" + n for n in MSGS])
 
@@ -36,91 +37,87 @@ def _sb(name, shape, dtype):
 
 
 for _n, _s, _d in (
-        ("HT", [WT], BF), ("F2", [WT], BF), ("F3", [WT], BF), ("TC", [S], BF), ("OC", [WT], F32),
-        ("ZF", [F], BF), ("EHI", [F], I32), ("EFI", [F], I32), ("EE", [F], F32), ("D", [F], BF), ("DF", [F], F32),
-        ("XE", [128], F32), ("DQ", [128], F32), ("I3", [13, 32], F32), ("Y3", [13, 32], F32), ("XI", [13, 16], I32),
-        ("HF", [2, L], I32), ("GA0", [512], BF), ("GA1", [512], BF), ("GA2", [512], BF),
-        ("CMH", [3328], BF), ("CMF", [3328], BF), ("ZR", [13, 256], BF),
-        ("RQZ", [L], BF), ("RQL", [L], U16), ("KFR", [16], F32), ("KFO", [16], F32),
+        ("HT", [WT], BF), ("F2", [WT], BF), ("F3", [WT], BF), ("OC", [WT], F32),
+        ("ZF", [F], BF), ("EHI", [F], I32), ("EFI", [F], I32), ("EH", [F + 32], F32), ("EF", [F + 32], F32),
+        ("D", [F], BF), ("DF", [F + L], F32), ("XH", [160], F32), ("XF", [160], F32), ("DQ", [128], F32),
+        ("YH", [448], F32), ("YF", [448], F32), ("YS", [192], F32), ("YT", [192], F32),
+        ("LH0", [224], U16), ("LF0", [224], U16), ("LDH", [128], U16), ("LDF", [128], U16),
+        ("GA0", [512], BF), ("GA1", [512], BF), ("GA2", [512], BF), ("CMH", [L, 16], BF), ("CMF", [L, 16], BF),
+        ("RQZ", [L], BF), ("RQL", [224], U16), ("KFR", [16], F32), ("KFO", [16], F32),
         ("U2Z", [L], BF), ("U2D", [16], U16), ("U3Z", [L], BF), ("U3D", [16], U16), ("V3Z", [L], BF), ("V3D", [16], U16),
-        ("HK", [L], F32), ("HS", [L], F32), ("FS", [L], F32), ("HKI", [16], I32), ("HSL", [16], I32), ("A1", [16], F32),
-        ("AP", [16], F32), ("YY", [16], F32), ("IX", [16], U16), ("D0", [16], F32), ("L1", [16], F32), ("D2", [16], F32),
-        ("WM", [16], F32), ("WI", [16], I32), ("WS", [16], I32), ("WR", [16], F32), ("WV", [16], F32), ("WN", [16], F32),
-        ("XB", [L], BF), ("B0", [L], BF), ("B1", [L], BF), ("E0", [13, 128], BF), ("E1", [6, 128], BF),
-        ("NU", [32], F32), ("UU", [32], BF), ("UC", [32], BF), ("QQ", [32], F32), ("TB", [1], F32), ("TU", [1], F32),
-        ("XM", [128], F32), ("XS", [128], F32), ("LVF", [1024], F32), ("LVW", [1024], F32), ("UF", [336], BF),
-        ("GW", [336], BF), ("BP", [336], BF), ("NB1", [L], F32), ("B2", [336], BF), ("B3", [L], F32), ("DL", [128], F32),
-        ("ND", [128], F32),
+        ("HS", [L], F32), ("FS", [221], F32), ("HKI", [16], I32), ("HSL", [16], I32), ("A1", [16], F32),
+        ("AP", [16], F32), ("YY", [16], F32), ("IX", [16], U16), ("WI", [16], I32), ("WU", [16], U16), ("UL", [16], U16),
+        ("DS", [16], F32), ("B0", [L], BF), ("B1", [L], BF), ("E0", [13, 128], BF), ("E1", [5, 128], BF),
+        ("NU", [32], F32), ("UU", [48], BF), ("UC", [32], BF), ("QQ", [32], F32), ("TB", [1], F32),
+        ("LD", [128], F32), ("XS", [128], F32), ("LVF", [1104], BF), ("LVW", [1104], BF), ("UF", [512], BF),
+        ("GW", [336], BF), ("BP", [512], BF), ("W2", [L], F32), ("ND", [128], F32), ("OQ", [L], F32), ("OX", [L], F32),
+        ("VB", [L], F32), ("Q1", [16], F32), ("Q2", [16], F32), ("Q3", [16], F32), ("QI", [16], U16), ("BL", [16], U16),
+        ("DUQ", [16], F32),
         ("PI", [1], I32), ("PJ", [1], I32), ("PK", [1], I32), ("PM", [1], F32), ("MH0", [1], F32), ("MH1", [1], F32),
-        ("PW", [1], F32), ("PX", [1], I32), ("PY", [1], F32), ("ML", [4], F32), ("MH", [4], F32), ("MB", [2], F32),
-        ("KIO", [L], F32), ("M16", [L], F32), ("RKM", [L], F32), ("KAD", [L], F32), ("C16", [32], F32), ("FW", [32], F32),
-        ("DMF", [32], F32), ("ONB", [128], BF), ("BA", [128], BF), ("BO", [128], BF), ("NBO", [128], BF), ("NT", [128], BF),
-        ("ID", [128], BF), ("WMU", [144], BF), ("EX0", [16], F32), ("EX1", [16], F32), ("W0", [16], BF), ("W1", [16], BF),
-        ("THR", [1], F32), ("CL", [264], F32), ("CI", [264], I32), ("CJ", [264], I32), ("CB", [264], F32),
-        ("LB", [2, 256], BF), ("HB", [2, 8], F32), ("CT0", [S + 64], BF), ("CT1", [S + 64], BF),
-        ("F2V", [416], F32), ("L128", [128], F32), ("BLF", [16], F32), ("BL", [16], U16), ("ON32", [32], F32),
+        ("PY", [1], F32), ("P2", [16], F32), ("P3", [16], F32), ("ML", [2], F32), ("MB", [4], F32), ("MC", [6], F32),
+        ("KIO", [L], F32), ("M16", [L], F32), ("RKM", [L], BF), ("RK8", [104], BF), ("KAD", [L], F32), ("C16", [32], F32),
+        ("FW", [32], F32), ("DMF", [32], F32), ("ONB", [128], BF), ("BA", [128], BF), ("BO", [128], BF), ("NBO", [128], BF),
+        ("NT", [128], BF), ("ID", [128], BF), ("IDF", [128], F32), ("WMU", [144], BF), ("BW", [1], BF),
+        ("CL", [264], F32), ("CI", [264], I32), ("CJ", [264], I32), ("CB", [264], F32),
+        ("LB", [256], BF), ("HB", [8], F32), ("CT", [S + 64], BF), ("JA", [L], BF), ("JB", [416], BF), ("JC", [320], BF),
+        ("QV", [416], F32), ("FQ", [F], F32), ("LM", [128], F32), ("ON32", [32], F32), ("TW", [32], F32), ("T01", [16], F32),
+        ("RK", [16], I32), ("RC", [16], I32), ("RP", [16], I32), ("RX", [16], F32), ("RY", [16], F32), ("PC", [16], F32),
 ):
     _sb(_n, _s, _d)
 for _t in range(3):
-    for _n, _s, _d in (("LI", [2, L], U16), ("KA", [L], F32), ("ZL", [L], BF), ("Z16", [13, 256], BF),
-                       ("DU", [16], F32), ("DS", [16], F32), ("DT", [16], U16), ("LW", [80 + 1024], F32),
-                       ("PL", [32], U16), ("LU", [16], U16)):
-        if not (_t == 0 and _n in ("ZL", "LW", "PL", "LU")):
+    for _n, _s, _d in (("KA", [L], F32), ("ZL", [L], BF), ("DU", [16], F32), ("DT", [16], U16), ("LW", [1024], F32),
+                       ("LF", [L], F32), ("PL", [32], U16), ("LU", [16], U16), ("LSH", [80], U16), ("LSF", [80], U16),
+                       ("RO", [16], U16), ("RQ", [16], U16)):
+        if _t > 0 or _n in ("KA", "DU", "DT", "RO", "RQ"):
             _sb("%s%d" % (_n, _t), _s, _d)
 for _d, _w in _fill.items():
     SCRATCH["S" + _d] = ("sbuf", [128, _w], _d)
-for _n in ["PH", "PF"] + ["T%d" % i for i in range(6)]:
+for _n in range(6):
+    SCRATCH["T%d" % _n] = ("psum", [128, 32, 16], F32)
+for _n in ("PH", "PF"):
     SCRATCH[_n] = ("psum", [128, 512], F32)
     PLACE[_n] = (_n, 0, 512)
+KINDS = [(13, 14), (5, 5), (8, 8)]
 
 
-def plan(T, topo):
-    n = len(T.cores)
-    out = {}
-    for r in range(n):
-        src = T.cores[r]
-        for m in MSGS:
-            dst = T.cores[(r + TO[m]) % n]
-            relay = None
-            if not topo.may_write(src, dst):
-                c = [x for x in topo.cores_of(src) if x != src and topo.may_write(x, dst) and topo.die(x) == topo.die(src)]
-                relay = c[0] if m == "F3" else c[-1]
-            out[(r, m)] = (src, relay, dst)
-    return out
-
-
-def engines(topo, a, b, m):
-    e = topo.engines(a, b)
-    if m in TABLES:
-        return e[:4] if len(e) == 8 else e[8:12]
-    return e[4:8]
+def helpers(T, topo, core):
+    c = [x for x in topo.cores_of(core) if x != core and all(topo.may_write(x, d) for d in T.cores)]
+    return [x for x in c if topo.die(x) == topo.die(core)][0], [x for x in c if topo.die(x) != topo.die(core)][0]
 
 
 def bits(e):
     return sum(1 << x for x in e)
 
 
+def near(topo, a, b, m):
+    e = topo.engines(a, b)
+    return e[:len(e) // 2] if m == "F2" else e[len(e) // 2:]
+
+
 def land(T, m):
-    return T[m][:, 0:S] if m in TABLES else T[m][:, :]
+    return T[m][:, 0:S] if m in ("F2", "F3") else T[m][:, :]
 
 
-def relay_program(g, core, T, topo, pl):
-    todo = sorted((ORDER.index(m), m, r) for (r, m), (s, y, d) in pl.items() if y == core)
-    for _, m, r in todo:
-        s, y, d = pl[(r, m)]
-        g.wait_ge(T.sem["a_" + m], len(engines(topo, s, y, m)))
-        rid, pid = topo.addr(d, y)
-        g.remote_dma(land(T, m), land(T, m), T.sem["a_" + m], T.sem["l_" + m], pid, rid, bits(engines(topo, y, d, m)))
-    for _, m, r in todo:
-        s, y, d = pl[(r, m)]
-        g.wait_ge(T.sem["l_" + m], len(engines(topo, y, d, m)))
+def helper_program(g, core, T, topo):
+    n = len(T.cores)
+    for r, src in enumerate(T.cores):
+        for me, todo in zip(helpers(T, topo, src), (SMALL, TABLES)):
+            if me != core:
+                continue
+            for got, m in todo:
+                d = T.cores[(r + TO[m]) % n]
+                if got == m:
+                    g.wait_ge(T.sem["a_" + m], len(near(topo, src, core, m)))
+                rid, pid = topo.addr(d, core)
+                g.remote_dma(land(T, m), land(T, got), T.sem["a_" + m], T.sem["l_" + m], pid, rid, topo.mask(core, d))
+            for got, m in todo:
+                g.wait_ge(T.sem["l_" + m], len(topo.engines(core, T.cores[(r + TO[m]) % n])))
 
 
 def rank_program(g, core, T, topo):
-    pl = plan(T, topo)
     rank = T.rank_of(core)
     if rank is None:
-        return relay_program(g, core, T, topo, pl)
+        return helper_program(g, core, T, topo)
     Q = {"V": g.vector, "A": g.scalar, "P": g.tensor, "G": g, "S": g.sync}
     cnt = {}
     know = {e: {} for e in Q}
@@ -134,8 +131,9 @@ def rank_program(g, core, T, topo):
         ap = T[name][p[0]:p[1], lo:hi] if step == 1 else T[name][p[0]:p[1], lo:hi:step]
         return (ap, name, (0, 1, lo, hi), None, -(-(hi - lo) // step))
 
-    def b3(name, c0, c1, lo, hi, p=(0, 128)):
-        return (T[name][p[0]:p[1], c0:c1, lo:hi], name, (c0, c1, lo, hi), None, (c1 - c0) * (hi - lo))
+    def b3(name, c0, c1, lo=0, hi=16, p=(0, 128), cs=1, step=1):
+        ap = T[name][p[0]:p[1], slice(c0, c1, cs if cs > 1 else None), slice(lo, hi, step if step > 1 else None)]
+        return (ap, name, (c0, c1, lo, hi), None, -(-(c1 - c0) // cs) * -(-(hi - lo) // step))
 
     def b2(name, c, lo, hi, p=(0, 128)):
         return (T[name][p[0]:p[1], c, lo:hi], name, (c, c + 1, lo, hi), None, hi - lo)
@@ -163,7 +161,7 @@ def rank_program(g, core, T, topo):
                     if not (psum and e2 != e):
                         if not (w or w2) or not hits(reg, r2):
                             continue
-                        if e2 == e and (e == "P" or not w2) and e in ENG:
+                        if e2 == e == "P":
                             continue
                     if deps.get(sem, (0, None))[0] < count:
                         deps[sem] = (count, snap)
@@ -183,8 +181,12 @@ def rank_program(g, core, T, topo):
         for w, lst in ((False, reads), (True, writes)):
             for name, reg, psum in lst:
                 keep = [x for x in hist.get(name, [])
-                        if not (inside(x[0], reg) and (w or (not x[1] and x[2] == e and x[3] == sem)))]
+                        if not (w and psum is False and inside(x[0], reg) and not strided(name)
+                                or (inside(x[0], reg) and x[1] == w and x[2] == e and x[3] == sem))]
                 hist[name] = keep + [(reg, w, e, sem, cnt[sem], snap)]
+
+    def strided(name):
+        return name in ("E0", "E1")
 
     def emit(e, f, out, ins):
         reads, writes = regions(ins + offsets(ins + [out])), regions([out])
@@ -202,10 +204,9 @@ def rank_program(g, core, T, topo):
             for name, reg, psum in lst:
                 for (r2, w2, j) in seen.get(name, []):
                     if nodes[j][0] == e == "P" and psum:
-                        if hits(reg, r2):
-                            before.setdefault(j, 0)
+                        before.setdefault(j, 0)
                     elif (psum and nodes[j][0] != e) or ((w or w2) and hits(reg, r2)):
-                        before[j] = max(before.get(j, 0), 1 if w2 or nodes[j][0] != e else 0)
+                        before[j] = 1
         for w, lst in ((False, reads), (True, writes)):
             for name, reg, psum in lst:
                 keep = [x for x in seen.get(name, []) if not (w and inside(x[0], reg) and not psum)]
@@ -215,18 +216,18 @@ def rank_program(g, core, T, topo):
 
     def op(e, f, out, ins, after=None):
         win = [x for x in ins if isinstance(x, tuple) and x[3]]
-        c = 0.00083 * max(x[4] for x in ins + [out] if isinstance(x, tuple))
+        c = 0.00087 * max(x[4] for x in ins + [out] if isinstance(x, tuple))
         if e == "G":
             dur = 0.15 + 2 * c
         elif out[3]:
             dur = 0.05 + 3.5 * c
         elif win:
-            dur = 0.06 + 1.56 * 0.00083 * out[4]
+            dur = 0.06 + 1.5 * 0.00087 * out[4]
         else:
             two = all(SCRATCH[x[1]][2] in (BF, U16) for x in ins + [out] if isinstance(x, tuple))
             both = len(ins) == 2 and all(isinstance(x, tuple) and x[4] == out[4] and SCRATCH[x[1]][0] == "sbuf" for x in ins)
-            dur = max(0.06, 0.05 + c * (0.5 if two else 2 if both else 1)) + (0.14 if e == "A" else 0)
-        node(e, lambda: emit(e, f, out, ins), regions(ins + offsets(ins + [out])), regions([out]), dur, 0.0, after)
+            dur = max(0.06, 0.05 + c * (0.5 if two and e == "V" else 2 if both else 1)) + (0.05 if e == "A" else 0)
+        return node(e, lambda: emit(e, f, out, ins), regions(ins + offsets(ins + [out])), regions([out]), dur, 0.0, after)
 
     def issue():
         tail, left, free, end, succ = [0.0] * len(nodes), [len(x[4]) for x in nodes], {}, {}, [[] for _ in nodes]
@@ -270,11 +271,14 @@ def rank_program(g, core, T, topo):
     def cp(out, a):
         op("V", lambda q: q.tensor_copy(A_(out), A_(a)), out, [a])
 
-    def scan(out, d0, d1, o0, o1):
-        op("V", lambda q: q.tensor_tensor_scan(A_(out), A_(d0), A_(d1), 0.0, o0, o1), out, [d0, d1])
+    def scan(out, d0, d1, o0, o1, first=0.0):
+        op("V", lambda q: q.tensor_tensor_scan(A_(out), A_(d0), A_(d1), first, o0, o1), out, [d0, d1, 0])
 
     def ms(out, v):
         op("V", lambda q: q.memset(A_(out), v), out, [])
+
+    def tr(out, a):
+        op("V", lambda q: q.transpose(A_(out), A_(a)), out, [a])
 
     def act(out, a, fn=AF.Copy, scale=1.0, bias=0.0):
         op("A", lambda q: q.activation(A_(out), A_(a), fn, bias=A_(bias), scale=A_(scale)), out, [a, scale, bias])
@@ -289,16 +293,10 @@ def rank_program(g, core, T, topo):
         emit("P", lambda q: q.matmul(A_(out), A_(l), A_(r), st, sp), out, [l, r])
         tiles[out[1]] = (tile, cnt["qP"])
 
-    def mm(out, l, r, st, sp, tile=None):
-        group.append((out, l, r, st, sp, tile))
-        if sp and not group[0][0] == "open":
-            close()
-
-    def close():
-        m = [x for x in group if x[0] != "open"]
-        group.clear()
+    def mms(*m):
+        m = [tuple(x) + (None,) * (6 - len(x)) for x in m]
         node("P", lambda: [mm_now(*x) for x in m], regions([x[1] for x in m] + [x[2] for x in m]), regions([x[0] for x in m]),
-             sum(0.02 + 0.00042 * max(64, x[0][4]) for x in m))
+             sum(0.02 + 0.00045 * max(64, x[0][4]) * (4 if SCRATCH[x[1][1]][2] == F32 else 1) for x in m))
 
     def iota(out, pat, base, cm, after=None):
         if SCRATCH[out[1]][2] == I32:
@@ -319,7 +317,7 @@ def rank_program(g, core, T, topo):
             sync(e, [], w)
             Q[e].dma_start(out[0], src).then_inc(T.sem["d_" + name], 16)
             note(e, [], w, "d_" + name, 16)
-        node(e, run, [], w, 0.1, 3.4 if out[4] > 700 else 2.4)
+        return node(e, run, [], w, 0.1, 3.6 if out[4] > 700 else 2.4)
 
     def store(e, dst, a, name):
         r = regions([a])
@@ -328,13 +326,14 @@ def rank_program(g, core, T, topo):
             sync(e, r, [])
             Q[e].dma_start(dst, a[0]).then_inc(T.sem["o_" + name], 16)
             note(e, r, [], "o_" + name, 16)
-        node(e, run, r, [], 0.1, 5.0 if name == "yt" else 2.0)
+        node(e, run, r, [], 0.1, 3.8 if name == "yt" else 2.0)
 
-    def send(m, src):
-        s, y, d = pl[(rank, m)]
-        to = d if y is None else y
+    small, big = helpers(T, topo, core)
+
+    def send(m, src, lats):
+        to = big if m == "F2" else T.cores[(rank + TO[m]) % len(T.cores)] if m == "U2D" else small
+        es = topo.engines(core, to) if m == "U2D" else near(topo, core, to, m)
         r = regions([src])
-        es = engines(topo, core, to, m)
         rid, pid = topo.addr(to, core)
 
         def run():
@@ -342,332 +341,363 @@ def rank_program(g, core, T, topo):
             g.remote_dma(land(T, m), src[0], T.sem["a_" + m], T.sem["l_" + m], pid, rid, bits(es))
             note("G", r, [], "l_" + m, len(es))
         k = node("G", run, r, [], 0.1)
-        for (r_, m_), (s_, y_, d_) in pl.items():
-            if d_ == core and m_ == m:
-                w = regions([b(m, 0, S) if m in TABLES else b(m)])
-                n = len(engines(topo, s_ if y_ is None else y_, d_, m))
-                lat = (1.7 + (9.0 if m in TABLES else 0.8 if src[4] > 100 else 0.0)) * (1 if y_ is None else 2)
-                node("n" + m, lambda: note("net", [], w, "a_" + m, n), [], w, 0.0, lat, k)
+        for x, lat in lats.items():
+            far = T.cores[(rank - TO[x]) % len(T.cores)]
+            by = far if x == "U2D" else helpers(T, topo, far)[x in ("F2", "F3")]
+            arrives(x, len(topo.engines(by, core)), lat, k)
         return k
 
-    load("S", b("EFI", 0, L), T.ef[:, 0:L], "ef0")
+    def arrives(x, n, lat, k):
+        w = regions([b(x, 0, S) if x in ("F2", "F3") else b(x)])
+        node("n" + x, lambda: note("net", [], w, "a_" + x, n), [], w, 0.0, lat, k)
+
+    load("S", b("ZF", 80, 288), T.zf[:, 0:L], "zf0")
+    load("A", b("EFI", 80, 304), T.ef[:, 0:224], "ef0")
+    load("S", b("EHI", 80, 304), T.eh[:, 0:224], "eh0")
     load("A", b("HT", 0, S), T.tab[:, :], "tab")
-    load("S", b("EHI", 0, L), T.eh[:, 0:L], "eh0")
-    load("S", b("ZF", 0, L), T.zf[:, 0:L], "zf0")
-    load("S", b("TC"), T.tab[:, :], "tc")
-    load("S", b("EFI", L, F), T.ef[:, L:F], "ef1")
-    load("S", b("EHI", L, F), T.eh[:, L:F], "eh1")
-    load("S", b("ZF", L, F), T.zf[:, L:F], "zf1")
+    for x, src, lo in (("ef", "EFI", 304), ("eh", "EHI", 304), ("zf", "ZF", 288)):
+        load("S", b(src, 0, 80), T[x][:, 544:F], x + "1")
+        load("S", b(src, lo, F), T[x][:, lo - 80:544], x + "2")
 
     ms(b("ONB"), 1.0)
     iota(b("PI"), [[0, 1]], 0, 1)
+    iota(b("C16"), [[16, 32]], 0, 0)
+    iota(b("PC"), [[0, 8], [1, 2]], 0, 0)
     iota(b("KIO"), [[0, 13], [1, 16]], 0, 0)
+    asel(b("ID"), b("ONB"), [[-1, 128]], OP.is_equal, 0, 1)
     asel(b("BA"), b("ONB"), [[-16, 8], [0, 16]], OP.is_ge, 0, 1)
     asel(b("BO"), b("BA"), [[16, 8], [0, 16]], OP.is_ge, 15, -1)
-    asel(b("ID"), b("ONB"), [[-1, 128]], OP.is_equal, 0, 1)
-    iota(b("EX0", 0, 13), [[16, 13]], 0, -1)
-    iota(b("EX1", 0, 13), [[16, 13]], -NB, -1)
     ts(b("PJ"), b("PI"), 15, OP.bitwise_and)
     ts(b("PK"), b("PI"), 4, OP.arith_shift_right, 1, OP.bitwise_and)
     cp(b("PM"), b("PJ"))
     cp(b("MH1"), b("PK"))
     ts(b("MH0"), b("MH1"), -1.0, OP.mult, 1.0, OP.add)
-    ts(b("PW"), b("PM"), -1.0, OP.mult, 11.0, OP.add)
-    act(b("PW"), b("PW"), AF.Exp, LN2)
-    for x in (0, 1):
-        ex = "EX%d" % x
-        ts(b(ex, 0, 13), b(ex, 0, 13), 60.0, OP.min, -60.0, OP.max)
-        act(b("W%d" % x, 0, 13), b(ex, 0, 13), AF.Exp, LN2)
-    ts(b("THR"), b("PW"), 2.5 / 2048.0, OP.mult)
-    ms(b("MB", 0, 1), 200.0)
-    ms(b("MB", 1, 2), -10.0)
+    ts(b("FW"), b("C16"), b("PM"), OP.add)
+    for i, v in enumerate((200.0, -11.0, 1.0, -200.0)):
+        ms(b("MB", i, i + 1), v)
+    for x in ("EH", "EF"):
+        ms(b(x, 0, 16), 0.0)
+        ms(b(x, 80, 96), 0.0)
+        ms(b(x, F + 16, F + 32), 0.0)
+    act(b("RKM"), b("KIO"), AF.Sigmoid, 400.0, b("MB", 3, 4))
     ms(b("WMU"), 0.0)
     ts(b("WMU", 15, 143, 16), b("BO", 0, 128, 16), float(PEN), OP.mult)
     ts(b("NBO"), b("BO"), -1.0, OP.mult)
-    ts(b("KAD"), b("KIO"), -2048.0, OP.mult, 30720.0, OP.add)
-    ts(b("RKM"), b("KIO"), 0.0, OP.is_gt)
+    act(b("IDF"), b("ID"))
+    ts(b("KAD"), b("KIO"), -4096.0, OP.mult, 61440.0, OP.add)
     ts(b("M16"), b("KIO"), b("PM"), OP.is_equal)
 
-    def pack(lo, hi):
-        ts(b("EE", lo, hi), b("EFI", lo, hi), 4096.0, OP.mult)
-        tt(b("EE", lo, hi), b("EE", lo, hi), b("EHI", lo, hi), OP.add)
+    def places(x):
+        nc, s = KINDS[x]
+        off = 32.0 * ((nc + 1) // 2) + 16
+        ts(b("RK", 0, s), b("FW", 0, s), 1.0 / s, OP.mult, 0.5 / s - 0.5, OP.add)
+        ts(b("RX", 0, s), b("RK", 0, s), -float(s), OP.mult)
+        tt(b("RC", 0, s), b("RX", 0, s), b("FW", 0, s), OP.add)
+        ts(b("RP", 0, s), b("RC", 0, s), 1, OP.bitwise_and)
+        ts(b("RX", 0, s), b("RP", 0, s), b("MH1"), OP.not_equal, off, OP.mult)
+        ts(b("RY", 0, s), b("RC", 0, s), 16.0, OP.mult)
+        tt(b("RX", 0, s), b("RX", 0, s), b("RK", 0, s), OP.add)
+        tt(b("RX", 0, s), b("RX", 0, s), b("RY", 0, s), OP.add)
+        ts(b("RO%d" % x, 0, s), b("RX", 0, s), 32.0 * (nc + 1) - 1, OP.min)
+        ts(b("RY", 0, nc), b("PC", 0, nc), b("MH1"), OP.not_equal, off, OP.mult)
+        tt(b("RY", 0, nc), b("RY", 0, nc), b("FW", 0, nc), OP.add)
+        cp(b("RQ%d" % x, 0, nc), b("RY", 0, nc))
 
-    def lists(x, c0, c1, t):
-        n0, n1 = 16 * c0, 16 * c1
-        ts(b3("I3", c0, c1, 0, 16), x, b("MH0"), OP.mult)
-        act(b3("I3", c0, c1, 16, 32), x, scale=b("MH1"))
-        y, i3 = b3("Y3", c0, c1, 0, 32), b3("I3", c0, c1, 0, 32)
-        op("V", lambda q: q.transpose(T.Y3[:, c0:c1, :], T.I3[:, c0:c1, :]), y, [i3])
-        tt(b3("XI", c0, c1, 0, 16), b3("Y3", c0, c1, 0, 16), b3("Y3", c0, c1, 16, 32), OP.add)
-        ts(b2("HF", 0, n0, n1), b3("XI", c0, c1, 0, 16), 2047, OP.bitwise_and)
-        ts(b2("HF", 1, n0, n1), b3("XI", c0, c1, 0, 16), 12, OP.arith_shift_right, 2047, OP.bitwise_and)
-        cp(b3("LI%d" % t, 0, 2, n0, n1), b3("HF", 0, 2, n0, n1))
-
-    def half(t, x):
-        return lambda lo, hi: b2("LI%d" % t, x, lo, hi)
-
-    def keyadd(c0, c1, t):
-        n0, n1 = 16 * c0, 16 * c1
-        tt(b("KA%d" % t, n0, n1), b("KAD", n0, n1), b2("HF", 0, n0, n1), OP.add)
-
-    def expand(z, src, c0, c1, cp=cp):
-        cp(b3(z, c0, c1, 0, 16), src)
-        for w in (16, 32, 64, 128):
-            cp(b3(z, c0, c1, w, 2 * w), b3(z, c0, c1, 0, w))
+    def lists(x, src, lo, y, out, key=None):
+        nc, s = KINDS[x]
+        n1, n2 = 32 * ((nc + 1) // 2), 32 * (nc // 2 + 1)
+        tr(b(y, 0, n1), b(src, lo, lo + n1))
+        tr(b(y, n1, n1 + n2), b(src, lo - 16, lo - 16 + n2))
+        cp(b(out, 0, 16 * s), ind(b(y, 0, n1 + n2), b("RO%d" % x, 0, s)))
+        if key:
+            tt(key, ind(b(y, 0, n1 + n2), b("RQ%d" % x, 0, nc)), b("KAD", 0, 16 * nc), OP.add)
 
     bank = [0]
 
-    def bulk(win, lst, z, cm, vch, ach):
-        for c0, c1 in ach:
-            w = 256 * (c1 - c0)
+    def look(x, win, lst, z, cm, c0, chunks, k1):
+        nc, s = KINDS[x]
+        k = 0
+        for k0, k in chunks:
+            n = k - k0
             ga, t = "GA%d" % (bank[0] % 3), "T%d" % (bank[0] % 6)
             bank[0] += 1
-            act(b(ga, 0, w), ind(b(win, 0, S), lst(16 * c0, 16 * c1)), scale=-1.0)
-            mm(b(t, 0, w), b("ID"), b3(z, c0, c1, 0, 256), True, False)
-            mm(b(t, 0, w), b("ID"), b(ga, 0, w), False, True)
-            act(b(cm, 256 * c0, 256 * c1), b(t, 0, w), AF.Sigmoid, 400.0, b("MB", 0, 1))
-        for c0, c1 in vch:
-            for c in range(c0, c1):
-                tt(b(cm, 256 * c, 256 * c + 256), ind(b(win, 0, S), lst(16 * c, 16 * c + 16)), b2(z, c, 0, 256), OP.is_le)
+            act(b(ga, 0, 16 * s * n), ind(win, b(lst, s * k0, s * k)), scale=-1.0)
+            m = []
+            for j in range(n):
+                o = b3(t, 0, nc * n, j, 16, step=n)
+                m += [(o, b("ID"), z, True, False), (o, b("ID"), b(ga, 16 * s * j, 16 * (s * j + nc)), False, True)]
+            mms(*m)
+            act(b3(cm, 16 * c0, 16 * (c0 + nc), k0, k), b3(t, 0, nc * n), AF.Sigmoid, 400.0, b("MB", 0, 1))
+        for j in range(k, k1):
+            lo, hi = 16 * c0, 16 * (c0 + nc)
+            tt((T[cm][:, lo:hi, j], cm, (lo, hi, j, j + 1), None, hi - lo), ind(win, b(lst, s * j, s * j + nc)), z, OP.is_le)
 
-    def psum(cm, dst, *cuts):
-        for c0, c1 in zip(cuts, cuts[1:]):
-            for m in range(16):
-                mm(b(dst, 16 * c0, 16 * c1), b("WMU", 15 - m, 143 - m), b(cm, 256 * c0 + m, 256 * c1, 16), m == 0, m == 15)
+    def pairs(n, w):
+        return [(k, min(n, k + w)) for k in range(0, n, w)]
 
-    def home_max(t):
-        tt(b("HK"), b("PH", 0, L), b("KA%d" % t), OP.add)
-        scan(b("HS"), b("RKM"), b("HK"), OP.mult, OP.max)
-        cp(b("HKI", 0, 13), b("HS", 15, L, 16))
-        ts(b("HSL", 0, 13), b("HKI", 0, 13), 2047, OP.bitwise_and)
-        ts(b("A1", 0, 13), b("HKI", 0, 13), float(9 * PEN), OP.is_ge, float(9 * PEN), OP.mult)
+    def sums(cm, c0, c1, key):
+        out = b("PH", 16 * c0, 16 * c1)
+        mms((out, b("IDF"), key, True, False))
+        mms(*[(out, b("WMU", 15 - m, 143 - m), b3(cm, 16 * c0 + m, 16 * c1, cs=16), False, m == 15) for m in range(16)])
+
+    def far_max(c0, c1, k0, k1, lo, out, other):
+        n = k1 - k0
+        hi = lo + n * (c1 - c0)
+        mms(*[(b("PF", lo, hi), b("WMU", 15 - m, 143 - m), b3("CMF", 16 * c0 + m, 16 * c1, k0, k1, cs=16), m == 0, m == 15)
+              for m in range(16)])
+        scan(b("FS", lo, hi), b("RKM" if n == 16 else "RK8", 0, hi - lo), b("PF", lo, hi), OP.mult, OP.max)
+        tt(out, b("FS", lo + n - 1, hi, n), other, OP.max)
+
+    def home_max():
+        top = b("HS", 15, L, 16)
+        scan(b("HS"), b("RKM"), b("PH", 0, L), OP.mult, OP.max)
+        cp(b("HKI", 0, 13), top)
+        ts(b("A1", 0, 13), top, 0.5 - 9 * PEN, OP.add, 4.0 * BIG, OP.mult)
+        ts(b("HSL", 0, 13), b("HKI", 0, 13), S - 1, OP.bitwise_and)
+        tt(b("A1", 0, 13), b("A1", 0, 13), top, OP.min)
         ts(b("AP", 0, 13), b("HSL", 0, 13), float(OKB), OP.add)
         tt(b("AP", 0, 13), b("AP", 0, 13), b("A1", 0, 13), OP.max)
 
-    JOBS = []
-    for h in (0, 1):
-        for a in (h, 2 + h):
-            JOBS += [(2 * a, "T%d" % a, 0, 0), (2 * a + 1, "T%d" % a, L, 0)]
-        JOBS += [(2 * h + x, "T4", 192 * h + 96 * x, 1) for x in (0, 1)]
-        JOBS += [(4 + 2 * h + x, ("T5", "PF")[h], L * h + 96 * x, 1) for x in (0, 1)]
+    CS = b("PF", 224, 237)
 
-    def decide(t, kf):
-        tt(b("YY", 0, 13), b("AP", 0, 13), kf, OP.max)
-        ts(b("IX", 0, 13), b("YY", 0, 13), float(OKB + S), OP.min, float(OKB), OP.subtract)
-        act(b("B1"), ind(b("CT1", 0, S + 16), b("IX", 0, 13)))
-        cp(b("B0"), ind(b("CT0", 0, S + 16), b("IX", 0, 13)))
-        for gg, t_, o, blk in JOBS:
-            pp, lo, n = (32 * (gg // 2), 32 * (gg // 2) + 32), (0, NB)[blk], (NB, 96)[blk]
-            bb = "B%d" % (gg % 2)
-            mm(b(t_, o, o + L - lo, p=(0, n)), b(bb, lo, lo + n, p=pp), b(bb, lo, L, p=pp), True, True, gg // 2)
-        for gg, t_, o, blk in JOBS:
-            w, pp = (L, 96)[blk], (0, (NB, 96)[blk])
-            out = b3("E%d" % blk, 0, (13, 6)[blk], 16 * gg, 16 * gg + 16, p=pp)
-            if t_ in ("T2", "T3", "PF"):
-                act(out, b(t_, o, o + w, p=pp), AF.Relu, 1.0, b("MB", 1, 2, p=pp))
+    def orders():
+        for a in range(4):
+            pp = (32 * a, 32 * a + 32)
+            mms((b3("T%d" % a, 0, 26), b("JA", 0, NB, p=pp), b("JB", p=pp), True, False, a))
+        for h in range(2):
+            pp = (64 * h, 64 * h + 32)
+            mms((b3("T%d" % (4 + h), 0, 20, p=(0, 80)), b("JA", NB, L, p=pp), b("JC", p=pp), True, False, 2 * h))
+
+    def decide(t, yy, grown):
+        ts(b("IX", 0, 13), yy, float(OKB + S), OP.min, float(OKB), OP.subtract)
+        act(b("B1"), ind(b("CT", 0, S + 16), b("IX", 0, 13)), scale=b("MH1"))
+        ts(b("B0"), ind(b("CT", 0, S + 16), b("IX", 0, 13)), b("MH0"), OP.mult)
+        for a in (0, 2, 1, 3):
+            pp = (32 * a, 32 * a + 32)
+            mms(*[(b3("T%d" % a, x, 26, cs=2), b("B%d" % x, 0, NB, p=pp), b("B%d" % x, p=pp), False, x == 1, a) for x in (0, 1)])
+            mms(*[(b3("T%d" % (4 + a // 2), 2 * (a % 2) + x, 20, cs=4, p=(0, 80)), b("B%d" % x, NB, L, p=pp),
+                   b("B%d" % x, NB, L, p=pp), False, x == 1 and a % 2 == 1, a) for x in (0, 1)])
+        for a in range(6):
+            if a < 4:
+                out, src = b3("E0", 0, 13, 32 * a, 32 * a + 32), b3("T%d" % a, 0, 26)
             else:
-                ts(out, b(t_, o, o + w, p=pp), 10.5, OP.is_ge)
-        ts(b("D0", 0, 13), b("YY", 0, 13), float(-OKB), OP.add)
-        group.append(("open",))
-        for c in range(13):
-            mm(b("PH", 416 + c, 417 + c), b2("E0", c, 0, 128, p=(0, NB)), b("W0", c, c + 1, p=(0, NB)), True, c < 7)
-            if c >= 7:
-                mm(b("PH", 416 + c, 417 + c), b2("E1", c - 7, 0, 128, p=(0, 96)), b("W1", c, c + 1, p=(0, 96)), False, True)
-        close()
-        tt(b("WM", 0, 13), b("HS", 15, L, 16), kf, OP.max)
-        cp(b("WI", 0, 13), b("WM", 0, 13))
-        ts(b("WS", 0, 13), b("WI", 0, 13), 15, OP.arith_shift_right)
-        ts(b("WR", 0, 13), b("WS", 0, 13), 9.0, OP.is_ge)
-        tt(b("WV", 0, 13), b("WR", 0, 13), b("WS", 0, 13), OP.mult)
-        tt(b("XB"), ind(b("WV", 0, 16), b("BL", 0, 13)), b("M16"), OP.mult)
-        mm(b("PF", L, 2 * L), b("BO"), b("XB"), True, True)
-        ts(b("L1", 0, 13), b("PH", 416, 429), b("THR"), OP.is_gt, 4096.0, OP.mult)
-        tt(b("D2", 0, 13), b("L1", 0, 13), b("D0", 0, 13), OP.max)
-        tt(b("DS%d" % t, 0, 13), b("D2", 0, 13), b("DU%d" % t, 0, 13), OP.min)
-        cp(b("DT%d" % t, 0, 13), b("DS%d" % t, 0, 13))
-
-    def ranks(n):
-        scan(b("UC", 0, n), b("ON32", 0, n), b("UU", 0, n), OP.mult, OP.add)
-        group.append(("open",))
-        mm(b("PF", 416, 416 + n), b("BO"), b("UC", 0, n), True, False)
-        mm(b("PF", 416, 416 + n), b("NT"), b("UU", 0, n), False, True)
-        mm(b("PF", 448, 449), b("BO"), b("UC", n - 1, n), True, True)
-        close()
+                out, src = b3("E1", 0, 5, 64 * a - 256, 64 * a - 192, p=(0, 80)), b3("T%d" % a, 0, 20, p=(0, 80))
+            if a in (2, 3, 5):
+                act(out, src, AF.Relu, 1.0, b("MB", 1, 2, p=(0, 80 if a == 5 else 128)))
+            else:
+                ts(out, src, 11.0 + 1.0 / 256, OP.is_gt)
+        mms((CS, b("IDF"), yy, True, False))
+        mms(*[(b("PF", 224 + c, 225 + c), b2("E0", c, 0, 128), b("BW"), False, False) for c in range(13)])
+        mms(*[(b("PF", 224 + c, 225 + c), b2("E1", c - 8, 0, 128, p=(0, 80)), b("BW", p=(0, 80)), False, c == 12) for c in range(8, 13)])
+        ts(b("WI", 0, 13), yy, 1.0 / PEN, OP.mult, -0.49999, OP.add)
+        cp(b("WU", 0, 13), b("WI", 0, 13))
+        act(grown, ind(b("TW"), b("WU", 0, 13)))
+        tt(b("DS", 0, 13), CS, b("DU%d" % t, 0, 13), OP.min)
+        ts(b("DT%d" % t, 0, 13), b("DS", 0, 13), float(OKB), OP.subtract)
 
     def lanes(t, n, fill, val):
         pls, lw, lu = "PL%d" % t, "LW%d" % t, "LU%d" % t
-        ts(b("TB"), b("PF", 448, 449), -1.0, OP.mult, float(fill), OP.add)
-        tt(b("QQ", 0, n), b("PF", 416, 416 + n), b("NU", 0, n), OP.max)
+        scan(b("UC", 0, n), b("ON32", 0, n), b("UU", 0, n), OP.mult, OP.add)
+        mms((b("PH", 224, 224 + n), b("BO"), b("UC", 0, n), True, False), (b("PH", 224, 224 + n), b("NT"), b("UU", 0, n), False, True),
+            (b("PH", 256, 257), b("BO"), b("UC", n - 1, n), True, True))
+        ts(b("NU", 0, n), b("UU", 0, n), 0.5, OP.is_lt)
+        tt(b("NU", 0, n), b("NU", 0, n), b("DMF", 0, n), OP.mult)
+        tt(b("QQ", 0, n), b("PH", 224, 224 + n), b("NU", 0, n), OP.max)
         cp(b(pls, 0, n), b("QQ", 0, n))
-        act(b(lw, 80, 208), b("L128"), AF.Identity, 1.0, b("TB"))
-        cp(ind(b(lw, 80, 80 + 1024), b(pls, 0, n)), val)
-        tt(b("XM"), b(lw, 80, 208), b("M16", 0, 128), OP.mult)
-        scan(b("XS"), b("RKM", 0, 128), b("XM"), OP.mult, OP.add)
+        ts(b("TB"), b("PH", 256, 257), -1.0, OP.mult, float(fill), OP.add)
+        scat(lw, 1024, pls, n, val)
+        act(b("LD"), b("LM"), AF.Relu, 1.0, b("TB"))
+        scan(b("XS"), b("LD"), b(lw, 0, 128), OP.max, OP.min)
         cp(b(lu, 0, 8), b("XS", 15, 128, 16))
 
-    AS, VS = [(0, 2), (2, 3)], [(3, 5)]
-    AD, VD = [(9, 11), (5, 6)], [(6, 9), (11, 13)]
-    A0, V0 = [(0, 2), (2, 3), (9, 11)], [(3, 9), (11, 13)]
+    def wrap(x):
+        act(b(x, S, S + PAD), b(x, 0, PAD))
 
     def step(t, ftab, update, later):
-        lu, hl, fl, z = "LU%d" % t, half(t, 0), half(t, 1), "Z16%d" % t
-        bulk("HT", hl, z, "CMH", VS, AS)
-        act(b("DQ"), ind(b("D"), b(lu, 0, 8)), scale=4097.0)
-        act(b("ZL%d" % t, 80, L), ind(b("ZF"), b(lu, 0, 8)))
-        tt(b("XE"), ind(b("EE"), b(lu, 0, 8)), b("DQ"), OP.add)
-        lists(b("XE"), 5, 13, t)
+        lu, zl = b("LU%d" % t, 0, 8), "ZL%d" % t
+        home, far = b("HT", 0, S + PAD), b(ftab, 0, S + PAD)
+        look(1, home, "LSH%d" % t, b(zl, 0, 80), "CMH", 0, pairs(16, 4), 16)
+        act(b("DQ"), ind(b("D"), lu))
+        act(b(zl, 80, L), ind(b("ZF"), lu))
+        tt(b("XH", 16, 144), ind(b("EH", 16, 16 + F), lu), b("DQ"), OP.add)
+        lists(2, "XH", 16, "YH", "LDH", b("KA%d" % t, 80, L))
+        tt(b("XF", 16, 144), ind(b("EF", 16, 16 + F), lu), b("DQ"), OP.add)
+        lists(2, "XF", 16, "YF", "LDF")
+        act(b("LF%d" % t, 80, L), ind(b("FQ"), lu))
         update()
-        bulk(ftab, fl, z, "CMF", VS, AS)
-        psum("CMH", "PH", 0, 5)
-        expand(z, b("ZL%d" % t, 80, L), 5, 13)
-        keyadd(5, 13, t)
-        bulk("HT", hl, z, "CMH", VD, AD)
-        psum("CMF", "PF", 0, 5)
-        bulk(ftab, fl, z, "CMF", VD, AD)
-        psum("CMH", "PH", 5, 9, 13)
-        psum("CMF", "PF", 5, 9)
-        home_max(t)
-        psum("CMF", "PF", 9, 13)
-        later()
-        scan(b("FS"), b("RKM"), b("PF", 0, L), OP.mult, OP.max)
-        decide(t, b("FS", 15, L, 16))
+        sums("CMH", 0, 5, b("KA%d" % t, 0, 80))
+        look(1, far, "LSF%d" % t, b(zl, 0, 80), "CMF", 0, pairs(16, 4), 16)
+        look(2, home, "LDH", b(zl, 80, L), "CMH", 5, pairs(KAD_, 4), 16)
+        sums("CMH", 5, 13, b("KA%d" % t, 80, L))
+        look(2, far, "LDF", b(zl, 80, L), "CMF", 5, pairs(KAD_, 4), 16)
+        home_max()
+        far_max(0, 5, 0, 16, 0, b("YY", 0, 5), b("AP", 0, 5))
+        far_max(5, 13, 0, 8, 80, b("AP", 5, 13), b("AP", 5, 13))
+        far_max(5, 13, 8, 16, 144, b("YY", 5, 13), b("AP", 5, 13))
+        orders()
+        later(b("YY", 0, 13))
 
-    send("RQZ", b("ZF", 0, L))
-    send("U3Z", b("ZF", 0, L))
-    send("U2Z", b("ZF", 0, L))
-    pack(0, L)
-    lists(b("EE", 0, L), 0, 13, 0)
-    asked = send("RQL", b2("LI0", 1, 0, L))
-    expand("Z160", b("ZF", 0, L), 0, 13)
-    keyadd(0, 13, 0)
-    send("F2", b("TC"))
-    send("F3", b("TC"))
+    z0 = b("ZF", 80, 288)
+    send("RQZ", z0, {"RQZ": 4.5, "U2Z": 7.0, "U3Z": 7.0})
+    places(0)
+    cp(b("EF", 96, 320), b("EFI", 80, 304))
+    lists(0, "EF", 96, "YF", "LF0")
+    asked = send("RQL", b("LF0"), {"RQL": 3.6})
+    cp(b("EH", 96, 320), b("EHI", 80, 304))
+    lists(0, "EH", 96, "YH", "LH0", b("KA0"))
+    send("F2", b("HT", 0, S), {"F2": 12.0, "F3": 20.0})
     asel(b("NT"), b("NBO"), [[-1, 128]], OP.is_ge, 0, 1)
     iota(b("CL", 0, 256), [[1, 256]], 0, 0)
     iota(b("CL", 256, 264), [[256, 8]], 0, 0)
-    iota(b("C16", 0, 26), [[16, 26]], 0, 0)
-    iota(b("BLF", 0, 13), [[1, 13]], 0, 0)
-    iota(b("F2V", 0, 80), [[1, 80]], 544, 0)
-    iota(b("F2V", 80, 416), [[1, 336]], 0, 0, asked)
-    bulk("HT", half(0, 0), "Z160", "CMH", V0, A0)
-    expand("ZR", b("RQZ"), 0, 13)
-    bulk("HT", lambda lo, hi: b("RQL", lo, hi), "ZR", "CMF", V0, A0)
-    psum("CMH", "PH", 0, 5, 9, 13)
-    psum("CMF", "PF", 0, 5, 9, 13)
-    cp(b("PX"), b("PW"))
-    cp(b("PY"), b("PX"))
-    ts(b("CI"), b("CL"), b("PY"), OP.mult)
+    iota(b("JA"), [[1, L]], 0, 0, asked)
+    iota(b("JB"), [[16, 13], [0, 2], [1, 16]], 0, 0, asked)
+    iota(b("JC"), [[16, 5], [0, 4], [1, 16]], NB, 0, asked)
+    iota(b("TW"), [[1, 32]], 0, 0)
+    for x in range(0, WT, 676):
+        iota(b("OC", x, x + 676), [[0, 676]], -1, 0, asked)
+    tab = b("HT", 0, S)
+    look(0, tab, "LH0", z0, "CMH", 0, pairs(KA0, 2), 16)
+    look(0, tab, "RQL", b("RQZ"), "CMF", 0, pairs(KR0, 2), 16)
+    sums("CMH", 0, 13, b("KA0"))
+    ms(b("KFO"), 0.0)
+    cp(b("RK8"), b("RKM", 0, L, 2))
+    far_max(0, 13, 0, 8, 0, b("KFO", 0, 13), b("KFO", 0, 13))
+    far_max(0, 13, 8, 16, 104, b("KFO", 0, 13), b("KFO", 0, 13))
+    told = send("KFR", b("KFO"), {"KFR": 3.2})
+    home_max()
+    ms(b("P2"), 0.5)
+    ms(b("ON32"), 1.0)
+    ms(b("Q1"), 0.0)
+    scan(b("P3"), b("P2"), b("Q1"), OP.mult, OP.add, 4096.0)
+    tt(b("P2"), b("P3"), b("M16", 0, 16), OP.mult)
+    scan(b("P3"), b("ON32", 0, 16), b("P2"), OP.mult, OP.add)
+    ts(b("CI"), b("CL"), b("P3", 15, 16), OP.mult)
     ts(b("CJ"), b("CI"), 2048, OP.bitwise_and)
     ts(b("CB"), b("CJ"), 1.0 / 1024.0, OP.mult, -1.0, OP.add)
-    ts(b("ML", 2, 3), b("PM"), 8.0, OP.is_lt)
-    ts(b("MH", 2, 3), b("PM"), 11.0, OP.is_lt)
-    tt(b("MH", 2, 3), b("MH", 2, 3), b("ML", 2, 3), OP.subtract)
-    for x in (0, 1):
-        tt(b("ML", x, x + 1), b("ML", 2, 3), b("MH%d" % x), OP.mult)
-        tt(b("MH", x, x + 1), b("MH", 2, 3), b("MH%d" % x), OP.mult)
-        ts(b2("LB", x, 0, 256), b("CB", 0, 256), b("ML", x, x + 1), OP.mult)
-        ts(b2("HB", x, 0, 8), b("CB", 256, 264), b("MH", x, x + 1), OP.mult)
-        ms(b("CT%d" % x, S, S + 16), 0.0)
-    ms(b("KFO"), 0.0)
-    scan(b("FS"), b("RKM"), b("PF", 0, L), OP.mult, OP.max)
-    cp(b("KFO", 0, 13), b("FS", 15, L, 16))
-    told = send("KFR", b("KFO"))
-    home_max(0)
-    iota(b("LW1", 0, 80), [[1, 80]], 544, 0, told)
-    iota(b("LW2", 0, 80), [[1, 80]], 464, 0, told)
-    iota(b("L128"), [[1, 128]], 0, 0)
-    for x in range(0, WT, 704):
-        iota(b("OC", x, x + 704), [[0, 704]], -1, 0, told)
-    for x in (0, 512):
-        iota(b("LVF", x, x + 512), [[0, 512]], x // 8, 0, told)
-        iota(b("LVW", x, x + 512), [[0, 512]], 0, 0, told)
+    ts(b("ML", 0, 1), b("PM"), 8.0, OP.is_lt)
+    ts(b("ML", 1, 2), b("PM"), 11.0, OP.is_lt)
+    tt(b("ML", 1, 2), b("ML", 1, 2), b("ML", 0, 1), OP.subtract)
+    ts(b("LB"), b("CB", 0, 256), b("ML", 0, 1), OP.mult)
+    ts(b("HB"), b("CB", 256, 264), b("ML", 1, 2), OP.mult)
+    ms(b("CT", S, S + 16), 0.0)
     for h in range(8):
-        act(b("CT1", 256 * h, 256 * h + 256), b2("LB", 1, 0, 256), AF.Identity, 1.0, b2("HB", 1, h, h + 1))
-        ts(b("CT0", 256 * h, 256 * h + 256), b2("LB", 0, 0, 256), b2("HB", 0, h, h + 1), OP.add)
-    ts(b("FW", 0, 26), b("C16", 0, 26), b("PM"), OP.add)
+        ts(b("CT", 256 * h, 256 * h + 256), b("LB"), b("HB", h, h + 1), OP.add)
+    ts(b("PJ"), b("PI"), 31, OP.bitwise_and)
+    ts(b("MC", 0, 1), b("PJ"), 0.0, OP.is_equal)
+    ts(b("MC", 1, 2), b("PJ"), 1.0, OP.is_equal, -1.0, OP.mult)
+    ts(b("MC", 2, 3), b("PJ"), 0.0, OP.is_equal, 1.0 / 128, OP.mult)
+    ts(b("MC", 3, 4), b("PJ"), 1.0, OP.is_equal, 1.0 / 128, OP.mult)
+    act(b("JA"), b("JA"), AF.Identity, b("MC", 1, 2), b("MC", 0, 1))
+    act(b("JB"), b("JB"), AF.Identity, b("MC", 2, 3), b("MC", 3, 4))
+    act(b("JC"), b("JC"), AF.Identity, b("MC", 2, 3), b("MC", 3, 4))
+    ms(b("BW"), BIG)
+    cp(b("T01"), b("TW", 0, 16))
+    ts(b("NU"), b("TW"), 9.0, OP.is_ge)
+    tt(b("TW"), b("TW"), b("NU"), OP.mult)
+    iota(b("FQ", 80, F), [[1, F - 80]], 0, 0, told)
+    iota(b("QV"), [[1, 416]], 0, 0, told)
+    iota(b("FQ", 0, 80), [[1, 80]], 544, 0, told)
+    iota(b("LF1", 0, 80), [[1, 80]], 544, 0, told)
+    iota(b("LF2", 0, 80), [[1, 80]], 464, 0, told)
+    iota(b("LM"), [[1, 128]], 0, 0, told)
+    ts(b("LM"), b("LM"), BIG, OP.add)
+    tt(b("LM"), b("LM"), b("M16", 0, 128), OP.mult)
+    ts(b("LM"), b("LM"), -BIG, OP.add)
     for t in range(3):
-        ts(b("DU%d" % t, 0, 13), b("FW", 0, 13), float(S + 256 * t), OP.add)
-    ts(b("DMF", 0, 26), b("FW", 0, 26), 512.0, OP.add)
-    cp(b("BL", 0, 13), b("BLF", 0, 13))
-    for n_, v_ in (("WV", 0.0), ("WN", 0.0), ("DT0", 0), ("DT1", 0), ("ON32", 1.0), ("D", 0.0), ("BP", 0.0)):
+        ts(b("DU%d" % t, 0, 13), b("FW", 0, 13), float(OKB + S + PAD + L * t), OP.add)
+    ts(b("DUQ", 0, 13), b("FW", 0, 13), float(OKB + S + F), OP.add)
+    ts(b("DMF"), b("FW"), 512.0, OP.add)
+    for n_, v_ in (("DT0", 0), ("DT1", 0), ("D", 0.0)):
         ms(b(n_), v_)
-    pack(L, F)
-    for t, f0 in ((1, 544), (2, 464)):
-        lists(b("EE", f0, f0 + 80), 0, 5, t)
-        keyadd(0, 5, t)
-        act(b("ZL%d" % t, 0, 80), b("ZF", f0, f0 + 80))
-        expand("Z16%d" % t, b("ZF", f0, f0 + 80), 0, 5, act)
-    decide(0, b("KFR", 0, 13))
-    send("U2D", b("DT0"))
-    send("U3D", b("DT0"))
+    for n_, lo, hi, v_ in (("XH", 0, 16, 0.0), ("XH", 144, 160, 0.0), ("XF", 0, 16, 0.0), ("XF", 144, 160, 0.0),
+                           ("BP", L, 336, 0.0), ("LVF", L, 592, 1.0), ("LVF", 592, 1104, 0.0),
+                           ("LVW", L, 1104, 0.0), ("LW1", 0, 128, BIG), ("LW2", 0, 128, BIG)):
+        ms(b(n_, lo, hi), v_)
+    places(1)
+    places(2)
+    for x in ("EH", "EF"):
+        cp(b(x, 16, 96), b(x + "I", 0, 80))
+        cp(b(x, 320, F + 16), b(x + "I", 304, F))
+    for t, q0 in ((1, 0), (2, 544)):
+        lists(1, "EH", 16 + q0, "YS", "LSH%d" % t, b("KA%d" % t, 0, 80))
+        lists(1, "EF", 16 + q0, "YT", "LSF%d" % t)
+        act(b("ZL%d" % t, 0, 80), b("ZF", q0, q0 + 80))
+    orders()
+    tt(b("YY", 0, 13), b("AP", 0, 13), b("KFR", 0, 13), OP.max)
+    decide(0, b("YY", 0, 13), b("D", 80, 288))
+    send("U2D", b("DT0"), {"U2D": 1.8})
+    send("U3D", b("DT0"), {"U3D": 3.2})
 
-    ts(b("UU", 0, 13), b("DS0", 0, 13), float(S), OP.is_ge)
-    ranks(13)
-    ts(b("NU", 0, 13), b("DS0", 0, 13), float(S), OP.is_lt)
-    tt(b("NU", 0, 13), b("NU", 0, 13), b("DMF", 0, 13), OP.mult)
-    scat("HT", WT, "DT0", 13, b("ZF", 0, L))
-    lanes(1, 13, 208, b("F2V", 80, 288))
-    act(b("D", 0, L), b("PF", L, 2 * L))
+    ts(b("UU", 0, 13), CS, float(OKB + S), OP.is_ge)
+    scat("HT", WT, "DT0", 13, z0)
+    wrap("HT")
+    lanes(1, 13, 288, b("QV", 80, 288))
 
     def update1():
-        send("V3Z", b("ZL1"))
+        send("V3Z", b("ZL1"), {"V3Z": 3.6})
         scat("F2", WT, "U2D", 13, b("U2Z"))
+        wrap("F2")
 
-    def later1():
-        scat("OC", WT, "DT0", 13, b("F2V", 80, 288))
+    def later1(yy):
+        scat("OC", WT, "DT0", 13, b("FQ", 80, 288))
         scat("F3", WT, "U3D", 13, b("U3Z"))
+        ts(b("A1", 0, 8), b("FW", 13, 21), b("TB"), OP.subtract, 80.0, OP.add)
+        cp(b("PL1", 13, 21), b("A1", 0, 8))
+        decide(1, yy, b("LVW", 0, L))
     step(1, "F2", update1, later1)
-    send("V3D", b("DT1"))
+    send("V3D", b("DT1"), {"V3D": 3.2})
 
-    ts(b("WN", 0, 13), b("DS1", 0, 13), float(S), OP.is_lt, 64.0, OP.mult)
-    tt(b("XB"), ind(b("WN", 0, 16), b("BL", 0, 13)), b("M16"), OP.mult)
-    mm(b("PH", L, 2 * L), b("BO"), b("XB"), True, True)
-    act(b("LVF", 0, 128), b("PH", L + 80, 2 * L))
-    act(b("LVW", 0, 128), b("PF", L + 80, 2 * L))
-    act(b("D", 544, F), b("PF", L, L + 80))
-    ts(b("TU"), b("TB"), -1.0, OP.mult)
-    ts(b("PL1", 13, 21), b("FW", 13, 21), b("TU"), OP.add)
-    scat("OC", WT, "DT1", 13, b("LW1", 0, L))
-    tt(b("BP", 0, L), ind(b("OC"), b("DT0", 0, 13)), b("F2V", 80, 288), OP.not_equal)
-    ts(b("UF"), ind(b("LVF"), b("PL1", 0, 21)), 64.0, OP.is_lt)
-    for x in ("BP", "UF"):
-        for m in range(16):
-            mm(b("PH", 450, 471), b("WMU", 15 - m, 143 - m), b(x, m, 336, 16), x == "BP" and m == 0, x == "UF" and m == 15)
-    ts(b("UU", 0, 5), b("DS1", 0, 5), float(S), OP.is_ge)
+    ts(b("UL", 0, 13), CS, float(OKB + S), OP.is_ge)
+    ts(b("UU", 0, 5), b("PF", 224, 229), float(OKB + S), OP.is_ge)
+    act(b("LVF", 0, L), ind(b("T01"), b("UL", 0, 13)))
+    act(b("UF", 0, 336), ind(b("LVF", 80, 1104), b("PL1", 0, 21)))
+    scat("OC", WT, "DT1", 13, b("LF1"))
+    tt(b("BP", 0, L), ind(b("OC"), b("DT0", 0, 13)), b("FQ", 80, 288), OP.not_equal)
     scat("HT", WT, "DT1", 13, b("ZL1"))
-    act(b("GW"), ind(b("LVW"), b("PL1", 0, 21)))
-    ts(b("UU", 5, 26), b("PH", 450, 471), 1.0, OP.is_ge)
-    ranks(26)
-    ts(b("NU", 0, 26), b("UU", 0, 26), -1.0, OP.mult, 1.0, OP.add)
-    tt(b("NU", 0, 26), b("NU", 0, 26), b("DMF", 0, 26), OP.mult)
-    lanes(2, 26, 336, b("F2V"))
-    for i, x in enumerate(("D", "GW", "BP")):
-        mm(b("T5", 0, 336), b("ID"), b(x, 0, 336), i == 0, i == 2)
-    act(b("D", 0, 336), b("T5", 0, 336))
+    wrap("HT")
+    for x in ("UF", "BP"):
+        mms(*[(b("PH", 288, 309), b("WMU", 15 - m, 143 - m), b(x, m, 336, 16), x == "UF" and m == 0, x == "BP" and m == 15)
+              for m in range(16)])
+    ts(b("UU", 5, 26), b("PH", 288, 309), 1.0, OP.is_ge)
+    lanes(2, 26, 416, b("QV"))
+    act(b("GW"), ind(b("LVW", 80, 1104), b("PL1", 0, 21)))
+    act(b("D", 0, 80), b("LVW", 0, 80))
+    mms(*[(b3("T5", 0, 21), b("ID"), x, i == 0, i == 2)
+          for i, x in enumerate((b("D", 80, 416), b("GW"), b("BP", 0, 336)))])
+    act(b("D", 80, 416), b3("T5", 0, 21))
 
-    def later2():
-        ts(b("NB1"), b("BP", 0, L), -1.0, OP.mult, 1.0, OP.add)
-        act(b("DL"), ind(b("D"), b("LU2", 0, 8)))
-        ms(b("DF", 336, 464), 0.0)
-    step(2, "F3", lambda: scat("F3", WT, "V3D", 13, b("V3Z")), later2)
+    def update2():
+        scat("F3", WT, "V3D", 13, b("V3Z"))
+        wrap("F3")
+        act(b("DF", 0, F), b("D"))
+
+    def later2(yy):
+        decide(2, yy, b("W2"))
+        tt(b("OQ"), ind(b("OC", 0, S + 16), b("IX", 0, 13)), b("M16"), OP.mult)
+        scan(b("OX"), b("RKM"), b("OQ"), OP.mult, OP.add)
+        occ = b("OX", 15, L, 16)
+        ts(b("Q1", 0, 13), occ, 544.0, OP.is_ge, -float(F), OP.mult)
+        ts(b("Q2", 0, 13), occ, 0.0, OP.is_lt, BIG, OP.mult)
+        tt(b("Q1", 0, 13), b("Q1", 0, 13), occ, OP.add)
+        ts(b("QI", 0, 13), b("Q1", 0, 13), 80.0, OP.add)
+        tt(b("Q2", 0, 13), b("Q2", 0, 13), b("Q1", 0, 13), OP.add)
+        ts(b("Q3", 0, 13), b("Q2", 0, 13), float(OKB + S + 80), OP.add)
+        act(b("VB"), ind(b("D"), b("QI", 0, 13)), AF.Identity, 1.0, b("MB", 2, 3))
+        tt(b("ND"), b("DQ"), b("W2", 80, L), OP.add)
+        act(b("DF", 544, F), b("W2", 0, 80))
+        scat("DF", F, "LU2", 8, b("ND"))
+    step(2, "F3", update2, later2)
 
     scat("HT", WT, "DT2", 13, b("ZL2"))
     store("S", T.yt[:, :], b("HT", 0, S), "yt")
-    scat("OC", WT, "DT2", 13, b("LW2", 0, L))
+    tt(b("Q1", 0, 13), CS, b("Q3", 0, 13), OP.max)
+    tt(b("Q2", 0, 13), b("Q1", 0, 13), b("DUQ", 0, 13), OP.min)
+    ts(b("BL", 0, 13), b("Q2", 0, 13), float(OKB + S), OP.subtract)
+    scat("OC", WT, "DT2", 13, b("LF2"))
     store("A", T.yo[:, :], (T.OC[0:128:16, 0:S], "OC", (0, 1, 0, S), None, S), "yo")
-    tt(b("B3"), ind(b("OC"), b("DT0", 0, 13)), b("F2V", 80, 288), OP.not_equal)
-    tt(b("HK"), ind(b("OC"), b("DT1", 0, 13)), b("LW1", 0, L), OP.not_equal)
-    tt(b("BP", 0, L), b("B3"), b("NB1"), OP.mult)
-    cp(b("LVW", 0, 128), b("HK", 80, L))
-    cp(b("B2"), ind(b("LVW"), b("PL1", 0, 21)))
-    for i, x in enumerate(("D", "BP", "B2")):
-        mm(b("T4", 0, 336), b("ID"), b(x, 0, 336), i == 0, i == 2)
-    tt(b("ND"), b("DL"), b("PF", L + 80, 2 * L), OP.add)
-    cp(b("DF", 464, 544), b("PF", L, L + 80))
-    tt(b("DF", 544, F), b("D", 544, F), b("HK", 0, 80), OP.add)
-    cp(b("DF", 0, 336), b("T4", 0, 336))
-    scat("DF", F, "LU2", 8, b("ND"))
-    store("S", T.yd[:, :], (T.DF[0:128:16, 0:F], "DF", (0, 1, 0, F), None, F), "yd")
+    scat("DF", F + L, "BL", 13, b("VB"))
+    store("S", T.yd[:, 0:544], (T.DF[0:128:16, 80:F], "DF", (0, 1, 80, F), None, 544), "yd")
+    store("A", T.yd[:, 544:F], (T.DF[0:128:16, 0:80], "DF", (0, 1, 0, 80), None, 80), "ye")
     issue()
     for s in SEMAPHORES:
         if s in cnt and know["G"].get(s, 0) < cnt[s]:

@@ -9,15 +9,26 @@ PEN = 65536
 OKB = 8 * PEN
 NB = 128
 BIG = 1048576.0
-LAG, SLACK = 0.08, 0.05
-KA0, KR0, KAD_ = 6, 6, 4
+LAG = 0.09
+PASSES = 6
+SPAN = []
+HOP = 1.4
+GA = 1.56
+KA0 = 6
+KR0 = 6
+KDH = 4
+KDF = 2
+HFIRST = 0
+ECUT = [(0, 7), (7, 13)]
+TRIES = 150
+RQX = 2.0
 
 ENG = "VAPG"
 LOADS = ["ef0", "eh0", "zf0", "tab", "ef1", "eh1", "zf1", "ef2", "eh2", "zf2"]
-MSGS = ["RQZ", "RQL", "KFR", "F2", "F3", "U2Z", "U2D", "U3Z", "U3D", "V3Z", "V3D"]
-TO = {"RQZ": 1, "RQL": 1, "KFR": -1, "F2": -2, "U2Z": -2, "U2D": -2, "F3": -3, "U3Z": -3, "U3D": -3, "V3Z": -3, "V3D": -3}
-SMALL = [("RQZ", "RQZ"), ("RQL", "RQL"), ("RQZ", "U2Z"), ("RQZ", "U3Z"), ("KFR", "KFR"), ("U3D", "U3D"), ("V3Z", "V3Z"), ("V3D", "V3D")]
-TABLES = [("F2", "F2"), ("F2", "F3")]
+MSGS = ["RQZ", "RQL", "KFR", "F2", "F3", "U2Z", "U2D", "V3Z", "V3D"]
+TO = {"RQZ": 1, "RQL": 1, "KFR": -1, "F2": -2, "U2Z": -2, "U2D": -2, "F3": -3, "V3Z": -3, "V3D": -3}
+SMALL = [("RQZ", "RQZ"), ("RQL", "RQL"), ("RQZ", "U2Z"), ("KFR", "KFR"), ("V3Z", "V3Z"), ("V3D", "V3D")]
+TABLES = [("F2", "F2"), ("F3", "F3")]
 STORES = ["yt", "yo", "yd", "ye"]
 SEMAPHORES = (["q" + e for e in ENG] + ["d_" + n for n in LOADS] + ["o_" + n for n in STORES]
               + ["a_" + n for n in MSGS] + ["l_" + n for n in MSGS])
@@ -38,14 +49,14 @@ def _sb(name, shape, dtype):
 
 for _n, _s, _d in (
         ("HT", [WT], BF), ("F2", [WT], BF), ("F3", [WT], BF), ("OC", [WT], F32),
-        ("ZF", [F], BF), ("EHI", [F], I32), ("EFI", [F], I32), ("EH", [F + 32], F32), ("EF", [F + 32], F32),
+        ("ZF", [F], BF), ("EH", [F + 32], I32), ("EF", [F + 32], I32), ("YA", [448], I32), ("YB", [448], I32),
         ("D", [F], BF), ("DF", [F + L], F32), ("XH", [160], F32), ("XF", [160], F32), ("DQ", [128], F32),
-        ("YH", [448], F32), ("YF", [448], F32), ("YS", [192], F32), ("YT", [192], F32),
+        ("YH", [288], F32), ("YF", [288], F32), ("YS", [192], I32), ("YT", [192], I32), ("KAB", [128], BF), ("IDN", [128], BF),
         ("LH0", [224], U16), ("LF0", [224], U16), ("LDH", [128], U16), ("LDF", [128], U16),
         ("GA0", [512], BF), ("GA1", [512], BF), ("GA2", [512], BF), ("CMH", [L, 16], BF), ("CMF", [L, 16], BF),
         ("RQZ", [L], BF), ("RQL", [224], U16), ("KFR", [16], F32), ("KFO", [16], F32),
-        ("U2Z", [L], BF), ("U2D", [16], U16), ("U3Z", [L], BF), ("U3D", [16], U16), ("V3Z", [L], BF), ("V3D", [16], U16),
-        ("HS", [L], F32), ("FS", [221], F32), ("HKI", [16], I32), ("HSL", [16], I32), ("A1", [16], F32),
+        ("U2Z", [L], BF), ("U2D", [16], U16), ("V3Z", [L], BF), ("V3D", [16], U16),
+        ("HS", [L], F32), ("FS", [424], F32), ("HKI", [16], I32), ("HSL", [16], I32), ("A1", [16], F32),
         ("AP", [16], F32), ("YY", [16], F32), ("IX", [16], U16), ("WI", [16], I32), ("WU", [16], U16), ("UL", [16], U16),
         ("DS", [16], F32), ("B0", [L], BF), ("B1", [L], BF), ("E0", [13, 128], BF), ("E1", [5, 128], BF),
         ("NU", [32], F32), ("UU", [48], BF), ("UC", [32], BF), ("QQ", [32], F32), ("TB", [1], F32),
@@ -54,12 +65,13 @@ for _n, _s, _d in (
         ("VB", [L], F32), ("Q1", [16], F32), ("Q2", [16], F32), ("Q3", [16], F32), ("QI", [16], U16), ("BL", [16], U16),
         ("DUQ", [16], F32),
         ("PI", [1], I32), ("PJ", [1], I32), ("PK", [1], I32), ("PM", [1], F32), ("MH0", [1], F32), ("MH1", [1], F32),
-        ("PY", [1], F32), ("P2", [16], F32), ("P3", [16], F32), ("ML", [2], F32), ("MB", [4], F32), ("MC", [6], F32),
+        ("PY", [1], F32), ("P2", [16], F32), ("P3", [16], F32), ("ML", [2], F32), ("MB", [16], F32), ("MC", [6], F32),
         ("KIO", [L], F32), ("M16", [L], F32), ("RKM", [L], BF), ("RK8", [104], BF), ("KAD", [L], F32), ("C16", [32], F32),
         ("FW", [32], F32), ("DMF", [32], F32), ("ONB", [128], BF), ("BA", [128], BF), ("BO", [128], BF), ("NBO", [128], BF),
         ("NT", [128], BF), ("ID", [128], BF), ("IDF", [128], F32), ("WMU", [144], BF), ("BW", [1], BF),
         ("CL", [264], F32), ("CI", [264], I32), ("CJ", [264], I32), ("CB", [264], F32),
-        ("LB", [256], BF), ("HB", [8], F32), ("CT", [S + 64], BF), ("JA", [L], BF), ("JB", [416], BF), ("JC", [320], BF),
+        ("LB", [256], BF), ("HB", [8], F32), ("CT", [S + 64], BF), ("FJ", [L], BF), ("BR", [L], BF), ("TH", [2], F32), ("TN", [2], F32), ("FM", [L], F32),
+        ("BX", [336], F32), ("BU", [16], U16),
         ("QV", [416], F32), ("FQ", [F], F32), ("LM", [128], F32), ("ON32", [32], F32), ("TW", [32], F32), ("T01", [16], F32),
         ("RK", [16], I32), ("RC", [16], I32), ("RP", [16], I32), ("RX", [16], F32), ("RY", [16], F32), ("PC", [16], F32),
 ):
@@ -91,7 +103,7 @@ def bits(e):
 
 def near(topo, a, b, m):
     e = topo.engines(a, b)
-    return e[:len(e) // 2] if m == "F2" else e[len(e) // 2:]
+    return e[len(e) // 2:] if m != "F2" else e[:len(e) // 2]
 
 
 def land(T, m):
@@ -196,10 +208,10 @@ def rank_program(g, core, T, topo):
 
     nodes, seen, group = [], {}, []
 
-    def node(e, run, reads, writes, dur, lat=0.0, after=None):
+    def node(e, run, reads, writes, dur, lat=0.0, after=None, done=1):
         k, before = len(nodes), {}
         if after is not None:
-            before[after] = 1
+            before[after] = done
         for w, lst in ((False, reads), (True, writes)):
             for name, reg, psum in lst:
                 for (r2, w2, j) in seen.get(name, []):
@@ -220,9 +232,9 @@ def rank_program(g, core, T, topo):
         if e == "G":
             dur = 0.15 + 2 * c
         elif out[3]:
-            dur = 0.05 + 3.5 * c
+            dur = 0.05 + 3.8 * c
         elif win:
-            dur = 0.06 + 1.5 * 0.00087 * out[4]
+            dur = 0.06 + GA * 0.00085 * out[4]
         else:
             two = all(SCRATCH[x[1]][2] in (BF, U16) for x in ins + [out] if isinstance(x, tuple))
             both = len(ins) == 2 and all(isinstance(x, tuple) and x[4] == out[4] and SCRATCH[x[1]][0] == "sbuf" for x in ins)
@@ -230,30 +242,71 @@ def rank_program(g, core, T, topo):
         return node(e, lambda: emit(e, f, out, ins), regions(ins + offsets(ins + [out])), regions([out]), dur, 0.0, after)
 
     def issue():
-        tail, left, free, end, succ = [0.0] * len(nodes), [len(x[4]) for x in nodes], {}, {}, [[] for _ in nodes]
-        for k, x in enumerate(nodes):
-            for j, full in x[4]:
-                succ[j].append((k, full))
-        for k in reversed(range(len(nodes))):
-            tail[k] = nodes[k][2] + max([0.0] + [tail[s] + (nodes[k][3] + LAG) * full for s, full in succ[k]])
-        ready, order = [k for k in range(len(nodes)) if not left[k]], []
-        while ready:
-            start, first = {}, {}
-            for k in ready:
-                e, run, dur, lat, before = nodes[k]
-                start[k] = max([free.get(e, 0.0)] + [end[j] - (0 if full else nodes[j][3]) + LAG * full for j, full in before])
-                first[e] = min(first.get(e, 1e9), start[k])
-            e = min(first, key=lambda x: first[x])
-            k = max((k for k in ready if nodes[k][0] == e and start[k] <= first[e] + SLACK), key=lambda k: (tail[k], -k))
-            ready.remove(k)
-            order.append(k)
-            free[e] = start[k] + nodes[k][2]
-            end[k] = free[e] + nodes[k][3]
-            for s, full in succ[k]:
-                left[s] -= 1
-                if not left[s]:
-                    ready.append(s)
-        for k in order:
+        n = len(nodes)
+        pred = [[(j, (nodes[j][3] + LAG) * full) for j, full in x[4]] for x in nodes]
+        succ = [[] for _ in nodes]
+        for k in range(n):
+            for j, gap in pred[k]:
+                succ[j].append((k, gap))
+
+        def place(order, before, last):
+            end, taken = [0.0] * n, {}
+            for k in order:
+                e, dur = nodes[k][0], nodes[k][2]
+                t = max([last[k]] + [end[j] + gap for j, gap in before[k]])
+                row = taken.setdefault(e, [])
+                i = 0
+                while i < len(row) and row[i][0] < t + dur - 1e-9:
+                    t = max(t, row[i][1])
+                    i += 1
+                row.insert(i, (t, t + dur))
+                end[k] = t + dur
+            return end
+
+        tail = [0.0] * n
+        for k in reversed(range(n)):
+            tail[k] = nodes[k][2] + max([nodes[k][3]] + [tail[s] + gap for s, gap in succ[k]])
+        def passes(tail, count):
+            best = None
+            for _ in range(count):
+                end = place(sorted(range(n), key=lambda k: (-tail[k], k)), pred, [0.0] * n)
+                span = max(end[k] + nodes[k][3] for k in range(n))
+                if best is None or span < best[0]:
+                    best = (span, end, tail)
+                tail = place(sorted(range(n), key=lambda k: (-end[k], -k)), succ, [x[3] for x in nodes])
+            return best
+
+        if not SPAN:
+            best, seed = passes(tail, PASSES), 1
+            now = best
+            for _ in range(TRIES):
+                end, held = now[1], []
+                k = max(range(n), key=lambda k: end[k] + nodes[k][3])
+                by = {(nodes[j][0], round(end[j], 6)): j for j in range(n)}
+                while True:
+                    t = end[k] - nodes[k][2]
+                    ready = max([(0.0, -1)] + [(end[j] + gap, j) for j, gap in pred[k]])
+                    if ready[0] < t - 1e-6:
+                        held.append((k, t - ready[0]))
+                        k = by[nodes[k][0], round(t, 6)]
+                    elif ready[1] < 0:
+                        break
+                    else:
+                        k = ready[1]
+                tail = [-(end[k] - nodes[k][2]) for k in range(n)]
+                for _ in range(2):
+                    seed = (seed * 1103515245 + 12345) % 2147483648
+                    k, wait = held[(seed >> 8) % len(held)]
+                    tail[k] += wait * (1 + (seed >> 4) % 4) / 4 + 0.01
+                for k in reversed(range(n)):
+                    tail[k] = max([tail[k]] + [tail[s] + 1e-6 for s, gap in succ[k]])
+                other = passes(tail, 2)
+                if other[0] <= now[0] + 0.05:
+                    now = other
+                if now[0] < best[0]:
+                    best = now
+            SPAN.extend(best)
+        for k in sorted(range(n), key=lambda k: (SPAN[1][k] - nodes[k][2], SPAN[1][k], k)):
             nodes[k][1]()
 
     def A_(o):
@@ -295,6 +348,8 @@ def rank_program(g, core, T, topo):
 
     def mms(*m):
         m = [tuple(x) + (None,) * (6 - len(x)) for x in m]
+        if len(m) > 4:
+            return [mms(*m[i:i + 4]) for i in range(0, len(m), 4)]
         node("P", lambda: [mm_now(*x) for x in m], regions([x[1] for x in m] + [x[2] for x in m]), regions([x[0] for x in m]),
              sum(0.02 + 0.00045 * max(64, x[0][4]) * (4 if SCRATCH[x[1][1]][2] == F32 else 1) for x in m))
 
@@ -310,14 +365,14 @@ def rank_program(g, core, T, topo):
     def scat(win, width, off, n, val):
         cp(ind(b(win, 0, width), b(off, 0, n)), val)
 
-    def load(e, out, src, name):
+    def load(e, out, src, name, behind):
         w = regions([out])
 
         def run():
             sync(e, [], w)
             Q[e].dma_start(out[0], src).then_inc(T.sem["d_" + name], 16)
             note(e, [], w, "d_" + name, 16)
-        return node(e, run, [], w, 0.1, 3.6 if out[4] > 700 else 2.4)
+        return node(e, run, [], w, 0.1, HOP + (2.0 if out[4] > 700 else 0.5), behind, 0)
 
     def store(e, dst, a, name):
         r = regions([a])
@@ -326,12 +381,12 @@ def rank_program(g, core, T, topo):
             sync(e, r, [])
             Q[e].dma_start(dst, a[0]).then_inc(T.sem["o_" + name], 16)
             note(e, r, [], "o_" + name, 16)
-        node(e, run, r, [], 0.1, 3.8 if name == "yt" else 2.0)
+        node(e, run, r, [], 0.1, HOP + (2.0 if name == "yt" else 0.3))
 
     small, big = helpers(T, topo, core)
 
     def send(m, src, lats):
-        to = big if m == "F2" else T.cores[(rank + TO[m]) % len(T.cores)] if m == "U2D" else small
+        to = big if m in ("F2", "F3") else T.cores[(rank + TO[m]) % len(T.cores)] if m == "U2D" else small
         es = topo.engines(core, to) if m == "U2D" else near(topo, core, to, m)
         r = regions([src])
         rid, pid = topo.addr(to, core)
@@ -351,13 +406,16 @@ def rank_program(g, core, T, topo):
         w = regions([b(x, 0, S) if x in ("F2", "F3") else b(x)])
         node("n" + x, lambda: note("net", [], w, "a_" + x, n), [], w, 0.0, lat, k)
 
-    load("S", b("ZF", 80, 288), T.zf[:, 0:L], "zf0")
-    load("A", b("EFI", 80, 304), T.ef[:, 0:224], "ef0")
-    load("S", b("EHI", 80, 304), T.eh[:, 0:224], "eh0")
-    load("A", b("HT", 0, S), T.tab[:, :], "tab")
-    for x, src, lo in (("ef", "EFI", 304), ("eh", "EHI", 304), ("zf", "ZF", 288)):
-        load("S", b(src, 0, 80), T[x][:, 544:F], x + "1")
-        load("S", b(src, lo, F), T[x][:, lo - 80:544], x + "2")
+    k = load("S", b("ZF", 80, 288), T.zf[:, 0:L], "zf0", None)
+    j = load("A", b("EF", 96, 320), T.ef[:, 0:224], "ef0", None)
+    k = load("S", b("EF", 16, 96), T.ef[:, 544:F], "ef1", k)
+    j = load("A", b("EH", 96, 320), T.eh[:, 0:224], "eh0", j)
+    k = load("S", b("EH", 16, 96), T.eh[:, 544:F], "eh1", k)
+    j = load("A", b("HT", 0, S), T.tab[:, :], "tab", j)
+    k = load("S", b("ZF", 0, 80), T.zf[:, 544:F], "zf1", k)
+    k = load("S", b("ZF", 288, F), T.zf[:, L:544], "zf2", k)
+    k = load("S", b("EH", 320, F + 16), T.eh[:, 224:544], "eh2", k)
+    k = load("S", b("EF", 320, F + 16), T.ef[:, 224:544], "ef2", k)
 
     ms(b("ONB"), 1.0)
     iota(b("PI"), [[0, 1]], 0, 1)
@@ -371,20 +429,32 @@ def rank_program(g, core, T, topo):
     ts(b("PK"), b("PI"), 4, OP.arith_shift_right, 1, OP.bitwise_and)
     cp(b("PM"), b("PJ"))
     cp(b("MH1"), b("PK"))
-    ts(b("MH0"), b("MH1"), -1.0, OP.mult, 1.0, OP.add)
     ts(b("FW"), b("C16"), b("PM"), OP.add)
-    for i, v in enumerate((200.0, -11.0, 1.0, -200.0)):
-        ms(b("MB", i, i + 1), v)
-    for x in ("EH", "EF"):
-        ms(b(x, 0, 16), 0.0)
-        ms(b(x, 80, 96), 0.0)
-        ms(b(x, F + 16, F + 32), 0.0)
-    act(b("RKM"), b("KIO"), AF.Sigmoid, 400.0, b("MB", 3, 4))
+    column = {}
+
+    def aff(out, a, scale, bias):
+        if not isinstance(bias, tuple):
+            bias = const(bias)
+        act(out, a, AF.Identity, scale, bias)
+
+    def const(v, p=(0, 128)):
+        if v not in column:
+            column[v] = len(column)
+            ms(b("MB", column[v], column[v] + 1), float(v))
+        return b("MB", column[v], column[v] + 1, p=p)
+
+    def fill(out, v, after):
+        iota(out, [[0, out[4]]], v, 0, after)
+
+    act(b("RKM"), b("KIO"), AF.Sigmoid, 400.0, const(-200))
+    aff(b("MH0"), b("MH1"), -1.0, 1)
     ms(b("WMU"), 0.0)
-    ts(b("WMU", 15, 143, 16), b("BO", 0, 128, 16), float(PEN), OP.mult)
-    ts(b("NBO"), b("BO"), -1.0, OP.mult)
+    act(b("WMU", 15, 143, 16), b("BO", 0, 128, 16), scale=float(PEN))
+    act(b("NBO"), b("BO"), scale=-1.0)
     act(b("IDF"), b("ID"))
-    ts(b("KAD"), b("KIO"), -4096.0, OP.mult, 61440.0, OP.add)
+    act(b("IDN"), b("ID"), scale=-1024.0)
+    aff(b("KAD"), b("KIO"), -4096.0, 61440)
+    act(b("KAB"), b("KAD", 0, 128))
     ts(b("M16"), b("KIO"), b("PM"), OP.is_equal)
 
     def places(x):
@@ -409,14 +479,18 @@ def rank_program(g, core, T, topo):
         tr(b(y, 0, n1), b(src, lo, lo + n1))
         tr(b(y, n1, n1 + n2), b(src, lo - 16, lo - 16 + n2))
         cp(b(out, 0, 16 * s), ind(b(y, 0, n1 + n2), b("RO%d" % x, 0, s)))
-        if key:
+        if key and x == 2:
+            act(key, ind(b(y, 0, n1 + n2), b("RQ%d" % x, 0, nc)))
+        elif key:
             tt(key, ind(b(y, 0, n1 + n2), b("RQ%d" % x, 0, nc)), b("KAD", 0, 16 * nc), OP.add)
 
     bank = [0]
 
     def look(x, win, lst, z, cm, c0, chunks, k1):
         nc, s = KINDS[x]
-        k = 0
+        for j in range(k1):
+            lo, hi = 16 * c0, 16 * (c0 + nc)
+            tt((T[cm][:, lo:hi, j], cm, (lo, hi, j, j + 1), None, hi - lo), ind(win, b(lst, s * j, s * j + nc)), z, OP.is_le)
         for k0, k in chunks:
             n = k - k0
             ga, t = "GA%d" % (bank[0] % 3), "T%d" % (bank[0] % 6)
@@ -427,70 +501,70 @@ def rank_program(g, core, T, topo):
                 o = b3(t, 0, nc * n, j, 16, step=n)
                 m += [(o, b("ID"), z, True, False), (o, b("ID"), b(ga, 16 * s * j, 16 * (s * j + nc)), False, True)]
             mms(*m)
-            act(b3(cm, 16 * c0, 16 * (c0 + nc), k0, k), b3(t, 0, nc * n), AF.Sigmoid, 400.0, b("MB", 0, 1))
-        for j in range(k, k1):
-            lo, hi = 16 * c0, 16 * (c0 + nc)
-            tt((T[cm][:, lo:hi, j], cm, (lo, hi, j, j + 1), None, hi - lo), ind(win, b(lst, s * j, s * j + nc)), z, OP.is_le)
+            act(b3(cm, 16 * c0, 16 * (c0 + nc), k0, k), b3(t, 0, nc * n), AF.Sigmoid, 400.0, const(200))
 
     def pairs(n, w):
-        return [(k, min(n, k + w)) for k in range(0, n, w)]
+        return [(k, min(16, k + w)) for k in range(16 - n, 16, w)], 16 - n
 
     def sums(cm, c0, c1, key):
         out = b("PH", 16 * c0, 16 * c1)
         mms((out, b("IDF"), key, True, False))
+        if c0:
+            mms((out, b("ID"), b("KAB"), False, False))
         mms(*[(out, b("WMU", 15 - m, 143 - m), b3(cm, 16 * c0 + m, 16 * c1, cs=16), False, m == 15) for m in range(16)])
 
-    def far_max(c0, c1, k0, k1, lo, out, other):
+    def far_max(c0, c1, k0, k1, bank, lo, out, other):
         n = k1 - k0
         hi = lo + n * (c1 - c0)
-        mms(*[(b("PF", lo, hi), b("WMU", 15 - m, 143 - m), b3("CMF", 16 * c0 + m, 16 * c1, k0, k1, cs=16), m == 0, m == 15)
+        mms(*[(b(bank, lo, hi), b("WMU", 15 - m, 143 - m), b3("CMF", 16 * c0 + m, 16 * c1, k0, k1, cs=16), m == 0, m == 15)
               for m in range(16)])
-        scan(b("FS", lo, hi), b("RKM" if n == 16 else "RK8", 0, hi - lo), b("PF", lo, hi), OP.mult, OP.max)
+        scan(b("FS", lo, hi), b("RKM" if n == 16 else "RK8", 0, hi - lo), b(bank, lo, hi), OP.mult, OP.max)
         tt(out, b("FS", lo + n - 1, hi, n), other, OP.max)
 
     def home_max():
         top = b("HS", 15, L, 16)
         scan(b("HS"), b("RKM"), b("PH", 0, L), OP.mult, OP.max)
         cp(b("HKI", 0, 13), top)
-        ts(b("A1", 0, 13), top, 0.5 - 9 * PEN, OP.add, 4.0 * BIG, OP.mult)
         ts(b("HSL", 0, 13), b("HKI", 0, 13), S - 1, OP.bitwise_and)
-        tt(b("A1", 0, 13), b("A1", 0, 13), top, OP.min)
+        ts(b("WI", 0, 13), b("HKI", 0, 13), 31 * PEN, OP.bitwise_and)
         ts(b("AP", 0, 13), b("HSL", 0, 13), float(OKB), OP.add)
-        tt(b("AP", 0, 13), b("AP", 0, 13), b("A1", 0, 13), OP.max)
+        tt(b("AP", 0, 13), b("AP", 0, 13), b("WI", 0, 13), OP.max)
 
     CS = b("PF", 224, 237)
 
-    def orders():
-        for a in range(4):
-            pp = (32 * a, 32 * a + 32)
-            mms((b3("T%d" % a, 0, 26), b("JA", 0, NB, p=pp), b("JB", p=pp), True, False, a))
-        for h in range(2):
-            pp = (64 * h, 64 * h + 32)
-            mms((b3("T%d" % (4 + h), 0, 20, p=(0, 80)), b("JA", NB, L, p=pp), b("JC", p=pp), True, False, 2 * h))
-
     def decide(t, yy, grown):
         ts(b("IX", 0, 13), yy, float(OKB + S), OP.min, float(OKB), OP.subtract)
-        act(b("B1"), ind(b("CT", 0, S + 16), b("IX", 0, 13)), scale=b("MH1"))
-        ts(b("B0"), ind(b("CT", 0, S + 16), b("IX", 0, 13)), b("MH0"), OP.mult)
+        tt(b("BR"), ind(b("CT", 0, S + 16), b("IX", 0, 13)), b("FJ"), OP.add)
+        ts(b("B0"), b("BR"), b("MH0"), OP.mult)
+        act(b("B1"), b("BR"), scale=b("MH1"))
         for a in (0, 2, 1, 3):
             pp = (32 * a, 32 * a + 32)
-            mms(*[(b3("T%d" % a, x, 26, cs=2), b("B%d" % x, 0, NB, p=pp), b("B%d" % x, p=pp), False, x == 1, a) for x in (0, 1)])
+            for x in (0, 1):
+                mms((b3("T%d" % a, x, 26, cs=2), b("B%d" % x, 0, NB, p=pp), b("BR", p=pp), True, True, a))
+        for a in (0, 2, 1, 3):
+            pp = (32 * a, 32 * a + 32)
             mms(*[(b3("T%d" % (4 + a // 2), 2 * (a % 2) + x, 20, cs=4, p=(0, 80)), b("B%d" % x, NB, L, p=pp),
-                   b("B%d" % x, NB, L, p=pp), False, x == 1 and a % 2 == 1, a) for x in (0, 1)])
-        for a in range(6):
+                   b("BR", NB, L, p=pp), True, True, a) for x in (0, 1)])
+
+        def over(a, c0, c1):
             if a < 4:
-                out, src = b3("E0", 0, 13, 32 * a, 32 * a + 32), b3("T%d" % a, 0, 26)
+                out, src, x, pp = b3("E0", c0, c1, 32 * a, 32 * a + 32), b3("T%d" % a, 2 * c0, 2 * c1), 0, (0, NB)
             else:
-                out, src = b3("E1", 0, 5, 64 * a - 256, 64 * a - 192, p=(0, 80)), b3("T%d" % a, 0, 20, p=(0, 80))
+                pp = (0, L - NB)
+                out, src, x = b3("E1", 0, 5, 64 * a - 256, 64 * a - 192, p=pp), b3("T%d" % a, 0, 20, p=pp), 1
             if a in (2, 3, 5):
-                act(out, src, AF.Relu, 1.0, b("MB", 1, 2, p=(0, 80 if a == 5 else 128)))
+                act(out, src, AF.Relu, 1024.0, b("TN", x, x + 1, p=pp))
             else:
-                ts(out, src, 11.0 + 1.0 / 256, OP.is_gt)
+                ts(out, src, b("TH", x, x + 1, p=pp), OP.is_gt)
         mms((CS, b("IDF"), yy, True, False))
-        mms(*[(b("PF", 224 + c, 225 + c), b2("E0", c, 0, 128), b("BW"), False, False) for c in range(13)])
+        for c0, c1 in ECUT:
+            for a in range(4):
+                over(a, c0, c1)
+            mms(*[(b("PF", 224 + c, 225 + c), b2("E0", c, 0, 128), b("BW"), False, False) for c in range(c0, c1)])
+        over(4, 0, 5)
+        over(5, 0, 5)
         mms(*[(b("PF", 224 + c, 225 + c), b2("E1", c - 8, 0, 128, p=(0, 80)), b("BW", p=(0, 80)), False, c == 12) for c in range(8, 13)])
-        ts(b("WI", 0, 13), yy, 1.0 / PEN, OP.mult, -0.49999, OP.add)
-        cp(b("WU", 0, 13), b("WI", 0, 13))
+        ts(b("WU", 0, 13), yy, float(OKB + S), OP.max, 1.0 / PEN, OP.mult)
         act(grown, ind(b("TW"), b("WU", 0, 13)))
         tt(b("DS", 0, 13), CS, b("DU%d" % t, 0, 13), OP.min)
         ts(b("DT%d" % t, 0, 13), b("DS", 0, 13), float(OKB), OP.subtract)
@@ -498,13 +572,12 @@ def rank_program(g, core, T, topo):
     def lanes(t, n, fill, val):
         pls, lw, lu = "PL%d" % t, "LW%d" % t, "LU%d" % t
         scan(b("UC", 0, n), b("ON32", 0, n), b("UU", 0, n), OP.mult, OP.add)
-        mms((b("PH", 224, 224 + n), b("BO"), b("UC", 0, n), True, False), (b("PH", 224, 224 + n), b("NT"), b("UU", 0, n), False, True),
-            (b("PH", 256, 257), b("BO"), b("UC", n - 1, n), True, True))
-        ts(b("NU", 0, n), b("UU", 0, n), 0.5, OP.is_lt)
-        tt(b("NU", 0, n), b("NU", 0, n), b("DMF", 0, n), OP.mult)
-        tt(b("QQ", 0, n), b("PH", 224, 224 + n), b("NU", 0, n), OP.max)
-        cp(b(pls, 0, n), b("QQ", 0, n))
-        ts(b("TB"), b("PH", 256, 257), -1.0, OP.mult, float(fill), OP.add)
+        out = b("PH", 224, 224 + n)
+        mms((out, b("NT"), b("UU", 0, n), True, False), (out, b("IDN"), b("UU", 0, n), False, False))
+        mms((out, b("BO"), b("UC", 0, n), False, True), (b("PH", 256, 257), b("BO"), b("UC", n - 1, n), True, True))
+        tt(b("QQ", 0, n), out, b("DMF", 0, n), OP.min)
+        ts(b(pls, 0, n), b("QQ", 0, n), 1023.0, OP.add)
+        ts(b("TB"), b("PH", 256, 257), -1.0, OP.mult, fill - BIG, OP.add)
         scat(lw, 1024, pls, n, val)
         act(b("LD"), b("LM"), AF.Relu, 1.0, b("TB"))
         scan(b("XS"), b("LD"), b(lw, 0, 128), OP.max, OP.min)
@@ -516,7 +589,7 @@ def rank_program(g, core, T, topo):
     def step(t, ftab, update, later):
         lu, zl = b("LU%d" % t, 0, 8), "ZL%d" % t
         home, far = b("HT", 0, S + PAD), b(ftab, 0, S + PAD)
-        look(1, home, "LSH%d" % t, b(zl, 0, 80), "CMH", 0, pairs(16, 4), 16)
+        look(1, home, "LSH%d" % t, b(zl, 0, 80), "CMH", 0, *pairs(16, 4))
         act(b("DQ"), ind(b("D"), lu))
         act(b(zl, 80, L), ind(b("ZF"), lu))
         tt(b("XH", 16, 144), ind(b("EH", 16, 16 + F), lu), b("DQ"), OP.add)
@@ -526,44 +599,43 @@ def rank_program(g, core, T, topo):
         act(b("LF%d" % t, 80, L), ind(b("FQ"), lu))
         update()
         sums("CMH", 0, 5, b("KA%d" % t, 0, 80))
-        look(1, far, "LSF%d" % t, b(zl, 0, 80), "CMF", 0, pairs(16, 4), 16)
-        look(2, home, "LDH", b(zl, 80, L), "CMH", 5, pairs(KAD_, 4), 16)
+        look(1, far, "LSF%d" % t, b(zl, 0, 80), "CMF", 0, *pairs(16, 4))
+        look(2, home, "LDH", b(zl, 80, L), "CMH", 5, *pairs(KDH, 4))
         sums("CMH", 5, 13, b("KA%d" % t, 80, L))
-        look(2, far, "LDF", b(zl, 80, L), "CMF", 5, pairs(KAD_, 4), 16)
+        look(2, far, "LDF", b(zl, 80, L), "CMF", 5, *pairs(KDF, 4))
         home_max()
-        far_max(0, 5, 0, 16, 0, b("YY", 0, 5), b("AP", 0, 5))
-        far_max(5, 13, 0, 8, 80, b("AP", 5, 13), b("AP", 5, 13))
-        far_max(5, 13, 8, 16, 144, b("YY", 5, 13), b("AP", 5, 13))
-        orders()
+        far_max(0, 5, 0, 16, "PF", 0, b("YY", 0, 5), b("AP", 0, 5))
+        far_max(5, 13, 0, 8, "PF", 80, b("AP", 5, 13), b("AP", 5, 13))
+        far_max(5, 13, 8, 16, "PH", 320, b("YY", 5, 13), b("AP", 5, 13))
         later(b("YY", 0, 13))
 
     z0 = b("ZF", 80, 288)
-    send("RQZ", z0, {"RQZ": 4.5, "U2Z": 7.0, "U3Z": 7.0})
+    send("RQZ", z0, {"RQZ": 2 * HOP + 2.0, "U2Z": 2 * HOP + 4.0})
     places(0)
-    cp(b("EF", 96, 320), b("EFI", 80, 304))
-    lists(0, "EF", 96, "YF", "LF0")
-    asked = send("RQL", b("LF0"), {"RQL": 3.6})
-    cp(b("EH", 96, 320), b("EHI", 80, 304))
-    lists(0, "EH", 96, "YH", "LH0", b("KA0"))
-    send("F2", b("HT", 0, S), {"F2": 12.0, "F3": 20.0})
-    asel(b("NT"), b("NBO"), [[-1, 128]], OP.is_ge, 0, 1)
+    lists(0, "EF", 96, "YA", "LF0")
+    asked = send("RQL", b("LF0"), {"RQL": 2 * HOP + RQX})
+    lists(0, "EH", 96, "YB", "LH0", b("KA0"))
+    send("F2", b("HT", 0, S), {"F2": 11.0})
+    asel(b("NT"), b("NBO"), [[-1, 128]], OP.is_gt, 0, 1)
     iota(b("CL", 0, 256), [[1, 256]], 0, 0)
     iota(b("CL", 256, 264), [[256, 8]], 0, 0)
-    iota(b("JA"), [[1, L]], 0, 0, asked)
-    iota(b("JB"), [[16, 13], [0, 2], [1, 16]], 0, 0, asked)
-    iota(b("JC"), [[16, 5], [0, 4], [1, 16]], NB, 0, asked)
+    iota(b("FJ"), [[1, L]], 48, 0, asked)
+    iota(b("TH"), [[NB, 2]], 48, 1, asked)
     iota(b("TW"), [[1, 32]], 0, 0)
     for x in range(0, WT, 676):
         iota(b("OC", x, x + 676), [[0, 676]], -1, 0, asked)
     tab = b("HT", 0, S)
-    look(0, tab, "LH0", z0, "CMH", 0, pairs(KA0, 2), 16)
-    look(0, tab, "RQL", b("RQZ"), "CMF", 0, pairs(KR0, 2), 16)
-    sums("CMH", 0, 13, b("KA0"))
+    look(0, tab, "LH0", z0, "CMH", 0, *pairs(KA0, 2))
+    look(0, tab, "RQL", b("RQZ"), "CMF", 0, *pairs(KR0, 2))
     ms(b("KFO"), 0.0)
-    cp(b("RK8"), b("RKM", 0, L, 2))
-    far_max(0, 13, 0, 8, 0, b("KFO", 0, 13), b("KFO", 0, 13))
-    far_max(0, 13, 8, 16, 104, b("KFO", 0, 13), b("KFO", 0, 13))
-    told = send("KFR", b("KFO"), {"KFR": 3.2})
+    act(b("RK8"), b("RKM", 0, L, 2))
+    if HFIRST:
+        sums("CMH", 0, 13, b("KA0"))
+    far_max(0, 13, 0, 8, "PF", 0, b("KFO", 0, 13), b("KFO", 0, 13))
+    far_max(0, 13, 8, 16, "PH", 320, b("KFO", 0, 13), b("KFO", 0, 13))
+    if not HFIRST:
+        sums("CMH", 0, 13, b("KA0"))
+    told = send("KFR", b("KFO"), {"KFR": 2 * HOP + 0.4})
     home_max()
     ms(b("P2"), 0.5)
     ms(b("ON32"), 1.0)
@@ -577,21 +649,18 @@ def rank_program(g, core, T, topo):
     ts(b("ML", 0, 1), b("PM"), 8.0, OP.is_lt)
     ts(b("ML", 1, 2), b("PM"), 11.0, OP.is_lt)
     tt(b("ML", 1, 2), b("ML", 1, 2), b("ML", 0, 1), OP.subtract)
-    ts(b("LB"), b("CB", 0, 256), b("ML", 0, 1), OP.mult)
-    ts(b("HB"), b("CB", 256, 264), b("ML", 1, 2), OP.mult)
-    ms(b("CT", S, S + 16), 0.0)
+    act(b("HB"), b("CB", 256, 264), scale=b("ML", 1, 2))
+    fill(b("CT", S, S + 16), 0, asked)
     for h in range(8):
-        ts(b("CT", 256 * h, 256 * h + 256), b("LB"), b("HB", h, h + 1), OP.add)
-    ts(b("PJ"), b("PI"), 31, OP.bitwise_and)
-    ts(b("MC", 0, 1), b("PJ"), 0.0, OP.is_equal)
-    ts(b("MC", 1, 2), b("PJ"), 1.0, OP.is_equal, -1.0, OP.mult)
-    ts(b("MC", 2, 3), b("PJ"), 0.0, OP.is_equal, 1.0 / 128, OP.mult)
-    ts(b("MC", 3, 4), b("PJ"), 1.0, OP.is_equal, 1.0 / 128, OP.mult)
-    act(b("JA"), b("JA"), AF.Identity, b("MC", 1, 2), b("MC", 0, 1))
-    act(b("JB"), b("JB"), AF.Identity, b("MC", 2, 3), b("MC", 3, 4))
-    act(b("JC"), b("JC"), AF.Identity, b("MC", 2, 3), b("MC", 3, 4))
+        aff(b("CT", 256 * h, 256 * h + 256), b("CB", 0, 256), b("ML", 0, 1), b("HB", h, h + 1))
+    ts(b("MC", 0, 1), b("PM"), 11.0, OP.is_equal, 1.0 / 256, OP.mult)
+    act(b("FJ"), b("FJ"), scale=b("MC", 0, 1))
+    ts(b("TN"), b("TH"), 0.5, OP.add, 1.0 / 65536, OP.mult)
+    tt(b("TN"), b("TN"), b("TH"), OP.mult)
+    ts(b("TH"), b("TN"), 11.0, OP.add)
+    ts(b("TN"), b("TH"), -1024.0, OP.mult)
     ms(b("BW"), BIG)
-    cp(b("T01"), b("TW", 0, 16))
+    act(b("T01"), b("TW", 0, 16))
     ts(b("NU"), b("TW"), 9.0, OP.is_ge)
     tt(b("TW"), b("TW"), b("NU"), OP.mult)
     iota(b("FQ", 80, F), [[1, F - 80]], 0, 0, told)
@@ -599,66 +668,63 @@ def rank_program(g, core, T, topo):
     iota(b("FQ", 0, 80), [[1, 80]], 544, 0, told)
     iota(b("LF1", 0, 80), [[1, 80]], 544, 0, told)
     iota(b("LF2", 0, 80), [[1, 80]], 464, 0, told)
-    iota(b("LM"), [[1, 128]], 0, 0, told)
-    ts(b("LM"), b("LM"), BIG, OP.add)
+    iota(b("LM"), [[1, 128]], int(BIG), 0, asked)
     tt(b("LM"), b("LM"), b("M16", 0, 128), OP.mult)
-    ts(b("LM"), b("LM"), -BIG, OP.add)
     for t in range(3):
-        ts(b("DU%d" % t, 0, 13), b("FW", 0, 13), float(OKB + S + PAD + L * t), OP.add)
-    ts(b("DUQ", 0, 13), b("FW", 0, 13), float(OKB + S + F), OP.add)
-    ts(b("DMF"), b("FW"), 512.0, OP.add)
-    for n_, v_ in (("DT0", 0), ("DT1", 0), ("D", 0.0)):
-        ms(b(n_), v_)
-    for n_, lo, hi, v_ in (("XH", 0, 16, 0.0), ("XH", 144, 160, 0.0), ("XF", 0, 16, 0.0), ("XF", 144, 160, 0.0),
-                           ("BP", L, 336, 0.0), ("LVF", L, 592, 1.0), ("LVF", 592, 1104, 0.0),
-                           ("LVW", L, 1104, 0.0), ("LW1", 0, 128, BIG), ("LW2", 0, 128, BIG)):
-        ms(b(n_, lo, hi), v_)
+        aff(b("DU%d" % t, 0, 13), b("FW", 0, 13), 1.0, OKB + S + PAD + L * t)
+    aff(b("DUQ", 0, 13), b("FW", 0, 13), 1.0, OKB + S + F)
+    aff(b("DMF"), b("FW"), 1.0, 512 - 1023)
+    for n_ in ("DT0", "DT1"):
+        ms(b(n_), 0)
+    for n_, lo, hi, v_ in (("EH", 0, 16, 0), ("EF", 0, 16, 0), ("EH", F + 16, F + 32, 0), ("EF", F + 16, F + 32, 0), ("LW1", 0, 128, int(BIG))):
+        fill(b(n_, lo, hi), v_, asked)
+    for n_, lo, hi, v_ in (("D", 288, F, 0), ("XH", 0, 160, 0), ("XF", 0, 160, 0), ("BP", L, 336, 0), ("BX", L, 336, 1), ("LVF", L, 592, 1),
+                           ("LVF", 592, 1104, 0), ("LVW", L, 656, 0), ("LVW", 656, 1104, 0), ("LW2", 0, 128, int(BIG)), ("D", 0, 80, 0)):
+        fill(b(n_, lo, hi), v_, told)
     places(1)
     places(2)
-    for x in ("EH", "EF"):
-        cp(b(x, 16, 96), b(x + "I", 0, 80))
-        cp(b(x, 320, F + 16), b(x + "I", 304, F))
     for t, q0 in ((1, 0), (2, 544)):
         lists(1, "EH", 16 + q0, "YS", "LSH%d" % t, b("KA%d" % t, 0, 80))
         lists(1, "EF", 16 + q0, "YT", "LSF%d" % t)
         act(b("ZL%d" % t, 0, 80), b("ZF", q0, q0 + 80))
-    orders()
     tt(b("YY", 0, 13), b("AP", 0, 13), b("KFR", 0, 13), OP.max)
     decide(0, b("YY", 0, 13), b("D", 80, 288))
-    send("U2D", b("DT0"), {"U2D": 1.8})
-    send("U3D", b("DT0"), {"U3D": 3.2})
+    send("U2D", b("DT0"), {"U2D": HOP + 0.3})
 
     ts(b("UU", 0, 13), CS, float(OKB + S), OP.is_ge)
     scat("HT", WT, "DT0", 13, z0)
     wrap("HT")
+    send("F3", b("HT", 0, S), {"F3": 11.0})
     lanes(1, 13, 288, b("QV", 80, 288))
 
     def update1():
-        send("V3Z", b("ZL1"), {"V3Z": 3.6})
+        send("V3Z", b("ZL1"), {"V3Z": 2 * HOP + 1.0})
         scat("F2", WT, "U2D", 13, b("U2Z"))
         wrap("F2")
 
     def later1(yy):
+        aff(b("FM"), b("FQ", 80, 288), 1.0, 2)
+        tt(b("FM"), b("FM"), b("M16"), OP.mult)
+        aff(b("FM"), b("FM"), 1.0, -2)
         scat("OC", WT, "DT0", 13, b("FQ", 80, 288))
-        scat("F3", WT, "U3D", 13, b("U3Z"))
-        ts(b("A1", 0, 8), b("FW", 13, 21), b("TB"), OP.subtract, 80.0, OP.add)
-        cp(b("PL1", 13, 21), b("A1", 0, 8))
+        ts(b("PL1", 13, 21), b("FW", 13, 21), b("TB"), OP.subtract, 80.0 - BIG, OP.add)
         decide(1, yy, b("LVW", 0, L))
     step(1, "F2", update1, later1)
-    send("V3D", b("DT1"), {"V3D": 3.2})
+    send("V3D", b("DT1"), {"V3D": 2 * HOP + 0.4})
 
     ts(b("UL", 0, 13), CS, float(OKB + S), OP.is_ge)
     ts(b("UU", 0, 5), b("PF", 224, 229), float(OKB + S), OP.is_ge)
     act(b("LVF", 0, L), ind(b("T01"), b("UL", 0, 13)))
     act(b("UF", 0, 336), ind(b("LVF", 80, 1104), b("PL1", 0, 21)))
     scat("OC", WT, "DT1", 13, b("LF1"))
-    tt(b("BP", 0, L), ind(b("OC"), b("DT0", 0, 13)), b("FQ", 80, 288), OP.not_equal)
+    tt(b("OQ"), ind(b("OC"), b("DT0", 0, 13)), b("FM"), OP.is_equal)
+    scan(b("BX", 0, L), b("RKM"), b("OQ"), OP.mult, OP.add)
     scat("HT", WT, "DT1", 13, b("ZL1"))
     wrap("HT")
-    for x in ("UF", "BP"):
-        mms(*[(b("PH", 288, 309), b("WMU", 15 - m, 143 - m), b(x, m, 336, 16), x == "UF" and m == 0, x == "BP" and m == 15)
-              for m in range(16)])
-    ts(b("UU", 5, 26), b("PH", 288, 309), 1.0, OP.is_ge)
+    mms(*[(b("PH", 288, 309), b("WMU", 15 - m, 143 - m), b("UF", m, 336, 16), m == 0, m == 15) for m in range(16)])
+    tt(b("UU", 5, 26), b("PH", 288, 309), b("BX", 15, 336, 16), OP.is_ge)
+    ts(b("BU", 0, 13), b("BX", 15, L, 16), 0.5, OP.is_lt)
+    act(b("BP", 0, L), ind(b("T01"), b("BU", 0, 13)))
     lanes(2, 26, 416, b("QV"))
     act(b("GW"), ind(b("LVW", 80, 1104), b("PL1", 0, 21)))
     act(b("D", 0, 80), b("LVW", 0, 80))
@@ -682,7 +748,7 @@ def rank_program(g, core, T, topo):
         ts(b("QI", 0, 13), b("Q1", 0, 13), 80.0, OP.add)
         tt(b("Q2", 0, 13), b("Q2", 0, 13), b("Q1", 0, 13), OP.add)
         ts(b("Q3", 0, 13), b("Q2", 0, 13), float(OKB + S + 80), OP.add)
-        act(b("VB"), ind(b("D"), b("QI", 0, 13)), AF.Identity, 1.0, b("MB", 2, 3))
+        act(b("VB"), ind(b("D"), b("QI", 0, 13)), AF.Identity, 1.0, const(1))
         tt(b("ND"), b("DQ"), b("W2", 80, L), OP.add)
         act(b("DF", 544, F), b("W2", 0, 80))
         scat("DF", F, "LU2", 8, b("ND"))

@@ -1,3 +1,4 @@
+import math
 from concourse.mybir import AluOpType, ActivationFunctionType
 OP = AluOpType
 AF = ActivationFunctionType
@@ -9,29 +10,45 @@ PEN = 65536
 OKB = 8 * PEN
 NB = 128
 BIG = 1048576.0
-LAG = 0.09
+KQ = 1.0 / 65536
+LAG = 0.14
 PASSES = 6
 SPAN = []
+NODES = []
 HOP = 1.4
 GA = 1.56
 KA0 = 6
-KR0 = 6
-KDH = 4
-KDF = 2
+KR0 = [(4, 6), (14, 16)]
+KD = (0, 0, 1, 1)
 HFIRST = 0
 ECUT = [(0, 7), (7, 13)]
-TRIES = 150
-RQX = 2.0
+TRIES = 6000
+RQX = 1.5
+LWA = ()
+PFX = 0.02
+SEED = 1
+SFIRST = 0
+UX = 0.3
+VX = 0.4
+KX = 0.4
+AFX = 0.11
+ONV = ("TS", "LD", "HT", "F2", "F3", "TB")
+EA = (2, 3, 5)
+ECA = [(0, 13)]
+CUT0 = 10
+PEC = 0.00045
+ORD = 2
 
 ENG = "VAPG"
 LOADS = ["ef0", "eh0", "zf0", "tab", "ef1", "eh1", "zf1", "ef2", "eh2", "zf2"]
 MSGS = ["RQZ", "RQL", "KFR", "F2", "F3", "U2Z", "U2D", "V3Z", "V3D"]
 TO = {"RQZ": 1, "RQL": 1, "KFR": -1, "F2": -2, "U2Z": -2, "U2D": -2, "F3": -3, "V3Z": -3, "V3D": -3}
 SMALL = [("RQZ", "RQZ"), ("RQL", "RQL"), ("RQZ", "U2Z"), ("KFR", "KFR"), ("V3Z", "V3Z"), ("V3D", "V3D")]
-TABLES = [("F2", "F2"), ("F3", "F3")]
+TABLES = ("F2", "F3")
+PARTS = 4
 STORES = ["yt", "yo", "yd", "ye"]
 SEMAPHORES = (["q" + e for e in ENG] + ["d_" + n for n in LOADS] + ["o_" + n for n in STORES]
-              + ["a_" + n for n in MSGS] + ["l_" + n for n in MSGS])
+              + ["a_" + n for n in MSGS] + ["l_" + n for n in MSGS] + ["p_%s%d" % (n, i) for n in TABLES for i in range(PARTS)])
 
 SCRATCH = {}
 PLACE = {}
@@ -52,33 +69,35 @@ for _n, _s, _d in (
         ("ZF", [F], BF), ("EH", [F + 32], I32), ("EF", [F + 32], I32), ("YA", [448], I32), ("YB", [448], I32),
         ("D", [F], BF), ("DF", [F + L], F32), ("XH", [160], F32), ("XF", [160], F32), ("DQ", [128], F32),
         ("YH", [288], F32), ("YF", [288], F32), ("YS", [192], I32), ("YT", [192], I32), ("KAB", [128], BF), ("IDN", [128], BF),
-        ("LH0", [224], U16), ("LF0", [224], U16), ("LDH", [128], U16), ("LDF", [128], U16),
-        ("GA0", [512], BF), ("GA1", [512], BF), ("GA2", [512], BF), ("CMH", [L, 16], BF), ("CMF", [L, 16], BF),
-        ("RQZ", [L], BF), ("RQL", [224], U16), ("KFR", [16], F32), ("KFO", [16], F32),
+        ("LH0", [256], U16), ("LF0", [256], U16), ("LDH", [128], U16), ("LDF", [128], U16),
+        ("GA0", [512], BF), ("GA1", [512], BF), ("GA2", [512], BF), ("GA3", [512], BF), ("GA4", [512], BF), ("GA5", [512], BF), ("CMH", [L, 16], BF), ("CMF", [L, 16], BF),
+        ("CDH", [256, 8], BF), ("CDF", [256, 8], BF), ("RK4", [184], BF), ("RKA", [160], BF), ("RKB", [112], BF), ("ZX1", [20, 16], BF), ("ZX2", [20, 16], BF),
+        ("RQZ", [L], BF), ("RQL", [256], U16), ("KFR", [16], F32), ("KFO", [16], F32),
         ("U2Z", [L], BF), ("U2D", [16], U16), ("V3Z", [L], BF), ("V3D", [16], U16),
         ("HS", [L], F32), ("FS", [424], F32), ("HKI", [16], I32), ("HSL", [16], I32), ("A1", [16], F32),
         ("AP", [16], F32), ("YY", [16], F32), ("IX", [16], U16), ("WI", [16], I32), ("WU", [16], U16), ("UL", [16], U16),
         ("DS", [16], F32), ("B0", [L], BF), ("B1", [L], BF), ("E0", [13, 128], BF), ("E1", [5, 128], BF),
-        ("NU", [32], F32), ("UU", [48], BF), ("UC", [32], BF), ("QQ", [32], F32), ("TB", [1], F32),
+        ("NU", [32], BF), ("UU", [48], BF), ("UC", [32], BF), ("QQ", [32], F32), ("TB", [1], F32),
         ("LD", [128], F32), ("XS", [128], F32), ("LVF", [1104], BF), ("LVW", [1104], BF), ("UF", [512], BF),
-        ("GW", [336], BF), ("BP", [512], BF), ("W2", [L], F32), ("ND", [128], F32), ("OQ", [L], F32), ("OX", [L], F32),
+        ("GW", [544], BF), ("BP", [336], BF), ("OQ", [L], F32), ("OX", [L], F32),
         ("VB", [L], F32), ("Q1", [16], F32), ("Q2", [16], F32), ("Q3", [16], F32), ("QI", [16], U16), ("BL", [16], U16),
         ("DUQ", [16], F32),
         ("PI", [1], I32), ("PJ", [1], I32), ("PK", [1], I32), ("PM", [1], F32), ("MH0", [1], F32), ("MH1", [1], F32),
         ("PY", [1], F32), ("P2", [16], F32), ("P3", [16], F32), ("ML", [2], F32), ("MB", [16], F32), ("MC", [6], F32),
-        ("KIO", [L], F32), ("M16", [L], F32), ("RKM", [L], BF), ("RK8", [104], BF), ("KAD", [L], F32), ("C16", [32], F32),
-        ("FW", [32], F32), ("DMF", [32], F32), ("ONB", [128], BF), ("BA", [128], BF), ("BO", [128], BF), ("NBO", [128], BF),
+        ("KIO", [L], F32), ("M16", [L], F32), ("RKM", [L], BF), ("KAD", [L], F32), ("C16", [48], F32),
+        ("FW", [48], F32), ("CF", [32], BF), ("CN", [32], BF), ("ONB", [128], BF), ("BA", [128], BF), ("BO", [128], BF), ("NBO", [128], BF),
         ("NT", [128], BF), ("ID", [128], BF), ("IDF", [128], F32), ("WMU", [144], BF), ("BW", [1], BF),
         ("CL", [264], F32), ("CI", [264], I32), ("CJ", [264], I32), ("CB", [264], F32),
         ("LB", [256], BF), ("HB", [8], F32), ("CT", [S + 64], BF), ("FJ", [L], BF), ("BR", [L], BF), ("TH", [2], F32), ("TN", [2], F32), ("FM", [L], F32),
         ("BX", [336], F32), ("BU", [16], U16),
-        ("QV", [416], F32), ("FQ", [F], F32), ("LM", [128], F32), ("ON32", [32], F32), ("TW", [32], F32), ("T01", [16], F32),
+        ("QV", [416], F32), ("QW", [416], F32), ("FQ", [F], F32), ("LM", [L], F32), ("ON32", [32], F32), ("TW", [32], F32), ("T01", [16], F32),
         ("RK", [16], I32), ("RC", [16], I32), ("RP", [16], I32), ("RX", [16], F32), ("RY", [16], F32), ("PC", [16], F32),
+        ("PX", [1], I32), ("RB", [3], F32), ("RZ0", [16], F32), ("RZ1", [16], F32), ("RZ2", [16], F32), ("M2", [16], BF), ("TS", [1], F32),
 ):
     _sb(_n, _s, _d)
 for _t in range(3):
-    for _n, _s, _d in (("KA", [L], F32), ("ZL", [L], BF), ("DU", [16], F32), ("DT", [16], U16), ("LW", [1024], F32),
-                       ("LF", [L], F32), ("PL", [32], U16), ("LU", [16], U16), ("LSH", [80], U16), ("LSF", [80], U16),
+    for _n, _s, _d in (("KA", [L], F32), ("ZL", [336], BF), ("DU", [16], F32), ("DT", [16], U16), ("LW", [1024], F32),
+                       ("LF", [L], F32), ("PL", [48], U16), ("LU", [16], U16), ("LSH", [80], U16), ("LSF", [80], U16),
                        ("RO", [16], U16), ("RQ", [16], U16)):
         if _t > 0 or _n in ("KA", "DU", "DT", "RO", "RQ"):
             _sb("%s%d" % (_n, _t), _s, _d)
@@ -89,12 +108,12 @@ for _n in range(6):
 for _n in ("PH", "PF"):
     SCRATCH[_n] = ("psum", [128, 512], F32)
     PLACE[_n] = (_n, 0, 512)
-KINDS = [(13, 14), (5, 5), (8, 8)]
+KINDS = [(13, 16), (5, 5), (8, 8)]
 
 
 def helpers(T, topo, core):
     c = [x for x in topo.cores_of(core) if x != core and all(topo.may_write(x, d) for d in T.cores)]
-    return [x for x in c if topo.die(x) == topo.die(core)][0], [x for x in c if topo.die(x) != topo.die(core)][0]
+    return [x for x in c if topo.die(x) == topo.die(core)][0], [x for x in c if topo.die(x) != topo.die(core)]
 
 
 def bits(e):
@@ -103,27 +122,29 @@ def bits(e):
 
 def near(topo, a, b, m):
     e = topo.engines(a, b)
-    return e[len(e) // 2:] if m != "F2" else e[:len(e) // 2]
+    return e[:len(e) // 2] if m in TABLES else e[len(e) // 2:]
 
 
-def land(T, m):
-    return T[m][:, 0:S] if m in ("F2", "F3") else T[m][:, :]
+def piece(T, m, i):
+    return T[m][:, S // PARTS * i:S // PARTS * (i + 1)]
 
 
 def helper_program(g, core, T, topo):
     n = len(T.cores)
     for r, src in enumerate(T.cores):
-        for me, todo in zip(helpers(T, topo, src), (SMALL, TABLES)):
-            if me != core:
-                continue
-            for got, m in todo:
-                d = T.cores[(r + TO[m]) % n]
-                if got == m:
-                    g.wait_ge(T.sem["a_" + m], len(near(topo, src, core, m)))
-                rid, pid = topo.addr(d, core)
-                g.remote_dma(land(T, m), land(T, got), T.sem["a_" + m], T.sem["l_" + m], pid, rid, topo.mask(core, d))
-            for got, m in todo:
-                g.wait_ge(T.sem["l_" + m], len(topo.engines(core, T.cores[(r + TO[m]) % n])))
+        small, big = helpers(T, topo, src)
+        todo = [("a_" + m if got == m else None, T[got][:, :], m, T[m][:, :]) for got, m in SMALL] if core == small else []
+        todo += [("p_%s%d" % (m, i), piece(T, m, i), m, piece(T, m, i)) for m in TABLES for i in range(PARTS) if big[i % len(big)] == core]
+        left = {}
+        for sem, have, m, land in todo:
+            d = T.cores[(r + TO[m]) % n]
+            if sem:
+                g.wait_ge(T.sem[sem], len(near(topo, src, core, m)))
+            rid, pid = topo.addr(d, core)
+            g.remote_dma(land, have, T.sem["a_" + m], T.sem["l_" + m], pid, rid, topo.mask(core, d))
+            left[m] = left.get(m, 0) + len(topo.engines(core, d))
+        for m in left:
+            g.wait_ge(T.sem["l_" + m], left[m])
 
 
 def rank_program(g, core, T, topo):
@@ -137,15 +158,15 @@ def rank_program(g, core, T, topo):
     hist = {}
 
     def b(name, lo=0, hi=None, step=1, p=(0, 128)):
-        name, first, width = PLACE[name]
+        whole, first, width = PLACE[name]
         hi = first + (width if hi is None else hi)
         lo += first
-        ap = T[name][p[0]:p[1], lo:hi] if step == 1 else T[name][p[0]:p[1], lo:hi:step]
-        return (ap, name, (0, 1, lo, hi), None, -(-(hi - lo) // step))
+        ap = T[whole][p[0]:p[1], lo:hi] if step == 1 else T[whole][p[0]:p[1], lo:hi:step]
+        return (ap, whole, (0, 1, lo, hi), None, -(-(hi - lo) // step), name)
 
     def b3(name, c0, c1, lo=0, hi=16, p=(0, 128), cs=1, step=1):
         ap = T[name][p[0]:p[1], slice(c0, c1, cs if cs > 1 else None), slice(lo, hi, step if step > 1 else None)]
-        return (ap, name, (c0, c1, lo, hi), None, -(-(c1 - c0) // cs) * -(-(hi - lo) // step))
+        return (ap, name, (c0, c1, lo, hi), None, -(-(c1 - c0) // cs) * -(-(hi - lo) // step), name)
 
     def b2(name, c, lo, hi, p=(0, 128)):
         return (T[name][p[0]:p[1], c, lo:hi], name, (c, c + 1, lo, hi), None, hi - lo)
@@ -198,7 +219,7 @@ def rank_program(g, core, T, topo):
                 hist[name] = keep + [(reg, w, e, sem, cnt[sem], snap)]
 
     def strided(name):
-        return name in ("E0", "E1")
+        return name in ("ZX1", "ZX2")
 
     def emit(e, f, out, ins):
         reads, writes = regions(ins + offsets(ins + [out])), regions([out])
@@ -223,10 +244,10 @@ def rank_program(g, core, T, topo):
             for name, reg, psum in lst:
                 keep = [x for x in seen.get(name, []) if not (w and inside(x[0], reg) and not psum)]
                 seen[name] = keep + [(reg, w, k)]
-        nodes.append((e, run, dur, lat, sorted(before.items())))
+        nodes.append((e, run, dur, lat, sorted(before.items()), writes))
         return k
 
-    def op(e, f, out, ins, after=None):
+    def op(e, f, out, ins, after=None, done=1):
         win = [x for x in ins if isinstance(x, tuple) and x[3]]
         c = 0.00087 * max(x[4] for x in ins + [out] if isinstance(x, tuple))
         if e == "G":
@@ -238,14 +259,20 @@ def rank_program(g, core, T, topo):
         else:
             two = all(SCRATCH[x[1]][2] in (BF, U16) for x in ins + [out] if isinstance(x, tuple))
             both = len(ins) == 2 and all(isinstance(x, tuple) and x[4] == out[4] and SCRATCH[x[1]][0] == "sbuf" for x in ins)
-            dur = max(0.06, 0.05 + c * (0.5 if two and e == "V" else 2 if both else 1)) + (0.05 if e == "A" else 0)
-        return node(e, lambda: emit(e, f, out, ins), regions(ins + offsets(ins + [out])), regions([out]), dur, 0.0, after)
+            dur = max(0.06, 0.05 + c * (0.5 if two and e == "V" else 2 if both else 1)) + (AFX if e == "A" else 0)
+            dur += 1.3 if out[1] == "RKM" else 0
+        return node(e, lambda: emit(e, f, out, ins), regions(ins + offsets(ins + [out])), regions([out]), dur, 0.0, after, done)
 
     def issue():
         n = len(nodes)
         pred = [[(j, (nodes[j][3] + LAG) * full) for j, full in x[4]] for x in nodes]
-        succ = [[] for _ in nodes]
+        succ, above = [[] for _ in nodes], [0] * n
         for k in range(n):
+            far = 0
+            for j, gap in pred[k]:
+                above[k] |= above[j] | 1 << j
+                far |= above[j] if nodes[j][2] + gap >= LAG else 0
+            pred[k] = [(j, gap) for j, gap in pred[k] if gap > LAG or not far >> j & 1]
             for j, gap in pred[k]:
                 succ[j].append((k, gap))
 
@@ -255,7 +282,10 @@ def rank_program(g, core, T, topo):
                 e, dur = nodes[k][0], nodes[k][2]
                 t = max([last[k]] + [end[j] + gap for j, gap in before[k]])
                 row = taken.setdefault(e, [])
-                i = 0
+                i, hi = 0, len(row)
+                while i < hi:
+                    mid = (i + hi) // 2
+                    i, hi = (mid + 1, hi) if row[mid][1] <= t else (i, mid)
                 while i < len(row) and row[i][0] < t + dur - 1e-9:
                     t = max(t, row[i][1])
                     i += 1
@@ -266,54 +296,62 @@ def rank_program(g, core, T, topo):
         tail = [0.0] * n
         for k in reversed(range(n)):
             tail[k] = nodes[k][2] + max([nodes[k][3]] + [tail[s] + gap for s, gap in succ[k]])
-        def passes(tail, count):
-            best = None
-            for _ in range(count):
-                end = place(sorted(range(n), key=lambda k: (-tail[k], k)), pred, [0.0] * n)
-                span = max(end[k] + nodes[k][3] for k in range(n))
-                if best is None or span < best[0]:
-                    best = (span, end, tail)
-                tail = place(sorted(range(n), key=lambda k: (-end[k], -k)), succ, [x[3] for x in nodes])
-            return best
+        lat, seed = [x[3] for x in nodes], [SEED]
 
-        if not SPAN:
-            best, seed = passes(tail, PASSES), 1
-            now = best
-            for _ in range(TRIES):
-                end, held = now[1], []
-                k = max(range(n), key=lambda k: end[k] + nodes[k][3])
-                by = {(nodes[j][0], round(end[j], 6)): j for j in range(n)}
-                while True:
-                    t = end[k] - nodes[k][2]
-                    ready = max([(0.0, -1)] + [(end[j] + gap, j) for j, gap in pred[k]])
-                    if ready[0] < t - 1e-6:
-                        held.append((k, t - ready[0]))
-                        k = by[nodes[k][0], round(t, 6)]
-                    elif ready[1] < 0:
-                        break
-                    else:
-                        k = ready[1]
-                tail = [-(end[k] - nodes[k][2]) for k in range(n)]
-                for _ in range(2):
-                    seed = (seed * 1103515245 + 12345) % 2147483648
-                    k, wait = held[(seed >> 8) % len(held)]
-                    tail[k] += wait * (1 + (seed >> 4) % 4) / 4 + 0.01
+        def forwards(key):
+            end = place(sorted(range(n), key=lambda k: (key[k], k)), pred, [0.0] * n)
+            span = max(end[k] + lat[k] for k in range(n))
+            return (span + 0.5 * sum(end) / n, span, end)
+
+        def turned(end):
+            return forwards([-x for x in place(sorted(range(n), key=lambda k: (-end[k], -k)), succ, lat)])
+
+        def draw():
+            seed[0] = (seed[0] * 1103515245 + 12345) % 2147483648
+            return (seed[0] >> 8) / 8388608.0
+
+        def moved(end):
+            k, held = max(range(n), key=lambda k: end[k] + lat[k]), []
+            by = {(nodes[j][0], round(end[j], 6)): j for j in range(n)}
+            key = [end[j] - nodes[j][2] for j in range(n)]
+            while k >= 0:
+                ready, j = max([(0.0, -1)] + [(end[j] + gap, j) for j, gap in pred[k]])
+                if ready < key[k] - 1e-6:
+                    j = by[nodes[k][0], round(key[k], 6)]
+                    held.append((k, ready, j))
+                k = j
+            k, ready, j = held[int(draw() * len(held))]
+            if draw() < 0.6:
+                key[k] = min(key[j], ready + (key[j] - ready) * draw()) - 1e-3
                 for k in reversed(range(n)):
-                    tail[k] = max([tail[k]] + [tail[s] + 1e-6 for s, gap in succ[k]])
-                other = passes(tail, 2)
-                if other[0] <= now[0] + 0.05:
+                    for s, gap in succ[k]:
+                        if key[k] >= key[s]:
+                            key[k] = key[s] - 1e-6
+            else:
+                key[j] = key[k] + 1e-3 + 2 * draw() * draw()
+                for k in range(n):
+                    for s, gap in pred[k]:
+                        if key[k] <= key[s]:
+                            key[k] = key[s] + 1e-6
+            return forwards(key)
+
+        NODES.append(nodes)
+        if not SPAN:
+            best = now = forwards([-x for x in tail])
+            for i in range(TRIES):
+                other = turned(now[2]) if i % 50 < (4 if i < 50 else 1) else moved(now[2])
+                if other[0] - now[0] < -0.1 * 0.1 ** (i / TRIES) * math.log(1 - draw()):
                     now = other
-                if now[0] < best[0]:
-                    best = now
-            SPAN.extend(best)
+                best = min(best, now)
+            SPAN.extend(best[1:])
         for k in sorted(range(n), key=lambda k: (SPAN[1][k] - nodes[k][2], SPAN[1][k], k)):
             nodes[k][1]()
 
     def A_(o):
         return o[0] if isinstance(o, tuple) else o
 
-    def tt(out, a, c, o):
-        op("V", lambda q: q.tensor_tensor(A_(out), A_(a), A_(c), o), out, [a, c])
+    def tt(out, a, c, o, behind=None):
+        return op("V", lambda q: q.tensor_tensor(A_(out), A_(a), A_(c), o), out, [a, c], behind, 0)
 
     def ts(out, a, s1, o1, s2=None, o2=None):
         if o2 is None:
@@ -334,6 +372,8 @@ def rank_program(g, core, T, topo):
         op("V", lambda q: q.transpose(A_(out), A_(a)), out, [a])
 
     def act(out, a, fn=AF.Copy, scale=1.0, bias=0.0):
+        if fn in (AF.Copy, AF.Identity) and out[-1] in ONV and not a[3]:
+            return cp(out, a) if (scale, bias) == (1.0, 0.0) else ts(out, a, scale, OP.mult, bias, OP.add)
         op("A", lambda q: q.activation(A_(out), A_(a), fn, bias=A_(bias), scale=A_(scale)), out, [a, scale, bias])
 
     tiles = {}
@@ -351,7 +391,7 @@ def rank_program(g, core, T, topo):
         if len(m) > 4:
             return [mms(*m[i:i + 4]) for i in range(0, len(m), 4)]
         node("P", lambda: [mm_now(*x) for x in m], regions([x[1] for x in m] + [x[2] for x in m]), regions([x[0] for x in m]),
-             sum(0.02 + 0.00045 * max(64, x[0][4]) * (4 if SCRATCH[x[1][1]][2] == F32 else 1) for x in m))
+             sum(PFX + PEC * max(64, x[0][4]) * (4 if SCRATCH[x[1][1]][2] == F32 else 1) for x in m))
 
     def iota(out, pat, base, cm, after=None):
         if SCRATCH[out[1]][2] == I32:
@@ -365,14 +405,14 @@ def rank_program(g, core, T, topo):
     def scat(win, width, off, n, val):
         cp(ind(b(win, 0, width), b(off, 0, n)), val)
 
-    def load(e, out, src, name, behind):
-        w = regions([out])
+    def load(e, out, src, name, behind, when=None):
+        w, r = regions([out]), regions([when])
 
         def run():
-            sync(e, [], w)
+            sync(e, r, w)
             Q[e].dma_start(out[0], src).then_inc(T.sem["d_" + name], 16)
             note(e, [], w, "d_" + name, 16)
-        return node(e, run, [], w, 0.1, HOP + (2.0 if out[4] > 700 else 0.5), behind, 0)
+        return node(e, run, r, w, 0.1, HOP + (2.0 if out[4] > 700 else 0.5), behind, 0)
 
     def store(e, dst, a, name):
         r = regions([a])
@@ -384,22 +424,27 @@ def rank_program(g, core, T, topo):
         node(e, run, r, [], 0.1, HOP + (2.0 if name == "yt" else 0.3))
 
     small, big = helpers(T, topo, core)
+    sent = [None]
 
     def send(m, src, lats):
-        to = big if m in ("F2", "F3") else T.cores[(rank + TO[m]) % len(T.cores)] if m == "U2D" else small
-        es = topo.engines(core, to) if m == "U2D" else near(topo, core, to, m)
         r = regions([src])
-        rid, pid = topo.addr(to, core)
+        if m in TABLES:
+            calls = [(big[i % len(big)], piece(T, m, i), piece(T, "HT", i), "p_%s%d" % (m, i)) for i in range(PARTS)]
+        else:
+            calls = [(T.cores[(rank + TO[m]) % len(T.cores)] if m == "U2D" else small, T[m][:, :], src[0], "a_" + m)]
 
         def run():
             sync("G", r, [])
-            g.remote_dma(land(T, m), src[0], T.sem["a_" + m], T.sem["l_" + m], pid, rid, bits(es))
-            note("G", r, [], "l_" + m, len(es))
-        k = node("G", run, r, [], 0.1)
+            for to, land, have, sem in calls:
+                es = topo.engines(core, to) if m == "U2D" else near(topo, core, to, m)
+                rid, pid = topo.addr(to, core)
+                g.remote_dma(land, have, T.sem[sem], T.sem["l_" + m], pid, rid, bits(es))
+                note("G", r, [], "l_" + m, len(es))
+        k = sent[0] = node("G", run, r, [], 1.2 if m == "RQZ" else 0.15 * len(calls), 0.0, sent[0], 0)
         for x, lat in lats.items():
             far = T.cores[(rank - TO[x]) % len(T.cores)]
-            by = far if x == "U2D" else helpers(T, topo, far)[x in ("F2", "F3")]
-            arrives(x, len(topo.engines(by, core)), lat, k)
+            by = [far] if x == "U2D" else helpers(T, topo, far)[1] * PARTS if x in TABLES else helpers(T, topo, far)[:1]
+            arrives(x, sum(len(topo.engines(y, core)) for y in by[:PARTS]), lat, k)
         return k
 
     def arrives(x, n, lat, k):
@@ -408,18 +453,14 @@ def rank_program(g, core, T, topo):
 
     k = load("S", b("ZF", 80, 288), T.zf[:, 0:L], "zf0", None)
     j = load("A", b("EF", 96, 320), T.ef[:, 0:224], "ef0", None)
-    k = load("S", b("EF", 16, 96), T.ef[:, 544:F], "ef1", k)
     j = load("A", b("EH", 96, 320), T.eh[:, 0:224], "eh0", j)
-    k = load("S", b("EH", 16, 96), T.eh[:, 544:F], "eh1", k)
     j = load("A", b("HT", 0, S), T.tab[:, :], "tab", j)
-    k = load("S", b("ZF", 0, 80), T.zf[:, 544:F], "zf1", k)
-    k = load("S", b("ZF", 288, F), T.zf[:, L:544], "zf2", k)
-    k = load("S", b("EH", 320, F + 16), T.eh[:, 224:544], "eh2", k)
-    k = load("S", b("EF", 320, F + 16), T.ef[:, 224:544], "ef2", k)
+    ms(b("EF", 80, 96), 0)
+    ms(b("EH", 80, 96), 0)
 
     ms(b("ONB"), 1.0)
     iota(b("PI"), [[0, 1]], 0, 1)
-    iota(b("C16"), [[16, 32]], 0, 0)
+    iota(b("C16"), [[16, 48]], 0, 0)
     iota(b("PC"), [[0, 8], [1, 2]], 0, 0)
     iota(b("KIO"), [[0, 13], [1, 16]], 0, 0)
     asel(b("ID"), b("ONB"), [[-1, 128]], OP.is_equal, 0, 1)
@@ -430,48 +471,59 @@ def rank_program(g, core, T, topo):
     cp(b("PM"), b("PJ"))
     cp(b("MH1"), b("PK"))
     ts(b("FW"), b("C16"), b("PM"), OP.add)
-    column = {}
 
     def aff(out, a, scale, bias):
-        if not isinstance(bias, tuple):
-            bias = const(bias)
-        act(out, a, AF.Identity, scale, bias)
-
-    def const(v, p=(0, 128)):
-        if v not in column:
-            column[v] = len(column)
-            ms(b("MB", column[v], column[v] + 1), float(v))
-        return b("MB", column[v], column[v] + 1, p=p)
+        if isinstance(bias, tuple):
+            act(out, a, AF.Identity, scale, bias)
+        else:
+            act(out, a, AF.Copy, scale, float(bias))
 
     def fill(out, v, after):
         iota(out, [[0, out[4]]], v, 0, after)
 
-    act(b("RKM"), b("KIO"), AF.Sigmoid, 400.0, const(-200))
+    act(b("RKM"), b("KIO"), AF.Sigmoid, 400.0, -200.0)
     aff(b("MH0"), b("MH1"), -1.0, 1)
     ms(b("WMU"), 0.0)
     act(b("WMU", 15, 143, 16), b("BO", 0, 128, 16), scale=float(PEN))
     act(b("NBO"), b("BO"), scale=-1.0)
     act(b("IDF"), b("ID"))
-    act(b("IDN"), b("ID"), scale=-1024.0)
+    ts(b("PY"), b("PM"), -1.0, OP.add)
+    act(b("IDN"), b("ID"), scale=b("PY"))
     aff(b("KAD"), b("KIO"), -4096.0, 61440)
     act(b("KAB"), b("KAD", 0, 128))
     ts(b("M16"), b("KIO"), b("PM"), OP.is_equal)
 
+    tt(b("PX"), b("PJ"), b("PK"), OP.add)
+    ts(b("PX"), b("PX"), 1, OP.bitwise_and)
+    ts(b("PC"), b("PC"), b("MH1"), OP.not_equal)
+
     def places(x):
         nc, s = KINDS[x]
         off = 32.0 * ((nc + 1) // 2) + 16
-        ts(b("RK", 0, s), b("FW", 0, s), 1.0 / s, OP.mult, 0.5 / s - 0.5, OP.add)
-        ts(b("RX", 0, s), b("RK", 0, s), -float(s), OP.mult)
-        tt(b("RC", 0, s), b("RX", 0, s), b("FW", 0, s), OP.add)
-        ts(b("RP", 0, s), b("RC", 0, s), 1, OP.bitwise_and)
-        ts(b("RX", 0, s), b("RP", 0, s), b("MH1"), OP.not_equal, off, OP.mult)
-        ts(b("RY", 0, s), b("RC", 0, s), 16.0, OP.mult)
-        tt(b("RX", 0, s), b("RX", 0, s), b("RK", 0, s), OP.add)
-        tt(b("RX", 0, s), b("RX", 0, s), b("RY", 0, s), OP.add)
-        ts(b("RO%d" % x, 0, s), b("RX", 0, s), 32.0 * (nc + 1) - 1, OP.min)
-        ts(b("RY", 0, nc), b("PC", 0, nc), b("MH1"), OP.not_equal, off, OP.mult)
-        tt(b("RY", 0, nc), b("RY", 0, nc), b("FW", 0, nc), OP.add)
-        cp(b("RQ%d" % x, 0, nc), b("RY", 0, nc))
+        if s == 5:
+            ts(b("RK", 0, s), b("FW", 0, s), 1.0 / s, OP.mult, 0.5 / s - 0.5, OP.add)
+            ts(b("RX", 0, s), b("RK", 0, s), -float(s), OP.mult)
+            tt(b("RC", 0, s), b("RX", 0, s), b("FW", 0, s), OP.add)
+            ts(b("RP", 0, s), b("RC", 0, s), 1, OP.bitwise_and)
+            ts(b("RX", 0, s), b("RP", 0, s), b("MH1"), OP.not_equal, off, OP.mult)
+            ts(b("RY", 0, s), b("RK", 0, s), 1.0 - 16 * s, OP.mult)
+            tt(b("RX", 0, s), b("RX", 0, s), b("RY", 0, s), OP.add)
+            aff(b("RY", 0, s), b("FW", 0, s), 16.0, 0)
+            tt(b("RX", 0, s), b("RX", 0, s), b("RY", 0, s), OP.add)
+            cp(b("RO%d" % x, 0, s), b("RX", 0, s))
+        else:
+            r = b("RB", x, x + 1)
+            if s == 16:
+                ts(r, b("PM"), nc - 1.0, OP.min, 16.0, OP.mult)
+            else:
+                ts(r, b("PM"), 8.0, OP.is_ge, -127.0, OP.mult)
+                aff(r, b("PM"), 16.0, r)
+            ts(r, b("PX"), off, OP.mult, r, OP.add)
+            ts(b("RO%d" % x, 0, s), b("C16", 0, s), 1.0 / s, OP.mult, r, OP.add)
+        r = b("RZ%d" % x, 0, nc)
+        aff(r, b("PC", 0, nc), off, b("PM"))
+        tt(r, r, b("C16", 0, nc), OP.add)
+        cp(b("RQ%d" % x, 0, nc), r)
 
     def lists(x, src, lo, y, out, key=None):
         nc, s = KINDS[x]
@@ -484,27 +536,57 @@ def rank_program(g, core, T, topo):
         elif key:
             tt(key, ind(b(y, 0, n1 + n2), b("RQ%d" % x, 0, nc)), b("KAD", 0, 16 * nc), OP.add)
 
-    bank = [0]
+    bank, row = [0], [None]
 
-    def look(x, win, lst, z, cm, c0, chunks, k1):
+    def look(x, win, lst, z, cm, c0, chunks, k1, wide=None):
         nc, s = KINDS[x]
-        for j in range(k1):
+        for j in k1:
             lo, hi = 16 * c0, 16 * (c0 + nc)
-            tt((T[cm][:, lo:hi, j], cm, (lo, hi, j, j + 1), None, hi - lo), ind(win, b(lst, s * j, s * j + nc)), z, OP.is_le)
+            row[0] = tt((T[cm][:, lo:hi, j], cm, (lo, hi, j, j + 1), None, hi - lo), ind(win, b(lst, s * j, s * j + nc)), z, OP.is_le,
+                        row[0] if j or x else None)
         for k0, k in chunks:
             n = k - k0
-            ga, t = "GA%d" % (bank[0] % 3), "T%d" % (bank[0] % 6)
+            ga, t = "GA%d" % (bank[0] % 6), "T%d" % (bank[0] % 6)
             bank[0] += 1
-            act(b(ga, 0, 16 * s * n), ind(win, b(lst, s * k0, s * k)), scale=-1.0)
+            if s == nc:
+                act(b(ga, 0, 16 * s * n), ind(win, b(lst, s * k0, s * k)), scale=-1.0)
             m = []
             for j in range(n):
-                o = b3(t, 0, nc * n, j, 16, step=n)
-                m += [(o, b("ID"), z, True, False), (o, b("ID"), b(ga, 16 * s * j, 16 * (s * j + nc)), False, True)]
+                o, got = b3(t, 0, nc * n, j, 16, step=n), b(ga, 16 * nc * j, 16 * nc * (j + 1))
+                if s != nc:
+                    act(got, ind(win, b(lst, s * (k0 + j), s * (k0 + j) + nc)), scale=-1.0)
+                m += [(o, b("ID"), got, False, j == n - 1)] if wide else [(o, b("ID"), z, True, False), (o, b("ID"), got, False, True)]
+            if wide:
+                mms((b3(t, 0, nc * n), b("ID"), wide, True, False))
             mms(*m)
-            act(b3(cm, 16 * c0, 16 * (c0 + nc), k0, k), b3(t, 0, nc * n), AF.Sigmoid, 400.0, const(200))
+            act(b3(cm, 16 * c0, 16 * (c0 + nc), k0, k), b3(t, 0, nc * n), AF.Sigmoid, 400.0, 200.0)
+
+    def look2(win, lst, z, cm, na):
+        for j in range(8):
+            out = (T[cm][:, :, j], cm, (0, 256, j, j + 1), None, 256)
+            got = ind(win, b(lst, 16 * j, 16 * j + 16))
+            if j < 8 - na:
+                row[0] = tt(out, got, z, OP.is_le, row[0])
+                continue
+            ga, t = b("GA%d" % (bank[0] % 6), 0, 256), b3("T%d" % (bank[0] % 6), 0, 16)
+            bank[0] += 1
+            act(ga, got, scale=-1.0)
+            mms((t, b("ID"), z, True, False))
+            mms((t, b("ID"), ga, False, True))
+            act(out, t, AF.Sigmoid, 400.0, 200.0)
+
+    def sums2(key):
+        out = b("PH", 80, L)
+        mms((out, b("IDF"), key, True, False), (out, b("ID"), b("KAB"), False, False))
+        mms(*[(b("PH", 80 + h, L, 2), b("WMU", 15 - m, 143 - m), b3("CDH", 128 * h + m, 128 * h + 128, 0, 8, cs=16), False, h + m == 16)
+              for h in (0, 1) for m in range(16)])
+
+    def far_sums(cm, r0, r1, k0, k1, bank, lo):
+        out = b(bank, lo, lo + (r1 - r0) // 16 * (k1 - k0))
+        mms(*[(out, b("WMU", 15 - m, 143 - m), b3(cm, r0 + m, r1, k0, k1, cs=16), m == 0, m == 15) for m in range(16)])
 
     def pairs(n, w):
-        return [(k, min(16, k + w)) for k in range(16 - n, 16, w)], 16 - n
+        return [(k, min(16, k + w)) for k in range(16 - n, 16, w)], range(16 - n)
 
     def sums(cm, c0, c1, key):
         out = b("PH", 16 * c0, 16 * c1)
@@ -552,18 +634,22 @@ def rank_program(g, core, T, topo):
             else:
                 pp = (0, L - NB)
                 out, src, x = b3("E1", 0, 5, 64 * a - 256, 64 * a - 192, p=pp), b3("T%d" % a, 0, 20, p=pp), 1
-            if a in (2, 3, 5):
+            if a in EA:
                 act(out, src, AF.Relu, 1024.0, b("TN", x, x + 1, p=pp))
             else:
                 ts(out, src, b("TH", x, x + 1, p=pp), OP.is_gt)
         mms((CS, b("IDF"), yy, True, False))
-        for c0, c1 in ECUT:
-            for a in range(4):
+        for a in range(4):
+            for c0, c1 in ECA if a in EA else ECUT:
                 over(a, c0, c1)
-            mms(*[(b("PF", 224 + c, 225 + c), b2("E0", c, 0, 128), b("BW"), False, False) for c in range(c0, c1)])
         over(4, 0, 5)
         over(5, 0, 5)
-        mms(*[(b("PF", 224 + c, 225 + c), b2("E1", c - 8, 0, 128, p=(0, 80)), b("BW", p=(0, 80)), False, c == 12) for c in range(8, 13)])
+        for i, (c0, c1) in enumerate(ECUT):
+            if i == ORD:
+                mms(*[(b("PF", 224 + c, 225 + c), b2("E1", c - 8, 0, 128, p=(0, 80)), b("BW", p=(0, 80)), False, False) for c in range(8, 13)])
+            mms(*[(b("PF", 224 + c, 225 + c), b2("E0", c, 0, 128), b("BW"), False, c == 12 and ORD < 2) for c in range(c0, c1)])
+        if ORD == 2:
+            mms(*[(b("PF", 224 + c, 225 + c), b2("E1", c - 8, 0, 128, p=(0, 80)), b("BW", p=(0, 80)), False, c == 12) for c in range(8, 13)])
         ts(b("WU", 0, 13), yy, float(OKB + S), OP.max, 1.0 / PEN, OP.mult)
         act(grown, ind(b("TW"), b("WU", 0, 13)))
         tt(b("DS", 0, 13), CS, b("DU%d" % t, 0, 13), OP.min)
@@ -572,16 +658,21 @@ def rank_program(g, core, T, topo):
     def lanes(t, n, fill, val):
         pls, lw, lu = "PL%d" % t, "LW%d" % t, "LU%d" % t
         scan(b("UC", 0, n), b("ON32", 0, n), b("UU", 0, n), OP.mult, OP.add)
+        tt(b("NU", 0, n), b("UU", 0, n), b("CN", 0, n), OP.mult)
         out = b("PH", 224, 224 + n)
-        mms((out, b("NT"), b("UU", 0, n), True, False), (out, b("IDN"), b("UU", 0, n), False, False))
-        mms((out, b("BO"), b("UC", 0, n), False, True), (b("PH", 256, 257), b("BO"), b("UC", n - 1, n), True, True))
-        tt(b("QQ", 0, n), out, b("DMF", 0, n), OP.min)
-        ts(b(pls, 0, n), b("QQ", 0, n), 1023.0, OP.add)
-        ts(b("TB"), b("PH", 256, 257), -1.0, OP.mult, fill - BIG, OP.add)
-        scat(lw, 1024, pls, n, val)
-        act(b("LD"), b("LM"), AF.Relu, 1.0, b("TB"))
+        mms((out, b("ID"), b("CF", 0, n), True, False))
+        mms((out, b("NT"), b("UU", 0, n), False, False), (out, b("IDN"), b("UU", 0, n), False, False))
+        mms((out, b("ID"), b("NU", 0, n), False, False), (out, b("BO"), b("UC", 0, n), False, True),
+            (b("PH", 256, 257), b("BO"), b("UC", n - 1, n), True, True))
+        ts(b(pls, 0, n), out, b("PM"), OP.subtract)
+        aff(b("TS"), b("PH", 256, 257), -KQ, (fill - BIG) * KQ + 0.5)
+        if t in LWA:
+            act(ind(b(lw, 0, 1024), b(pls, 0, n)), val, AF.Sigmoid)
+        else:
+            scat(lw, 1024, pls, n, b("QW", 416 - 16 * n - (128 if t == 1 else 0), 288 if t == 1 else 416))
+        aff(b("LD"), b("LM", 0, 128), KQ, b("TS"))
         scan(b("XS"), b("LD"), b(lw, 0, 128), OP.max, OP.min)
-        cp(b(lu, 0, 8), b("XS", 15, 128, 16))
+        ts(b(lu, 0, 8), b("XS", 15, 128, 16), 1.0 / KQ, OP.mult, 0.3 - 0.5 / KQ, OP.add)
 
     def wrap(x):
         act(b(x, S, S + PAD), b(x, 0, PAD))
@@ -589,9 +680,10 @@ def rank_program(g, core, T, topo):
     def step(t, ftab, update, later):
         lu, zl = b("LU%d" % t, 0, 8), "ZL%d" % t
         home, far = b("HT", 0, S + PAD), b(ftab, 0, S + PAD)
-        look(1, home, "LSH%d" % t, b(zl, 0, 80), "CMH", 0, *pairs(16, 4))
+        look(1, b("HT", 0, S), "LSH%d" % t, b(zl, 0, 80), "CMH", 0, *pairs(16, 4), b3("ZX%d" % t, 0, 20))
         act(b("DQ"), ind(b("D"), lu))
         act(b(zl, 80, L), ind(b("ZF"), lu))
+        act(b(zl, L, 336), b(zl, 80, L))
         tt(b("XH", 16, 144), ind(b("EH", 16, 16 + F), lu), b("DQ"), OP.add)
         lists(2, "XH", 16, "YH", "LDH", b("KA%d" % t, 80, L))
         tt(b("XF", 16, 144), ind(b("EF", 16, 16 + F), lu), b("DQ"), OP.add)
@@ -599,26 +691,38 @@ def rank_program(g, core, T, topo):
         act(b("LF%d" % t, 80, L), ind(b("FQ"), lu))
         update()
         sums("CMH", 0, 5, b("KA%d" % t, 0, 80))
-        look(1, far, "LSF%d" % t, b(zl, 0, 80), "CMF", 0, *pairs(16, 4))
-        look(2, home, "LDH", b(zl, 80, L), "CMH", 5, *pairs(KDH, 4))
-        sums("CMH", 5, 13, b("KA%d" % t, 80, L))
-        look(2, far, "LDF", b(zl, 80, L), "CMF", 5, *pairs(KDF, 4))
+        look2(home, "LDH", b(zl, 80, 336), "CDH", KD[2 * t - 2])
+        look(1, b(ftab, 0, S), "LSF%d" % t, b(zl, 0, 80), "CMF", 0, *pairs(16, 4), b3("ZX%d" % t, 0, 20))
+        sums2(b("KA%d" % t, 80, L))
+        look2(far, "LDF", b(zl, 80, 336), "CDF", KD[2 * t - 1])
         home_max()
-        far_max(0, 5, 0, 16, "PF", 0, b("YY", 0, 5), b("AP", 0, 5))
-        far_max(5, 13, 0, 8, "PF", 80, b("AP", 5, 13), b("AP", 5, 13))
-        far_max(5, 13, 8, 16, "PH", 320, b("YY", 5, 13), b("AP", 5, 13))
+        if SFIRST:
+            far_sums("CMF", 0, 80, 0, 16, "PF", 0)
+        far_sums("CDF", 0, 256, 0, 4, "PF", 80)
+        if not SFIRST:
+            far_sums("CMF", 0, 80, 0, 16, "PF", 0)
+        far_sums("CDF", 0, 256, 4, 8, "PH", 320)
+        scan(b("FS", 0, 144), b("RK4", 0, 144), b("PF", 0, 144), OP.mult, OP.max)
+        scan(b("FS", 320, 384), b("RK4", 80, 144), b("PH", 320, 384), OP.mult, OP.max)
+        tt(b("YY", 0, 5), b("FS", 15, 80, 16), b("AP", 0, 5), OP.max)
+        for lo in (80, 112, 320, 352):
+            tt(b("AP" if lo < 352 else "YY", 5, 13), b("FS", lo + 3, lo + 32, 4), b("AP", 5, 13), OP.max)
         later(b("YY", 0, 13))
 
     z0 = b("ZF", 80, 288)
-    send("RQZ", z0, {"RQZ": 2 * HOP + 2.0, "U2Z": 2 * HOP + 4.0})
+    send("RQZ", z0, {"RQZ": 2 * HOP + 1.5, "U2Z": 2 * HOP + 4.0})
     places(0)
     lists(0, "EF", 96, "YA", "LF0")
     asked = send("RQL", b("LF0"), {"RQL": 2 * HOP + RQX})
     lists(0, "EH", 96, "YB", "LH0", b("KA0"))
-    send("F2", b("HT", 0, S), {"F2": 11.0})
+    k = load("S", b("ZF", 0, 80), T.zf[:, 544:F], "zf1", asked, b("LH0"))
+    k = load("S", b("EH", 16, 96), T.eh[:, 544:F], "eh1", k)
+    k = load("S", b("EF", 16, 96), T.ef[:, 544:F], "ef1", k)
+    k = load("S", b("EH", 320, F + 16), T.eh[:, 224:544], "eh2", k)
+    k = load("S", b("EF", 320, F + 16), T.ef[:, 224:544], "ef2", k)
+    k = load("S", b("ZF", 288, F), T.zf[:, L:544], "zf2", k)
+    send("F2", b("HT", 0, S), {"F2": 16.0})
     asel(b("NT"), b("NBO"), [[-1, 128]], OP.is_gt, 0, 1)
-    iota(b("CL", 0, 256), [[1, 256]], 0, 0)
-    iota(b("CL", 256, 264), [[256, 8]], 0, 0)
     iota(b("FJ"), [[1, L]], 48, 0, asked)
     iota(b("TH"), [[NB, 2]], 48, 1, asked)
     iota(b("TW"), [[1, 32]], 0, 0)
@@ -626,40 +730,42 @@ def rank_program(g, core, T, topo):
         iota(b("OC", x, x + 676), [[0, 676]], -1, 0, asked)
     tab = b("HT", 0, S)
     look(0, tab, "LH0", z0, "CMH", 0, *pairs(KA0, 2))
-    look(0, tab, "RQL", b("RQZ"), "CMF", 0, *pairs(KR0, 2))
+    look(0, tab, "RQL", b("RQZ"), "CMF", 0, KR0, [k for k in range(16) if not any(x <= k < y for x, y in KR0)])
     ms(b("KFO"), 0.0)
-    act(b("RK8"), b("RKM", 0, L, 2))
+    act(b("RK4", 0, 80), b("RKM", 0, 80))
+    for lo in (80, 132):
+        act(b("RK4", lo, lo + 52), b("RKM", 0, L, 4))
     if HFIRST:
         sums("CMH", 0, 13, b("KA0"))
-    far_max(0, 13, 0, 8, "PF", 0, b("KFO", 0, 13), b("KFO", 0, 13))
-    far_max(0, 13, 8, 16, "PH", 320, b("KFO", 0, 13), b("KFO", 0, 13))
+    w = CUT0
+    iota(b("RKA", 0, 13 * w), [[0, 13], [1, w]], 0, 0, asked)
+    iota(b("RKB", 0, 13 * (16 - w)), [[0, 13], [1, 16 - w]], 0, 0, asked)
+    for x, n_ in (("RKA", 13 * w), ("RKB", 13 * (16 - w))):
+        act(b(x, 0, n_), b(x, 0, n_), AF.Sign)
+    far_sums("CMF", 0, L, 0, w, "PF", 0)
+    far_sums("CMF", 0, L, w, 16, "PH", 320)
+    scan(b("FS", 0, 13 * w), b("RKA", 0, 13 * w), b("PF", 0, 13 * w), OP.mult, OP.max)
+    scan(b("FS", 320, 528 - 13 * w), b("RKB", 0, 208 - 13 * w), b("PH", 320, 528 - 13 * w), OP.mult, OP.max)
+    tt(b("KFO", 0, 13), b("FS", w - 1, 13 * w, w), b("FS", 335 - w, 528 - 13 * w, 16 - w), OP.max)
     if not HFIRST:
         sums("CMH", 0, 13, b("KA0"))
-    told = send("KFR", b("KFO"), {"KFR": 2 * HOP + 0.4})
+    told = send("KFR", b("KFO"), {"KFR": 2 * HOP + KX})
     home_max()
-    ms(b("P2"), 0.5)
-    ms(b("ON32"), 1.0)
-    ms(b("Q1"), 0.0)
-    scan(b("P3"), b("P2"), b("Q1"), OP.mult, OP.add, 4096.0)
-    tt(b("P2"), b("P3"), b("M16", 0, 16), OP.mult)
-    scan(b("P3"), b("ON32", 0, 16), b("P2"), OP.mult, OP.add)
-    ts(b("CI"), b("CL"), b("P3", 15, 16), OP.mult)
-    ts(b("CJ"), b("CI"), 2048, OP.bitwise_and)
-    ts(b("CB"), b("CJ"), 1.0 / 1024.0, OP.mult, -1.0, OP.add)
-    ts(b("ML", 0, 1), b("PM"), 8.0, OP.is_lt)
-    ts(b("ML", 1, 2), b("PM"), 11.0, OP.is_lt)
-    tt(b("ML", 1, 2), b("ML", 1, 2), b("ML", 0, 1), OP.subtract)
-    act(b("HB"), b("CB", 256, 264), scale=b("ML", 1, 2))
+    fill(b("ON32"), 1, asked)
+    ts(b("CT", 0, 1), b("PM"), 11.0, OP.is_lt, -1.0, OP.mult)
+    act(b("M2"), b("M16", 0, 16), scale=2.0)
     fill(b("CT", S, S + 16), 0, asked)
-    for h in range(8):
-        aff(b("CT", 256 * h, 256 * h + 256), b("CB", 0, 256), b("ML", 0, 1), b("HB", h, h + 1))
-    ts(b("MC", 0, 1), b("PM"), 11.0, OP.is_equal, 1.0 / 256, OP.mult)
+    for j in range(11):
+        for lo in range(0, 1 << j, 512):
+            hi = min(1 << j, lo + 512)
+            ts(b("CT", (1 << j) + lo, (1 << j) + hi), b("CT", lo, hi), b("M2", j, j + 1), OP.add)
+    act(b("MC", 0, 1), b("M2", 11, 12), scale=1.0 / 512)
     act(b("FJ"), b("FJ"), scale=b("MC", 0, 1))
-    ts(b("TN"), b("TH"), 0.5, OP.add, 1.0 / 65536, OP.mult)
+    aff(b("TN"), b("TH"), 1.0 / 65536, 0.5 / 65536)
     tt(b("TN"), b("TN"), b("TH"), OP.mult)
-    ts(b("TH"), b("TN"), 11.0, OP.add)
-    ts(b("TN"), b("TH"), -1024.0, OP.mult)
-    ms(b("BW"), BIG)
+    aff(b("TH"), b("TN"), 1.0, 11)
+    act(b("TN"), b("TH"), scale=-1024.0)
+    fill(b("BW"), int(BIG), asked)
     act(b("T01"), b("TW", 0, 16))
     ts(b("NU"), b("TW"), 9.0, OP.is_ge)
     tt(b("TW"), b("TW"), b("NU"), OP.mult)
@@ -668,12 +774,18 @@ def rank_program(g, core, T, topo):
     iota(b("FQ", 0, 80), [[1, 80]], 544, 0, told)
     iota(b("LF1", 0, 80), [[1, 80]], 544, 0, told)
     iota(b("LF2", 0, 80), [[1, 80]], 464, 0, told)
-    iota(b("LM"), [[1, 128]], int(BIG), 0, asked)
-    tt(b("LM"), b("LM"), b("M16", 0, 128), OP.mult)
+    if len(LWA) < 2:
+        aff(b("QW"), b("QV"), KQ, 0.5)
+    if LWA:
+        act(b("QV"), b("QV"), scale=4 * KQ)
+    iota(b("LM"), [[1, L]], int(BIG), 0, asked)
+    tt(b("LM"), b("LM"), b("M16"), OP.mult)
+    aff(b("FM"), b("LM"), 1.0, -BIG)
     for t in range(3):
         aff(b("DU%d" % t, 0, 13), b("FW", 0, 13), 1.0, OKB + S + PAD + L * t)
     aff(b("DUQ", 0, 13), b("FW", 0, 13), 1.0, OKB + S + F)
-    aff(b("DMF"), b("FW"), 1.0, 512 - 1023)
+    aff(b("CF"), b("C16", 0, 32), -1.0, 1008)
+    aff(b("CN"), b("C16", 0, 32), 1.0, -1008)
     for n_ in ("DT0", "DT1"):
         ms(b(n_), 0)
     for n_, lo, hi, v_ in (("EH", 0, 16, 0), ("EF", 0, 16, 0), ("EH", F + 16, F + 32, 0), ("EF", F + 16, F + 32, 0), ("LW1", 0, 128, int(BIG))):
@@ -687,30 +799,30 @@ def rank_program(g, core, T, topo):
         lists(1, "EH", 16 + q0, "YS", "LSH%d" % t, b("KA%d" % t, 0, 80))
         lists(1, "EF", 16 + q0, "YT", "LSF%d" % t)
         act(b("ZL%d" % t, 0, 80), b("ZF", q0, q0 + 80))
+        for j in range(4):
+            act(b3("ZX%d" % t, 0, 20, j, 16, step=4), b("ZF", q0, q0 + 80))
     tt(b("YY", 0, 13), b("AP", 0, 13), b("KFR", 0, 13), OP.max)
     decide(0, b("YY", 0, 13), b("D", 80, 288))
-    send("U2D", b("DT0"), {"U2D": HOP + 0.3})
+    send("U2D", b("DT0"), {"U2D": HOP + UX})
 
     ts(b("UU", 0, 13), CS, float(OKB + S), OP.is_ge)
     scat("HT", WT, "DT0", 13, z0)
     wrap("HT")
-    send("F3", b("HT", 0, S), {"F3": 11.0})
+    send("F3", b("HT", 0, S), {"F3": 17.0})
     lanes(1, 13, 288, b("QV", 80, 288))
+    aff(b("TB"), b("TS"), -1.0 / KQ, 80 - BIG + 0.5 / KQ)
 
     def update1():
-        send("V3Z", b("ZL1"), {"V3Z": 2 * HOP + 1.0})
+        send("V3Z", b("ZL1", 0, L), {"V3Z": 2 * HOP + 1.0})
         scat("F2", WT, "U2D", 13, b("U2Z"))
         wrap("F2")
 
     def later1(yy):
-        aff(b("FM"), b("FQ", 80, 288), 1.0, 2)
-        tt(b("FM"), b("FM"), b("M16"), OP.mult)
-        aff(b("FM"), b("FM"), 1.0, -2)
         scat("OC", WT, "DT0", 13, b("FQ", 80, 288))
-        ts(b("PL1", 13, 21), b("FW", 13, 21), b("TB"), OP.subtract, 80.0 - BIG, OP.add)
+        ts(b("PL1", 13, 21), b("FW", 13, 21), b("TB"), OP.add)
         decide(1, yy, b("LVW", 0, L))
     step(1, "F2", update1, later1)
-    send("V3D", b("DT1"), {"V3D": 2 * HOP + 0.4})
+    send("V3D", b("DT1"), {"V3D": 2 * HOP + VX})
 
     ts(b("UL", 0, 13), CS, float(OKB + S), OP.is_ge)
     ts(b("UU", 0, 5), b("PF", 224, 229), float(OKB + S), OP.is_ge)
@@ -719,26 +831,27 @@ def rank_program(g, core, T, topo):
     scat("OC", WT, "DT1", 13, b("LF1"))
     tt(b("OQ"), ind(b("OC"), b("DT0", 0, 13)), b("FM"), OP.is_equal)
     scan(b("BX", 0, L), b("RKM"), b("OQ"), OP.mult, OP.add)
-    scat("HT", WT, "DT1", 13, b("ZL1"))
+    scat("HT", WT, "DT1", 13, b("ZL1", 0, L))
     wrap("HT")
     mms(*[(b("PH", 288, 309), b("WMU", 15 - m, 143 - m), b("UF", m, 336, 16), m == 0, m == 15) for m in range(16)])
     tt(b("UU", 5, 26), b("PH", 288, 309), b("BX", 15, 336, 16), OP.is_ge)
     ts(b("BU", 0, 13), b("BX", 15, L, 16), 0.5, OP.is_lt)
     act(b("BP", 0, L), ind(b("T01"), b("BU", 0, 13)))
     lanes(2, 26, 416, b("QV"))
-    act(b("GW"), ind(b("LVW", 80, 1104), b("PL1", 0, 21)))
+    act(b("GW", 0, 336), ind(b("LVW", 80, 1104), b("PL1", 0, 21)))
     act(b("D", 0, 80), b("LVW", 0, 80))
     mms(*[(b3("T5", 0, 21), b("ID"), x, i == 0, i == 2)
-          for i, x in enumerate((b("D", 80, 416), b("GW"), b("BP", 0, 336)))])
+          for i, x in enumerate((b("D", 80, 416), b("GW", 0, 336), b("BP")))])
     act(b("D", 80, 416), b3("T5", 0, 21))
 
     def update2():
         scat("F3", WT, "V3D", 13, b("V3Z"))
         wrap("F3")
-        act(b("DF", 0, F), b("D"))
+        aff(b("TB"), b("TS"), -1.0 / KQ, 0.5 / KQ - BIG)
+        ts(b("PL2", 26, 34), b("FW", 26, 34), b("TB"), OP.add)
 
     def later2(yy):
-        decide(2, yy, b("W2"))
+        decide(2, yy, b("LVW", 0, L))
         tt(b("OQ"), ind(b("OC", 0, S + 16), b("IX", 0, 13)), b("M16"), OP.mult)
         scan(b("OX"), b("RKM"), b("OQ"), OP.mult, OP.add)
         occ = b("OX", 15, L, 16)
@@ -748,13 +861,16 @@ def rank_program(g, core, T, topo):
         ts(b("QI", 0, 13), b("Q1", 0, 13), 80.0, OP.add)
         tt(b("Q2", 0, 13), b("Q2", 0, 13), b("Q1", 0, 13), OP.add)
         ts(b("Q3", 0, 13), b("Q2", 0, 13), float(OKB + S + 80), OP.add)
-        act(b("VB"), ind(b("D"), b("QI", 0, 13)), AF.Identity, 1.0, const(1))
-        tt(b("ND"), b("DQ"), b("W2", 80, L), OP.add)
-        act(b("DF", 544, F), b("W2", 0, 80))
-        scat("DF", F, "LU2", 8, b("ND"))
+        act(b("VB"), ind(b("D"), b("QI", 0, 13)), AF.Copy, 1.0, 1.0)
+        act(b("GW"), ind(b("LVW", 80, 1104), b("PL2", 0, 34)))
+        act(b("DF", 544, F), b("LVW", 0, 80))
+        for x, lo, hi in (("T0", 0, 512), ("T1", 512, 544)):
+            out = b3(x, 0, (hi - lo) // 16)
+            mms((out, b("ID"), b("D", lo, hi), True, False), (out, b("ID"), b("GW", lo, hi), False, True))
+            act(b("DF", lo, hi), out)
     step(2, "F3", update2, later2)
 
-    scat("HT", WT, "DT2", 13, b("ZL2"))
+    scat("HT", WT, "DT2", 13, b("ZL2", 0, L))
     store("S", T.yt[:, :], b("HT", 0, S), "yt")
     tt(b("Q1", 0, 13), CS, b("Q3", 0, 13), OP.max)
     tt(b("Q2", 0, 13), b("Q1", 0, 13), b("DUQ", 0, 13), OP.min)

@@ -6,12 +6,12 @@ F32, BF, I32, U16 = "float32", "bfloat16", "int32", "uint16"
 F, L, S = 624, 208, 2048
 PAD = 32
 WT = S + PAD + 3 * L
-PEN = 65536
+PEN = 8192
 OKB = 8 * PEN
 NB = 128
 BIG = 1048576.0
 KQ = 1.0 / 65536
-LAG = 0.14
+LAG = 0.18
 PASSES = 6
 SPAN = []
 NODES = []
@@ -19,20 +19,28 @@ HOP = 1.4
 GA = 1.56
 KA0 = 6
 KR0 = [(4, 6), (14, 16)]
-KD = (0, 0, 1, 1)
-HFIRST = 0
-ECUT = [(0, 7), (7, 13)]
+KD = (1, 0, 2, 0)
+HFIRST = 1
+ECUT = [(0, 8), (8, 13)]
 TRIES = 6000
 RQX = 1.5
 LWA = ()
 PFX = 0.02
-SEED = 1
+SEED = 10
 SFIRST = 0
+MIX = (4, 4)
+NS = 4
+ECV = [(0, 8), (8, 13)]
+T0 = 0.15
+F3L = 23.0
+CF = 1.2
+SC = 3.8
+ONG = ("F2", "F3", "ZL1", "ZL2", "D", "DF")
 UX = 0.3
 VX = 0.4
 KX = 0.4
 AFX = 0.11
-ONV = ("TS", "LD", "HT", "F2", "F3", "TB")
+ONV = ("TS", "TB", "HT")
 EA = (2, 3, 5)
 ECA = [(0, 13)]
 CUT0 = 10
@@ -71,7 +79,7 @@ for _n, _s, _d in (
         ("YH", [288], F32), ("YF", [288], F32), ("YS", [192], I32), ("YT", [192], I32), ("KAB", [128], BF), ("IDN", [128], BF),
         ("LH0", [256], U16), ("LF0", [256], U16), ("LDH", [128], U16), ("LDF", [128], U16),
         ("GA0", [512], BF), ("GA1", [512], BF), ("GA2", [512], BF), ("GA3", [512], BF), ("GA4", [512], BF), ("GA5", [512], BF), ("CMH", [L, 16], BF), ("CMF", [L, 16], BF),
-        ("CDH", [256, 8], BF), ("CDF", [256, 8], BF), ("RK4", [184], BF), ("RKA", [160], BF), ("RKB", [112], BF), ("ZX1", [20, 16], BF), ("ZX2", [20, 16], BF),
+        ("CDH", [256, 8], BF), ("CDF", [256, 8], BF), ("RK4", [L], BF), ("RKA", [L], BF), ("ZX1", [80, 6], BF), ("ZX2", [80, 6], BF),
         ("RQZ", [L], BF), ("RQL", [256], U16), ("KFR", [16], F32), ("KFO", [16], F32),
         ("U2Z", [L], BF), ("U2D", [16], U16), ("V3Z", [L], BF), ("V3D", [16], U16),
         ("HS", [L], F32), ("FS", [424], F32), ("HKI", [16], I32), ("HSL", [16], I32), ("A1", [16], F32),
@@ -86,9 +94,9 @@ for _n, _s, _d in (
         ("PY", [1], F32), ("P2", [16], F32), ("P3", [16], F32), ("ML", [2], F32), ("MB", [16], F32), ("MC", [6], F32),
         ("KIO", [L], F32), ("M16", [L], F32), ("RKM", [L], BF), ("KAD", [L], F32), ("C16", [48], F32),
         ("FW", [48], F32), ("CF", [32], BF), ("CN", [32], BF), ("ONB", [128], BF), ("BA", [128], BF), ("BO", [128], BF), ("NBO", [128], BF),
-        ("NT", [128], BF), ("ID", [128], BF), ("IDF", [128], F32), ("WMU", [144], BF), ("BW", [1], BF),
-        ("CL", [264], F32), ("CI", [264], I32), ("CJ", [264], I32), ("CB", [264], F32),
-        ("LB", [256], BF), ("HB", [8], F32), ("CT", [S + 64], BF), ("FJ", [L], BF), ("BR", [L], BF), ("TH", [2], F32), ("TN", [2], F32), ("FM", [L], F32),
+        ("NT", [128], BF), ("ID", [128], BF), ("IDF", [128], F32), ("WMU", [144], BF), ("WMH", [144], BF), ("BW", [1], BF),
+        ("CT", [S + 64], BF), ("FJ", [416], BF), ("FJ2", [416], BF), ("FJ4", [320], BF),
+        ("TH", [2], F32), ("TN", [2], F32), ("FM", [L], F32),
         ("BX", [336], F32), ("BU", [16], U16),
         ("QV", [416], F32), ("QW", [416], F32), ("FQ", [F], F32), ("LM", [L], F32), ("ON32", [32], F32), ("TW", [32], F32), ("T01", [16], F32),
         ("RK", [16], I32), ("RC", [16], I32), ("RP", [16], I32), ("RX", [16], F32), ("RY", [16], F32), ("PC", [16], F32),
@@ -105,7 +113,7 @@ for _d, _w in _fill.items():
     SCRATCH["S" + _d] = ("sbuf", [128, _w], _d)
 for _n in range(6):
     SCRATCH["T%d" % _n] = ("psum", [128, 32, 16], F32)
-for _n in ("PH", "PF"):
+for _n in ("PH", "PF", "T0", "T1")[:NS - 2]:
     SCRATCH[_n] = ("psum", [128, 512], F32)
     PLACE[_n] = (_n, 0, 512)
 KINDS = [(13, 16), (5, 5), (8, 8)]
@@ -244,7 +252,7 @@ def rank_program(g, core, T, topo):
             for name, reg, psum in lst:
                 keep = [x for x in seen.get(name, []) if not (w and inside(x[0], reg) and not psum)]
                 seen[name] = keep + [(reg, w, k)]
-        nodes.append((e, run, dur, lat, sorted(before.items()), writes))
+        nodes.append((e, run, dur * CF, lat, sorted(before.items()), writes))
         return k
 
     def op(e, f, out, ins, after=None, done=1):
@@ -253,7 +261,7 @@ def rank_program(g, core, T, topo):
         if e == "G":
             dur = 0.15 + 2 * c
         elif out[3]:
-            dur = 0.05 + 3.8 * c
+            dur = 0.05 + SC * c
         elif win:
             dur = 0.06 + GA * 0.00085 * out[4]
         else:
@@ -340,7 +348,7 @@ def rank_program(g, core, T, topo):
             best = now = forwards([-x for x in tail])
             for i in range(TRIES):
                 other = turned(now[2]) if i % 50 < (4 if i < 50 else 1) else moved(now[2])
-                if other[0] - now[0] < -0.1 * 0.1 ** (i / TRIES) * math.log(1 - draw()):
+                if other[0] - now[0] < -T0 * 0.05 ** (i / TRIES) * math.log(1 - draw()):
                     now = other
                 best = min(best, now)
             SPAN.extend(best[1:])
@@ -360,7 +368,7 @@ def rank_program(g, core, T, topo):
             op("V", lambda q: q.tensor_scalar(A_(out), A_(a), A_(s1), A_(s2), o1, o2), out, [a, s1, s2])
 
     def cp(out, a):
-        op("V", lambda q: q.tensor_copy(A_(out), A_(a)), out, [a])
+        return op("V", lambda q: q.tensor_copy(A_(out), A_(a)), out, [a])
 
     def scan(out, d0, d1, o0, o1, first=0.0):
         op("V", lambda q: q.tensor_tensor_scan(A_(out), A_(d0), A_(d1), first, o0, o1), out, [d0, d1, 0])
@@ -368,13 +376,20 @@ def rank_program(g, core, T, topo):
     def ms(out, v):
         op("V", lambda q: q.memset(A_(out), v), out, [])
 
-    def tr(out, a):
-        op("V", lambda q: q.transpose(A_(out), A_(a)), out, [a])
+    def tr(out, a, behind):
+        return op("V", lambda q: q.transpose(A_(out), A_(a)), out, [a], behind, 0)
+
+    table = [None]
 
     def act(out, a, fn=AF.Copy, scale=1.0, bias=0.0):
+        if (fn, scale, bias) == (AF.Copy, 1.0, 0.0) and out[-1] in ONG and not a[3] and SCRATCH[a[1]][0] == "sbuf":
+            return asel(out, a, [[0, out[4]]], OP.is_ge, 0, 0)
         if fn in (AF.Copy, AF.Identity) and out[-1] in ONV and not a[3]:
             return cp(out, a) if (scale, bias) == (1.0, 0.0) else ts(out, a, scale, OP.mult, bias, OP.add)
-        op("A", lambda q: q.activation(A_(out), A_(a), fn, bias=A_(bias), scale=A_(scale)), out, [a, scale, bias])
+        k = op("A", lambda q: q.activation(A_(out), A_(a), fn, bias=A_(bias), scale=A_(scale)), out, [a, scale, bias],
+               table[0] if a[3] else None, 0)
+        if out[1] == "RKM":
+            table[0] = k
 
     tiles = {}
 
@@ -391,7 +406,7 @@ def rank_program(g, core, T, topo):
         if len(m) > 4:
             return [mms(*m[i:i + 4]) for i in range(0, len(m), 4)]
         node("P", lambda: [mm_now(*x) for x in m], regions([x[1] for x in m] + [x[2] for x in m]), regions([x[0] for x in m]),
-             sum(PFX + PEC * max(64, x[0][4]) * (4 if SCRATCH[x[1][1]][2] == F32 else 1) for x in m))
+             sum(PFX + PEC * max(min(64, x[1][4]), x[0][4]) * (4 if SCRATCH[x[1][1]][2] == F32 else 1) for x in m))
 
     def iota(out, pat, base, cm, after=None):
         if SCRATCH[out[1]][2] == I32:
@@ -399,8 +414,8 @@ def rank_program(g, core, T, topo):
         else:
             op("G", lambda q: q.iota(A_(out), pat, base, cm, allow_small_or_imprecise_dtypes=True), out, [], after)
 
-    def asel(out, a, pat, o, base, cm):
-        op("G", lambda q: q.affine_select(A_(out), A_(a), pat, o, 0.0, base, cm), out, [a])
+    def asel(out, a, pat, o, base, cm, after=None):
+        op("G", lambda q: q.affine_select(A_(out), A_(a), pat, o, 0.0, base, cm), out, [a], after, 0)
 
     def scat(win, width, off, n, val):
         cp(ind(b(win, 0, width), b(off, 0, n)), val)
@@ -464,7 +479,9 @@ def rank_program(g, core, T, topo):
     iota(b("PC"), [[0, 8], [1, 2]], 0, 0)
     iota(b("KIO"), [[0, 13], [1, 16]], 0, 0)
     asel(b("ID"), b("ONB"), [[-1, 128]], OP.is_equal, 0, 1)
-    asel(b("BA"), b("ONB"), [[-16, 8], [0, 16]], OP.is_ge, 0, 1)
+    z0 = b("ZF", 80, 288)
+    first = send("RQZ", z0, {"RQZ": 2 * HOP + 1.5, "U2Z": 2 * HOP + 4.0})
+    asel(b("BA"), b("ONB"), [[-16, 8], [0, 16]], OP.is_ge, 0, 1, first)
     asel(b("BO"), b("BA"), [[16, 8], [0, 16]], OP.is_ge, 15, -1)
     ts(b("PJ"), b("PI"), 15, OP.bitwise_and)
     ts(b("PK"), b("PI"), 4, OP.arith_shift_right, 1, OP.bitwise_and)
@@ -489,8 +506,8 @@ def rank_program(g, core, T, topo):
     act(b("IDF"), b("ID"))
     ts(b("PY"), b("PM"), -1.0, OP.add)
     act(b("IDN"), b("ID"), scale=b("PY"))
-    aff(b("KAD"), b("KIO"), -4096.0, 61440)
-    act(b("KAB"), b("KAD", 0, 128))
+    act(b("WMH"), b("WMU"), scale=16.0)
+    aff(b("KAD"), b("KIO"), -4096.0, OKB + 61440)
     ts(b("M16"), b("KIO"), b("PM"), OP.is_equal)
 
     tt(b("PX"), b("PJ"), b("PK"), OP.add)
@@ -521,22 +538,39 @@ def rank_program(g, core, T, topo):
             ts(r, b("PX"), off, OP.mult, r, OP.add)
             ts(b("RO%d" % x, 0, s), b("C16", 0, s), 1.0 / s, OP.mult, r, OP.add)
         r = b("RZ%d" % x, 0, nc)
+        if s == 8:
+            iota(r, [[8, 2], [1, 2], [64, 2]], 0, 0)
+            ts(b("RC", 8, 9), b("PJ"), 2, OP.arith_shift_right)
+            tt(b("RC", 9, 10), b("RC", 8, 9), b("PK"), OP.add)
+            ts(b("RC", 9, 10), b("RC", 9, 10), 1, OP.bitwise_and)
+            ts(b("RY", 8, 9), b("RC", 8, 9), 8.0, OP.mult, b("PM"), OP.add)
+            ts(b("RY", 8, 9), b("RY", 8, 9), b("PM"), OP.add)
+            ts(b("RY", 8, 9), b("RC", 9, 10), off, OP.mult, b("RY", 8, 9), OP.add)
+            return ts(b("RQ%d" % x, 0, nc), r, b("RY", 8, 9), OP.add)
         aff(r, b("PC", 0, nc), off, b("PM"))
         tt(r, r, b("C16", 0, nc), OP.add)
         cp(b("RQ%d" % x, 0, nc), r)
 
-    def lists(x, src, lo, y, out, key=None):
+    def lists(x, src, lo, y, out, key=None, behind=None):
         nc, s = KINDS[x]
         n1, n2 = 32 * ((nc + 1) // 2), 32 * (nc // 2 + 1)
-        tr(b(y, 0, n1), b(src, lo, lo + n1))
-        tr(b(y, n1, n1 + n2), b(src, lo - 16, lo - 16 + n2))
-        cp(b(out, 0, 16 * s), ind(b(y, 0, n1 + n2), b("RO%d" % x, 0, s)))
+        tr(b(y, 0, n1), b(src, lo, lo + n1), behind)
+        tr(b(y, n1, n1 + n2), b(src, lo - 16, lo - 16 + n2), behind)
+        row[1] = cp(b(out, 0, 16 * s), ind(b(y, 0, n1 + n2), b("RO%d" % x, 0, s)))
         if key and x == 2:
             act(key, ind(b(y, 0, n1 + n2), b("RQ%d" % x, 0, nc)))
         elif key:
             tt(key, ind(b(y, 0, n1 + n2), b("RQ%d" % x, 0, nc)), b("KAD", 0, 16 * nc), OP.add)
 
-    bank, row = [0], [None]
+    bank, row = [0, 0, 0], [None, None]
+
+    def free_bank(n):
+        bank[0] += 1
+        bank[1 + (n == 6)] += 1
+        return "T%d" % (bank[0] % 6 if NS == 4 else bank[2] % 2 if n == 6 else 2 + bank[1] % 4)
+
+    def cols(t, n, lo=0, step=1):
+        return b(t, lo, n, step) if t in PLACE else b3(t, 0, n // 16, lo, 16, step=step)
 
     def look(x, win, lst, z, cm, c0, chunks, k1, wide=None):
         nc, s = KINDS[x]
@@ -546,30 +580,28 @@ def rank_program(g, core, T, topo):
                         row[0] if j or x else None)
         for k0, k in chunks:
             n = k - k0
-            ga, t = "GA%d" % (bank[0] % 6), "T%d" % (bank[0] % 6)
-            bank[0] += 1
+            ga, t = "GA%d" % (bank[0] % 6), free_bank(n)
             if s == nc:
                 act(b(ga, 0, 16 * s * n), ind(win, b(lst, s * k0, s * k)), scale=-1.0)
             m = []
             for j in range(n):
-                o, got = b3(t, 0, nc * n, j, 16, step=n), b(ga, 16 * nc * j, 16 * nc * (j + 1))
+                o, got = cols(t, 16 * nc * n, j, n), b(ga, 16 * nc * j, 16 * nc * (j + 1))
                 if s != nc:
                     act(got, ind(win, b(lst, s * (k0 + j), s * (k0 + j) + nc)), scale=-1.0)
                 m += [(o, b("ID"), got, False, j == n - 1)] if wide else [(o, b("ID"), z, True, False), (o, b("ID"), got, False, True)]
             if wide:
-                mms((b3(t, 0, nc * n), b("ID"), wide, True, False))
+                mms((cols(t, 16 * nc * n), b("ID"), b3(wide, 0, 16 * nc, 0, n), True, False))
             mms(*m)
-            act(b3(cm, 16 * c0, 16 * (c0 + nc), k0, k), b3(t, 0, nc * n), AF.Sigmoid, 400.0, 200.0)
+            act(b3(cm, 16 * c0, 16 * (c0 + nc), k0, k), cols(t, 16 * nc * n), AF.Sigmoid, 400.0, 200.0)
 
-    def look2(win, lst, z, cm, na):
-        for j in range(8):
+    def look2(win, lst, z, cm, na, j0=0, j1=8):
+        for j in range(j0, j1):
             out = (T[cm][:, :, j], cm, (0, 256, j, j + 1), None, 256)
             got = ind(win, b(lst, 16 * j, 16 * j + 16))
             if j < 8 - na:
                 row[0] = tt(out, got, z, OP.is_le, row[0])
                 continue
-            ga, t = b("GA%d" % (bank[0] % 6), 0, 256), b3("T%d" % (bank[0] % 6), 0, 16)
-            bank[0] += 1
+            ga, t = b("GA%d" % (bank[0] % 6), 0, 256), cols(free_bank(1), 256)
             act(ga, got, scale=-1.0)
             mms((t, b("ID"), z, True, False))
             mms((t, b("ID"), ga, False, True))
@@ -578,7 +610,7 @@ def rank_program(g, core, T, topo):
     def sums2(key):
         out = b("PH", 80, L)
         mms((out, b("IDF"), key, True, False), (out, b("ID"), b("KAB"), False, False))
-        mms(*[(b("PH", 80 + h, L, 2), b("WMU", 15 - m, 143 - m), b3("CDH", 128 * h + m, 128 * h + 128, 0, 8, cs=16), False, h + m == 16)
+        mms(*[(b("PH", 80 + 64 * h, 144 + 64 * h), b("WMH", 15 - m, 143 - m), b3("CDH", m, 256, 4 * h, 4 * h + 4, cs=16), False, h + m == 16)
               for h in (0, 1) for m in range(16)])
 
     def far_sums(cm, r0, r1, k0, k1, bank, lo):
@@ -593,7 +625,7 @@ def rank_program(g, core, T, topo):
         mms((out, b("IDF"), key, True, False))
         if c0:
             mms((out, b("ID"), b("KAB"), False, False))
-        mms(*[(out, b("WMU", 15 - m, 143 - m), b3(cm, 16 * c0 + m, 16 * c1, cs=16), False, m == 15) for m in range(16)])
+        mms(*[(out, b("WMH", 15 - m, 143 - m), b3(cm, 16 * c0 + m, 16 * c1, cs=16), False, m == 15) for m in range(16)])
 
     def far_max(c0, c1, k0, k1, bank, lo, out, other):
         n = k1 - k0
@@ -603,33 +635,42 @@ def rank_program(g, core, T, topo):
         scan(b("FS", lo, hi), b("RKM" if n == 16 else "RK8", 0, hi - lo), b(bank, lo, hi), OP.mult, OP.max)
         tt(out, b("FS", lo + n - 1, hi, n), other, OP.max)
 
-    def home_max():
-        top = b("HS", 15, L, 16)
-        scan(b("HS"), b("RKM"), b("PH", 0, L), OP.mult, OP.max)
-        cp(b("HKI", 0, 13), top)
-        ts(b("HSL", 0, 13), b("HKI", 0, 13), S - 1, OP.bitwise_and)
-        ts(b("WI", 0, 13), b("HKI", 0, 13), 31 * PEN, OP.bitwise_and)
-        ts(b("AP", 0, 13), b("HSL", 0, 13), float(OKB), OP.add)
-        tt(b("AP", 0, 13), b("AP", 0, 13), b("WI", 0, 13), OP.max)
+    def home_max(t):
+        scan(b("HS"), b("RK4" if t else "RKM"), b("PH", 0, L), OP.mult, OP.max)
+        if t:
+            tt(b("A1"), b("HS", 83, 144, 4), b("HS", 147, L, 4), OP.max)
+            cp(b("HKI", 0, 5), b("HS", 15, 80, 16))
+            tt(b("HKI", 5, 13), b("A1", 0, 8), b("A1", 8, 16), OP.max)
+        else:
+            cp(b("HKI", 0, 13), b("HS", 15, L, 16))
+        ts(b("HSL", 0, 13), b("HKI", 0, 13), OKB + S - 1, OP.bitwise_and)
+        ts(b("WI", 0, 13), b("HKI", 0, 13), 4, OP.arith_shift_right, 31 * PEN, OP.bitwise_and)
+        tt(b("AP", 0, 13), b("HSL", 0, 13), b("WI", 0, 13), OP.max)
 
     CS = b("PF", 224, 237)
 
     def decide(t, yy, grown):
         ts(b("IX", 0, 13), yy, float(OKB + S), OP.min, float(OKB), OP.subtract)
-        tt(b("BR"), ind(b("CT", 0, S + 16), b("IX", 0, 13)), b("FJ"), OP.add)
-        ts(b("B0"), b("BR"), b("MH0"), OP.mult)
-        act(b("B1"), b("BR"), scale=b("MH1"))
+        ts(b("B0"), ind(b("CT", 0, S + 16), b("IX", 0, 13)), b("MH0"), OP.mult)
+        act(b("B1"), ind(b("CT", 0, S + 16), b("IX", 0, 13)), scale=b("MH1"))
         for a in (0, 2, 1, 3):
             pp = (32 * a, 32 * a + 32)
+            mms((cols("T%d" % a, 2 * L), b("FJ", 0, NB, p=pp), b("FJ2" if a > NS - 5 else "FJ", 0, 2 * L, p=pp), True, False, a))
             for x in (0, 1):
-                mms((b3("T%d" % a, x, 26, cs=2), b("B%d" % x, 0, NB, p=pp), b("BR", p=pp), True, True, a))
+                out = b3("T%d" % a, x, 26, cs=2) if a > NS - 5 else b("T%d" % a, L * x, L * x + L)
+                mms((out, b("B%d" % x, 0, NB, p=pp), b("B%d" % x, p=pp), False, x == 1, a))
+        for h in (0, 1):
+            pp = (64 * h, 64 * h + 32)
+            mms((b3("T%d" % (4 + h), 0, 20, p=(0, 80)), b("FJ", NB, L, p=pp), b("FJ4", p=pp), True, False, 2 * h))
         for a in (0, 2, 1, 3):
             pp = (32 * a, 32 * a + 32)
             mms(*[(b3("T%d" % (4 + a // 2), 2 * (a % 2) + x, 20, cs=4, p=(0, 80)), b("B%d" % x, NB, L, p=pp),
-                   b("BR", NB, L, p=pp), True, True, a) for x in (0, 1)])
+                   b("B%d" % x, NB, L, p=pp), False, a % 2 + x == 2, a) for x in (0, 1)])
 
         def over(a, c0, c1):
-            if a < 4:
+            if a < NS - 4:
+                out, src, x, pp = b3("E0", 0, 13, 32 * a + 16 * c0, 32 * a + 16 * c1), b("T%d" % a, L * c0, L * c1), 0, (0, NB)
+            elif a < 4:
                 out, src, x, pp = b3("E0", c0, c1, 32 * a, 32 * a + 32), b3("T%d" % a, 2 * c0, 2 * c1), 0, (0, NB)
             else:
                 pp = (0, L - NB)
@@ -640,16 +681,13 @@ def rank_program(g, core, T, topo):
                 ts(out, src, b("TH", x, x + 1, p=pp), OP.is_gt)
         mms((CS, b("IDF"), yy, True, False))
         for a in range(4):
-            for c0, c1 in ECA if a in EA else ECUT:
+            for c0, c1 in ECA if a in EA else ((0, 1), (1, 2)) if NS == 6 else ECV:
                 over(a, c0, c1)
         over(4, 0, 5)
         over(5, 0, 5)
-        for i, (c0, c1) in enumerate(ECUT):
-            if i == ORD:
-                mms(*[(b("PF", 224 + c, 225 + c), b2("E1", c - 8, 0, 128, p=(0, 80)), b("BW", p=(0, 80)), False, False) for c in range(8, 13)])
-            mms(*[(b("PF", 224 + c, 225 + c), b2("E0", c, 0, 128), b("BW"), False, c == 12 and ORD < 2) for c in range(c0, c1)])
-        if ORD == 2:
-            mms(*[(b("PF", 224 + c, 225 + c), b2("E1", c - 8, 0, 128, p=(0, 80)), b("BW", p=(0, 80)), False, c == 12) for c in range(8, 13)])
+        for c0, c1 in ECUT:
+            mms(*[(b("PF", 224 + c, 225 + c), b2("E0", c, 0, 128), b("BW"), False, False) for c in range(c0, c1)])
+        mms(*[(b("PF", 224 + c, 225 + c), b2("E1", c - 8, 0, 128, p=(0, 80)), b("BW", p=(0, 80)), False, c == 12) for c in range(8, 13)])
         ts(b("WU", 0, 13), yy, float(OKB + S), OP.max, 1.0 / PEN, OP.mult)
         act(grown, ind(b("TW"), b("WU", 0, 13)))
         tt(b("DS", 0, 13), CS, b("DU%d" % t, 0, 13), OP.min)
@@ -680,7 +718,7 @@ def rank_program(g, core, T, topo):
     def step(t, ftab, update, later):
         lu, zl = b("LU%d" % t, 0, 8), "ZL%d" % t
         home, far = b("HT", 0, S + PAD), b(ftab, 0, S + PAD)
-        look(1, b("HT", 0, S), "LSH%d" % t, b(zl, 0, 80), "CMH", 0, *pairs(16, 4), b3("ZX%d" % t, 0, 20))
+        look(1, b("HT", 0, S), "LSH%d" % t, b(zl, 0, 80), "CMH", 0, *pairs(16, NS), "ZX%d" % t)
         act(b("DQ"), ind(b("D"), lu))
         act(b(zl, 80, L), ind(b("ZF"), lu))
         act(b(zl, L, 336), b(zl, 80, L))
@@ -691,11 +729,13 @@ def rank_program(g, core, T, topo):
         act(b("LF%d" % t, 80, L), ind(b("FQ"), lu))
         update()
         sums("CMH", 0, 5, b("KA%d" % t, 0, 80))
-        look2(home, "LDH", b(zl, 80, 336), "CDH", KD[2 * t - 2])
-        look(1, b(ftab, 0, S), "LSF%d" % t, b(zl, 0, 80), "CMF", 0, *pairs(16, 4), b3("ZX%d" % t, 0, 20))
+        look2(home, "LDH", b(zl, 80, 336), "CDH", KD[2 * t - 2], 0, MIX[0])
+        look2(far, "LDF", b(zl, 80, 336), "CDF", KD[2 * t - 1], 0, MIX[1])
+        look2(home, "LDH", b(zl, 80, 336), "CDH", KD[2 * t - 2], MIX[0])
+        look(1, b(ftab, 0, S), "LSF%d" % t, b(zl, 0, 80), "CMF", 0, *pairs(16, NS), "ZX%d" % t)
         sums2(b("KA%d" % t, 80, L))
-        look2(far, "LDF", b(zl, 80, 336), "CDF", KD[2 * t - 1])
-        home_max()
+        look2(far, "LDF", b(zl, 80, 336), "CDF", KD[2 * t - 1], MIX[1])
+        home_max(t)
         if SFIRST:
             far_sums("CMF", 0, 80, 0, 16, "PF", 0)
         far_sums("CDF", 0, 256, 0, 4, "PF", 80)
@@ -705,16 +745,16 @@ def rank_program(g, core, T, topo):
         scan(b("FS", 0, 144), b("RK4", 0, 144), b("PF", 0, 144), OP.mult, OP.max)
         scan(b("FS", 320, 384), b("RK4", 80, 144), b("PH", 320, 384), OP.mult, OP.max)
         tt(b("YY", 0, 5), b("FS", 15, 80, 16), b("AP", 0, 5), OP.max)
-        for lo in (80, 112, 320, 352):
-            tt(b("AP" if lo < 352 else "YY", 5, 13), b("FS", lo + 3, lo + 32, 4), b("AP", 5, 13), OP.max)
+        tt(b("QQ", 0, 8), b("FS", 83, 112, 4), b("FS", 115, 144, 4), OP.max)
+        tt(b("QQ", 8, 16), b("FS", 323, 352, 4), b("FS", 355, 384, 4), OP.max)
+        tt(b("AP", 5, 13), b("QQ", 0, 8), b("AP", 5, 13), OP.max)
+        tt(b("YY", 5, 13), b("QQ", 8, 16), b("AP", 5, 13), OP.max)
         later(b("YY", 0, 13))
 
-    z0 = b("ZF", 80, 288)
-    send("RQZ", z0, {"RQZ": 2 * HOP + 1.5, "U2Z": 2 * HOP + 4.0})
     places(0)
     lists(0, "EF", 96, "YA", "LF0")
     asked = send("RQL", b("LF0"), {"RQL": 2 * HOP + RQX})
-    lists(0, "EH", 96, "YB", "LH0", b("KA0"))
+    lists(0, "EH", 96, "YB", "LH0", b("KA0"), row[1] - 1)
     k = load("S", b("ZF", 0, 80), T.zf[:, 544:F], "zf1", asked, b("LH0"))
     k = load("S", b("EH", 16, 96), T.eh[:, 544:F], "eh1", k)
     k = load("S", b("EF", 16, 96), T.ef[:, 544:F], "ef1", k)
@@ -723,7 +763,7 @@ def rank_program(g, core, T, topo):
     k = load("S", b("ZF", 288, F), T.zf[:, L:544], "zf2", k)
     send("F2", b("HT", 0, S), {"F2": 16.0})
     asel(b("NT"), b("NBO"), [[-1, 128]], OP.is_gt, 0, 1)
-    iota(b("FJ"), [[1, L]], 48, 0, asked)
+    iota(b("FJ"), [[0, 2], [1, L]], 48, 0, asked)
     iota(b("TH"), [[NB, 2]], 48, 1, asked)
     iota(b("TW"), [[1, 32]], 0, 0)
     for x in range(0, WT, 676):
@@ -733,24 +773,24 @@ def rank_program(g, core, T, topo):
     look(0, tab, "RQL", b("RQZ"), "CMF", 0, KR0, [k for k in range(16) if not any(x <= k < y for x, y in KR0)])
     ms(b("KFO"), 0.0)
     act(b("RK4", 0, 80), b("RKM", 0, 80))
-    for lo in (80, 132):
-        act(b("RK4", lo, lo + 52), b("RKM", 0, L, 4))
+    iota(b("RK4", 80, L), [[0, 32], [1, 4]], 0, 0, asked)
+    act(b("RK4", 80, L), b("RK4", 80, L), AF.Sign)
+    for h in (0, 1):
+        iota(b("KAB", 64 * h, 64 * h + 64), [[-4096, 2], [0, 8], [-8192, 4]], OKB + 61440 - 32768 * h, 0, asked)
     if HFIRST:
         sums("CMH", 0, 13, b("KA0"))
     w = CUT0
     iota(b("RKA", 0, 13 * w), [[0, 13], [1, w]], 0, 0, asked)
-    iota(b("RKB", 0, 13 * (16 - w)), [[0, 13], [1, 16 - w]], 0, 0, asked)
-    for x, n_ in (("RKA", 13 * w), ("RKB", 13 * (16 - w))):
-        act(b(x, 0, n_), b(x, 0, n_), AF.Sign)
+    iota(b("RKA", 13 * w, L), [[0, 13], [1, 16 - w]], 0, 0, asked)
+    act(b("RKA"), b("RKA"), AF.Sign)
     far_sums("CMF", 0, L, 0, w, "PF", 0)
-    far_sums("CMF", 0, L, w, 16, "PH", 320)
-    scan(b("FS", 0, 13 * w), b("RKA", 0, 13 * w), b("PF", 0, 13 * w), OP.mult, OP.max)
-    scan(b("FS", 320, 528 - 13 * w), b("RKB", 0, 208 - 13 * w), b("PH", 320, 528 - 13 * w), OP.mult, OP.max)
-    tt(b("KFO", 0, 13), b("FS", w - 1, 13 * w, w), b("FS", 335 - w, 528 - 13 * w, 16 - w), OP.max)
+    far_sums("CMF", 0, L, w, 16, "PF", 13 * w)
+    scan(b("FS", 0, L), b("RKA"), b("PF", 0, L), OP.mult, OP.max)
+    tt(b("KFO", 0, 13), b("FS", w - 1, 13 * w, w), b("FS", 12 * w + 15, L, 16 - w), OP.max)
     if not HFIRST:
         sums("CMH", 0, 13, b("KA0"))
     told = send("KFR", b("KFO"), {"KFR": 2 * HOP + KX})
-    home_max()
+    home_max(0)
     fill(b("ON32"), 1, asked)
     ts(b("CT", 0, 1), b("PM"), 11.0, OP.is_lt, -1.0, OP.mult)
     act(b("M2"), b("M16", 0, 16), scale=2.0)
@@ -759,8 +799,11 @@ def rank_program(g, core, T, topo):
         for lo in range(0, 1 << j, 512):
             hi = min(1 << j, lo + 512)
             ts(b("CT", (1 << j) + lo, (1 << j) + hi), b("CT", lo, hi), b("M2", j, j + 1), OP.add)
-    act(b("MC", 0, 1), b("M2", 11, 12), scale=1.0 / 512)
-    act(b("FJ"), b("FJ"), scale=b("MC", 0, 1))
+    ts(b("MC", 0, 1), b("M2", 11, 12), b("MH0"), OP.mult, 1.0 / 512, OP.mult)
+    iota(b("FJ2"), [[16, 13], [0, 2], [1, 16]], 48, 0, asked)
+    iota(b("FJ4"), [[16, 5], [0, 4], [1, 16]], NB + 48, 0, asked)
+    for x in ("FJ", "FJ2", "FJ4"):
+        act(b(x), b(x), scale=b("MC", 0, 1))
     aff(b("TN"), b("TH"), 1.0 / 65536, 0.5 / 65536)
     tt(b("TN"), b("TN"), b("TH"), OP.mult)
     aff(b("TH"), b("TN"), 1.0, 11)
@@ -799,8 +842,8 @@ def rank_program(g, core, T, topo):
         lists(1, "EH", 16 + q0, "YS", "LSH%d" % t, b("KA%d" % t, 0, 80))
         lists(1, "EF", 16 + q0, "YT", "LSF%d" % t)
         act(b("ZL%d" % t, 0, 80), b("ZF", q0, q0 + 80))
-        for j in range(4):
-            act(b3("ZX%d" % t, 0, 20, j, 16, step=4), b("ZF", q0, q0 + 80))
+        for j in range(NS):
+            act((T["ZX%d" % t][:, :, j], "ZX%d" % t, (0, 80, j, j + 1), None, 80, "ZX%d" % t), b("ZF", q0, q0 + 80))
     tt(b("YY", 0, 13), b("AP", 0, 13), b("KFR", 0, 13), OP.max)
     decide(0, b("YY", 0, 13), b("D", 80, 288))
     send("U2D", b("DT0"), {"U2D": HOP + UX})
@@ -808,7 +851,7 @@ def rank_program(g, core, T, topo):
     ts(b("UU", 0, 13), CS, float(OKB + S), OP.is_ge)
     scat("HT", WT, "DT0", 13, z0)
     wrap("HT")
-    send("F3", b("HT", 0, S), {"F3": 17.0})
+    send("F3", b("HT", 0, S), {"F3": F3L})
     lanes(1, 13, 288, b("QV", 80, 288))
     aff(b("TB"), b("TS"), -1.0 / KQ, 80 - BIG + 0.5 / KQ)
 
@@ -865,7 +908,7 @@ def rank_program(g, core, T, topo):
         act(b("GW"), ind(b("LVW", 80, 1104), b("PL2", 0, 34)))
         act(b("DF", 544, F), b("LVW", 0, 80))
         for x, lo, hi in (("T0", 0, 512), ("T1", 512, 544)):
-            out = b3(x, 0, (hi - lo) // 16)
+            out = cols(x, hi - lo)
             mms((out, b("ID"), b("D", lo, hi), True, False), (out, b("ID"), b("GW", lo, hi), False, True))
             act(b("DF", lo, hi), out)
     step(2, "F3", update2, later2)
@@ -881,6 +924,6 @@ def rank_program(g, core, T, topo):
     store("S", T.yd[:, 0:544], (T.DF[0:128:16, 80:F], "DF", (0, 1, 80, F), None, 544), "yd")
     store("A", T.yd[:, 544:F], (T.DF[0:128:16, 0:80], "DF", (0, 1, 0, 80), None, 80), "ye")
     issue()
-    for s in SEMAPHORES:
+    for s in sorted(SEMAPHORES, key=lambda x: (x[:2] == "o_", x[0] == "q")):
         if s in cnt and know["G"].get(s, 0) < cnt[s]:
             g.wait_ge(T.sem[s], cnt[s])

import math
from concourse.mybir import AluOpType, ActivationFunctionType
OP = AluOpType
AF = ActivationFunctionType
F32, BF, I32, U16 = "float32", "bfloat16", "int32", "uint16"
F, L, S = 624, 208, 2048
PAD = 32
WT = S + PAD + 3 * L
PEN = 8192
OKB = 8 * PEN
NB = 128
BIG = 1048576.0
KQ = 1.0 / 65536
LAG = 0.18
PASSES = 6
SPAN = []
NODES = []
HOP = 1.4
GA = 1.56
KA0 = 6
KR0 = [(4, 6), (14, 16)]
KD = (1, 0, 2, 0)
HFIRST = 1
ECUT = [(0, 8), (8, 13)]
TRIES = 6000
RQX = 1.5
LWA = ()
PFX = 0.02
SEED = 10
SFIRST = 0
MIX = (4, 4)
NS = 4
ECV = [(0, 8), (8, 13)]
T0 = 0.15
F3L = 23.0
CF = 1.2
SC = 3.8
ONG = ("F2", "F3", "ZL1", "ZL2", "D", "DF")
UX = 0.3
VX = 0.4
KX = 0.4
AFX = 0.11
ONV = ("TS", "TB", "HT")
EA = (2, 3, 5)
ECA = [(0, 13)]
CUT0 = 10
PEC = 0.00045
ORD = 2

ENG = "VAPG"
LOADS = ["ef0", "eh0", "zf0", "tab", "ef1", "eh1", "zf1", "ef2", "eh2", "zf2"]
MSGS = ["RQZ", "RQL", "KFR", "F2", "F3", "U2Z", "U2D", "V3Z", "V3D"]
TO = {"RQZ": 1, "RQL": 1, "KFR": -1, "F2": -2, "U2Z": -2, "U2D": -2, "F3": -3, "V3Z": -3, "V3D": -3}
SMALL = [("RQZ", "RQZ"), ("RQL", "RQL"), ("RQZ", "U2Z"), ("KFR", "KFR"), ("V3Z", "V3Z"), ("V3D", "V3D")]
TABLES = ("F2", "F3")
PARTS = 4
STORES = ["yt", "yo", "yd", "ye"]
SEMAPHORES = (["q" + e for e in ENG] + ["d_" + n for n in LOADS] + ["o_" + n for n in STORES]
              + ["a_" + n for n in MSGS] + ["l_" + n for n in MSGS] + ["p_%s%d" % (n, i) for n in TABLES for i in range(PARTS)])

SCRATCH = {}
PLACE = {}
_fill = {F32: 0, BF: 0, I32: 0, U16: 0}


def _sb(name, shape, dtype):
    if len(shape) == 1 and shape[0] <= 48 and name not in MSGS + ["KFO", "DT0", "DT1"]:
        PLACE[name] = ("S" + dtype, _fill[dtype], shape[0])
        _fill[dtype] += -(-shape[0] // 16) * 16
        return
    SCRATCH[name] = ("sbuf", [128] + shape, dtype)
    PLACE[name] = (name, 0, shape[0])


for _n, _s, _d in (
        ("HT", [WT], BF), ("F2", [WT], BF), ("F3", [WT], BF), ("OC", [WT], F32),
        ("ZF", [F], BF), ("EH", [F + 32], I32), ("EF", [F + 32], I32), ("YA", [448], I32), ("YB", [448], I32),
        ("D", [F], BF), ("DF", [F + L], F32), ("XH", [160], F32), ("XF", [160], F32), ("DQ", [128], F32),
        ("YH", [288], F32), ("YF", [288], F32), ("YS", [192], I32), ("YT", [192], I32), ("KAB", [128], BF), ("IDN", [128], BF),
        ("LH0", [256], U16), ("LF0", [256], U16), ("LDH", [128], U16), ("LDF", [128], U16),
        ("GA0", [512], BF), ("GA1", [512], BF), ("GA2", [512], BF), ("GA3", [512], BF), ("GA4", [512], BF), ("GA5", [512], BF), ("CMH", [L, 16], BF), ("CMF", [L, 16], BF),
        ("CDH", [256, 8], BF), ("CDF", [256, 8], BF), ("RK4", [L], BF), ("RKA", [L], BF), ("ZX1", [80, 6], BF), ("ZX2", [80, 6], BF),
        ("RQZ", [L], BF), ("RQL", [256], U16), ("KFR", [16], F32), ("KFO", [16], F32),
        ("U2Z", [L], BF), ("U2D", [16], U16), ("V3Z", [L], BF), ("V3D", [16], U16),
        ("HS", [L], F32), ("FS", [424], F32), ("HKI", [16], I32), ("HSL", [16], I32), ("A1", [16], F32),
        ("AP", [16], F32), ("YY", [16], F32), ("IX", [16], U16), ("WI", [16], I32), ("WU", [16], U16), ("UL", [16], U16),
        ("DS", [16], F32), ("B0", [L], BF), ("B1", [L], BF), ("E0", [13, 128], BF), ("E1", [5, 128], BF),
        ("NU", [32], BF), ("UU", [48], BF), ("UC", [32], BF), ("QQ", [32], F32), ("TB", [1], F32),
        ("LD", [128], F32), ("XS", [128], F32), ("LVF", [1104], BF), ("LVW", [1104], BF), ("UF", [512], BF),
        ("GW", [544], BF), ("BP", [336], BF), ("OQ", [L], F32), ("OX", [L], F32),
        ("VB", [L], F32), ("Q1", [16], F32), ("Q2", [16], F32), ("Q3", [16], F32), ("QI", [16], U16), ("BL", [16], U16),
        ("DUQ", [16], F32),
        ("PI", [1], I32), ("PJ", [1], I32), ("PK", [1], I32), ("PM", [1], F32), ("MH0", [1], F32), ("MH1", [1], F32),
        ("PY", [1], F32), ("P2", [16], F32), ("P3", [16], F32), ("ML", [2], F32), ("MB", [16], F32), ("MC", [6], F32),
        ("KIO", [L], F32), ("M16", [L], F32), ("RKM", [L], BF), ("KAD", [L], F32), ("C16", [48], F32),
        ("FW", [48], F32), ("CF", [32], BF), ("CN", [32], BF), ("ONB", [128], BF), ("BA", [128], BF), ("BO", [128], BF), ("NBO", [128], BF),
        ("NT", [128], BF), ("ID", [128], BF), ("IDF", [128], F32), ("WMU", [144], BF), ("WMH", [144], BF), ("BW", [1], BF),
        ("CT", [S + 64], BF), ("FJ", [416], BF), ("FJ2", [416], BF), ("FJ4", [320], BF),
        ("TH", [2], F32), ("TN", [2], F32), ("FM", [L], F32),
        ("BX", [336], F32), ("BU", [16], U16),
        ("QV", [416], F32), ("QW", [416], F32), ("FQ", [F], F32), ("LM", [L], F32), ("ON32", [32], F32), ("TW", [32], F32), ("T01", [16], F32),
        ("RK", [16], I32), ("RC", [16], I32), ("RP", [16], I32), ("RX", [16], F32), ("RY", [16], F32), ("PC", [16], F32),
        ("PX", [1], I32), ("RB", [3], F32), ("RZ0", [16], F32), ("RZ1", [16], F32), ("RZ2", [16], F32), ("M2", [16], BF), ("TS", [1], F32),
):
    _sb(_n, _s, _d)
for _t in range(3):
    for _n, _s, _d in (("KA", [L], F32), ("ZL", [336], BF), ("DU", [16], F32), ("DT", [16], U16), ("LW", [1024], F32),
                       ("LF", [L], F32), ("PL", [48], U16), ("LU", [16], U16), ("LSH", [80], U16), ("LSF", [80], U16),
                       ("RO", [16], U16), ("RQ", [16], U16)):
        if _t > 0 or _n in ("KA", "DU", "DT", "RO", "RQ"):
            _sb("%s%d" % (_n, _t), _s, _d)
for _d, _w in _fill.items():
    SCRATCH["S" + _d] = ("sbuf", [128, _w], _d)
for _n in range(6):
    SCRATCH["T%d" % _n] = ("psum", [128, 32, 16], F32)
for _n in ("PH", "PF", "T0", "T1")[:NS - 2]:
    SCRATCH[_n] = ("psum", [128, 512], F32)
    PLACE[_n] = (_n, 0, 512)
KINDS = [(13, 16), (5, 5), (8, 8)]


def helpers(T, topo, core):
    c = [x for x in topo.cores_of(core) if x != core and all(topo.may_write(x, d) for d in T.cores)]
    return [x for x in c if topo.die(x) == topo.die(core)][0], [x for x in c if topo.die(x) != topo.die(core)]


def bits(e):
    return sum(1 << x for x in e)


def near(topo, a, b, m):
    e = topo.engines(a, b)
    return e[:len(e) // 2] if m in TABLES else e[len(e) // 2:]


def piece(T, m, i):
    return T[m][:, S // PARTS * i:S // PARTS * (i + 1)]


def helper_program(g, core, T, topo):
    n = len(T.cores)
    for r, src in enumerate(T.cores):
        small, big = helpers(T, topo, src)
        todo = [("a_" + m if got == m else None, T[got][:, :], m, T[m][:, :]) for got, m in SMALL] if core == small else []
        todo += [("p_%s%d" % (m, i), piece(T, m, i), m, piece(T, m, i)) for m in TABLES for i in range(PARTS) if big[i % len(big)] == core]
        left = {}
        for sem, have, m, land in todo:
            d = T.cores[(r + TO[m]) % n]
            if sem:
                g.wait_ge(T.sem[sem], len(near(topo, src, core, m)))
            rid, pid = topo.addr(d, core)
            g.remote_dma(land, have, T.sem["a_" + m], T.sem["l_" + m], pid, rid, topo.mask(core, d))
            left[m] = left.get(m, 0) + len(topo.engines(core, d))
        for m in left:
            g.wait_ge(T.sem["l_" + m], left[m])


def rank_program(g, core, T, topo):
    rank = T.rank_of(core)
    if rank is None:
        return helper_program(g, core, T, topo)
    Q = {"V": g.vector, "A": g.scalar, "P": g.tensor, "G": g, "S": g.sync}
    cnt = {}
    know = {e: {} for e in Q}
    know["net"] = {}
    hist = {}

    def b(name, lo=0, hi=None, step=1, p=(0, 128)):
        whole, first, width = PLACE[name]
        hi = first + (width if hi is None else hi)
        lo += first
        ap = T[whole][p[0]:p[1], lo:hi] if step == 1 else T[whole][p[0]:p[1], lo:hi:step]
        return (ap, whole, (0, 1, lo, hi), None, -(-(hi - lo) // step), name)

    def b3(name, c0, c1, lo=0, hi=16, p=(0, 128), cs=1, step=1):
        ap = T[name][p[0]:p[1], slice(c0, c1, cs if cs > 1 else None), slice(lo, hi, step if step > 1 else None)]
        return (ap, name, (c0, c1, lo, hi), None, -(-(c1 - c0) // cs) * -(-(hi - lo) // step), name)

    def b2(name, c, lo, hi, p=(0, 128)):
        return (T[name][p[0]:p[1], c, lo:hi], name, (c, c + 1, lo, hi), None, hi - lo)

    def ind(win, off):
        return (win[0].indirect(off[0]), win[1], win[2], off, 16 * off[4])

    def hits(x, y):
        return x[0] < y[1] and y[0] < x[1] and x[2] < y[3] and y[2] < x[3]

    def inside(x, y):
        return x[0] >= y[0] and x[1] <= y[1] and x[2] >= y[2] and x[3] <= y[3]

    def regions(ops):
        return [(o[1], o[2], SCRATCH[o[1]][0] == "psum") for o in ops if isinstance(o, tuple)]

    def offsets(ops):
        return [o[3] for o in ops if isinstance(o, tuple) and o[3]]

    def sync(e, reads, writes):
        deps = {}
        for w, lst in ((False, reads), (True, writes)):
            for name, reg, psum in lst:
                for (r2, w2, e2, sem, count, snap) in hist.get(name, []):
                    if not (psum and e2 != e):
                        if not (w or w2) or not hits(reg, r2):
                            continue
                        if e2 == e == "P":
                            continue
                    if deps.get(sem, (0, None))[0] < count:
                        deps[sem] = (count, snap)
        k = know[e]
        for sem in sorted(deps, key=lambda x: -len(deps[x][1])):
            count, snap = deps[sem]
            if k.get(sem, 0) < count:
                Q[e].wait_ge(T.sem[sem], count)
                k[sem] = count
                for s2, v in snap.items():
                    if k.get(s2, 0) < v:
                        k[s2] = v

    def note(e, reads, writes, sem, n):
        cnt[sem] = cnt.get(sem, 0) + n
        snap = dict(know[e])
        for w, lst in ((False, reads), (True, writes)):
            for name, reg, psum in lst:
                keep = [x for x in hist.get(name, [])
                        if not (w and psum is False and inside(x[0], reg) and not strided(name)
                                or (inside(x[0], reg) and x[1] == w and x[2] == e and x[3] == sem))]
                hist[name] = keep + [(reg, w, e, sem, cnt[sem], snap)]

    def strided(name):
        return name in ("ZX1", "ZX2")

    def emit(e, f, out, ins):
        reads, writes = regions(ins + offsets(ins + [out])), regions([out])
        sync(e, reads, writes)
        f(Q[e]).then_inc(T.sem["q" + e], 1)
        note(e, reads, writes, "q" + e, 1)

    nodes, seen, group = [], {}, []

    def node(e, run, reads, writes, dur, lat=0.0, after=None, done=1):
        k, before = len(nodes), {}
        if after is not None:
            before[after] = done
        for w, lst in ((False, reads), (True, writes)):
            for name, reg, psum in lst:
                for (r2, w2, j) in seen.get(name, []):
                    if nodes[j][0] == e == "P" and psum:
                        before.setdefault(j, 0)
                    elif (psum and nodes[j][0] != e) or ((w or w2) and hits(reg, r2)):
                        before[j] = 1
        for w, lst in ((False, reads), (True, writes)):
            for name, reg, psum in lst:
                keep = [x for x in seen.get(name, []) if not (w and inside(x[0], reg) and not psum)]
                seen[name] = keep + [(reg, w, k)]
        nodes.append((e, run, dur * CF, lat, sorted(before.items()), writes))
        return k

    def op(e, f, out, ins, after=None, done=1):
        win = [x for x in ins if isinstance(x, tuple) and x[3]]
        c = 0.00087 * max(x[4] for x in ins + [out] if isinstance(x, tuple))
        if e == "G":
            dur = 0.15 + 2 * c
        elif out[3]:
            dur = 0.05 + SC * c
        elif win:
            dur = 0.06 + GA * 0.00085 * out[4]
        else:
            two = all(SCRATCH[x[1]][2] in (BF, U16) for x in ins + [out] if isinstance(x, tuple))
            both = len(ins) == 2 and all(isinstance(x, tuple) and x[4] == out[4] and SCRATCH[x[1]][0] == "sbuf" for x in ins)
            dur = max(0.06, 0.05 + c * (0.5 if two and e == "V" else 2 if both else 1)) + (AFX if e == "A" else 0)
            dur += 1.3 if out[1] == "RKM" else 0
        return node(e, lambda: emit(e, f, out, ins), regions(ins + offsets(ins + [out])), regions([out]), dur, 0.0, after, done)

    def issue():
        n = len(nodes)
        pred = [[(j, (nodes[j][3] + LAG) * full) for j, full in x[4]] for x in nodes]
        succ, above = [[] for _ in nodes], [0] * n
        for k in range(n):
            far = 0
            for j, gap in pred[k]:
                above[k] |= above[j] | 1 << j
                far |= above[j] if nodes[j][2] + gap >= LAG else 0
            pred[k] = [(j, gap) for j, gap in pred[k] if gap > LAG or not far >> j & 1]
            for j, gap in pred[k]:
                succ[j].append((k, gap))

        def place(order, before, last):
            end, taken = [0.0] * n, {}
            for k in order:
                e, dur = nodes[k][0], nodes[k][2]
                t = max([last[k]] + [end[j] + gap for j, gap in before[k]])
                row = taken.setdefault(e, [])
                i, hi = 0, len(row)
                while i < hi:
                    mid = (i + hi) // 2
                    i, hi = (mid + 1, hi) if row[mid][1] <= t else (i, mid)
                while i < len(row) and row[i][0] < t + dur - 1e-9:
                    t = max(t, row[i][1])
                    i += 1
                row.insert(i, (t, t + dur))
                end[k] = t + dur
            return end

        tail = [0.0] * n
        for k in reversed(range(n)):
            tail[k] = nodes[k][2] + max([nodes[k][3]] + [tail[s] + gap for s, gap in succ[k]])
        lat, seed = [x[3] for x in nodes], [SEED]

        def forwards(key):
            end = place(sorted(range(n), key=lambda k: (key[k], k)), pred, [0.0] * n)
            span = max(end[k] + lat[k] for k in range(n))
            return (span + 0.5 * sum(end) / n, span, end)

        def turned(end):
            return forwards([-x for x in place(sorted(range(n), key=lambda k: (-end[k], -k)), succ, lat)])

        def draw():
            seed[0] = (seed[0] * 1103515245 + 12345) % 2147483648
            return (seed[0] >> 8) / 8388608.0

        def moved(end):
            k, held = max(range(n), key=lambda k: end[k] + lat[k]), []
            by = {(nodes[j][0], round(end[j], 6)): j for j in range(n)}
            key = [end[j] - nodes[j][2] for j in range(n)]
            while k >= 0:
                ready, j = max([(0.0, -1)] + [(end[j] + gap, j) for j, gap in pred[k]])
                if ready < key[k] - 1e-6:
                    j = by[nodes[k][0], round(key[k], 6)]
                    held.append((k, ready, j))
                k = j
            k, ready, j = held[int(draw() * len(held))]
            if draw() < 0.6:
                key[k] = min(key[j], ready + (key[j] - ready) * draw()) - 1e-3
                for k in reversed(range(n)):
                    for s, gap in succ[k]:
                        if key[k] >= key[s]:
                            key[k] = key[s] - 1e-6
            else:
                key[j] = key[k] + 1e-3 + 2 * draw() * draw()
                for k in range(n):
                    for s, gap in pred[k]:
                        if key[k] <= key[s]:
                            key[k] = key[s] + 1e-6
            return forwards(key)

        NODES.append(nodes)
        if not SPAN:
            best = now = forwards([-x for x in tail])
            for i in range(TRIES):
                other = turned(now[2]) if i % 50 < (4 if i < 50 else 1) else moved(now[2])
                if other[0] - now[0] < -T0 * 0.05 ** (i / TRIES) * math.log(1 - draw()):
                    now = other
                best = min(best, now)
            SPAN.extend(best[1:])
        for k in sorted(range(n), key=lambda k: (SPAN[1][k] - nodes[k][2], SPAN[1][k], k)):
            nodes[k][1]()

    def A_(o):
        return o[0] if isinstance(o, tuple) else o

    def tt(out, a, c, o, behind=None):
        return op("V", lambda q: q.tensor_tensor(A_(out), A_(a), A_(c), o), out, [a, c], behind, 0)

    def ts(out, a, s1, o1, s2=None, o2=None):
        if o2 is None:
            op("V", lambda q: q.tensor_scalar(A_(out), A_(a), A_(s1), None, o1), out, [a, s1])
        else:
            op("V", lambda q: q.tensor_scalar(A_(out), A_(a), A_(s1), A_(s2), o1, o2), out, [a, s1, s2])

    def cp(out, a):
        return op("V", lambda q: q.tensor_copy(A_(out), A_(a)), out, [a])

    def scan(out, d0, d1, o0, o1, first=0.0):
        op("V", lambda q: q.tensor_tensor_scan(A_(out), A_(d0), A_(d1), first, o0, o1), out, [d0, d1, 0])

    def ms(out, v):
        op("V", lambda q: q.memset(A_(out), v), out, [])

    def tr(out, a, behind):
        return op("V", lambda q: q.transpose(A_(out), A_(a)), out, [a], behind, 0)

    table = [None]

    def act(out, a, fn=AF.Copy, scale=1.0, bias=0.0):
        if (fn, scale, bias) == (AF.Copy, 1.0, 0.0) and out[-1] in ONG and not a[3] and SCRATCH[a[1]][0] == "sbuf":
            return asel(out, a, [[0, out[4]]], OP.is_ge, 0, 0)
        if fn in (AF.Copy, AF.Identity) and out[-1] in ONV and not a[3]:
            return cp(out, a) if (scale, bias) == (1.0, 0.0) else ts(out, a, scale, OP.mult, bias, OP.add)
        k = op("A", lambda q: q.activation(A_(out), A_(a), fn, bias=A_(bias), scale=A_(scale)), out, [a, scale, bias],
               table[0] if a[3] else None, 0)
        if out[1] == "RKM":
            table[0] = k

    tiles = {}

    def mm_now(out, l, r, st, sp, tile):
        was = tiles.get(out[1], (tile, 0))
        if tile is not None and was[0] != tile and know["P"].get("qP", 0) < was[1]:
            g.tensor.wait_ge(T.sem.qP, was[1])
            know["P"]["qP"] = was[1]
        emit("P", lambda q: q.matmul(A_(out), A_(l), A_(r), st, sp), out, [l, r])
        tiles[out[1]] = (tile, cnt["qP"])

    def mms(*m):
        m = [tuple(x) + (None,) * (6 - len(x)) for x in m]
        if len(m) > 4:
            return [mms(*m[i:i + 4]) for i in range(0, len(m), 4)]
        node("P", lambda: [mm_now(*x) for x in m], regions([x[1] for x in m] + [x[2] for x in m]), regions([x[0] for x in m]),
             sum(PFX + PEC * max(min(64, x[1][4]), x[0][4]) * (4 if SCRATCH[x[1][1]][2] == F32 else 1) for x in m))

    def iota(out, pat, base, cm, after=None):
        if SCRATCH[out[1]][2] == I32:
            op("G", lambda q: q.iota(A_(out), pat, base, cm), out, [], after)
        else:
            op("G", lambda q: q.iota(A_(out), pat, base, cm, allow_small_or_imprecise_dtypes=True), out, [], after)

    def asel(out, a, pat, o, base, cm, after=None):
        op("G", lambda q: q.affine_select(A_(out), A_(a), pat, o, 0.0, base, cm), out, [a], after, 0)

    def scat(win, width, off, n, val):
        cp(ind(b(win, 0, width), b(off, 0, n)), val)

    def load(e, out, src, name, behind, when=None):
        w, r = regions([out]), regions([when])

        def run():
            sync(e, r, w)
            Q[e].dma_start(out[0], src).then_inc(T.sem["d_" + name], 16)
            note(e, [], w, "d_" + name, 16)
        return node(e, run, r, w, 0.1, HOP + (2.0 if out[4] > 700 else 0.5), behind, 0)

    def store(e, dst, a, name):
        r = regions([a])

        def run():
            sync(e, r, [])
            Q[e].dma_start(dst, a[0]).then_inc(T.sem["o_" + name], 16)
            note(e, r, [], "o_" + name, 16)
        node(e, run, r, [], 0.1, HOP + (2.0 if name == "yt" else 0.3))

    small, big = helpers(T, topo, core)
    sent = [None]

    def send(m, src, lats):
        r = regions([src])
        if m in TABLES:
            calls = [(big[i % len(big)], piece(T, m, i), piece(T, "HT", i), "p_%s%d" % (m, i)) for i in range(PARTS)]
        else:
            calls = [(T.cores[(rank + TO[m]) % len(T.cores)] if m == "U2D" else small, T[m][:, :], src[0], "a_" + m)]

        def run():
            sync("G", r, [])
            for to, land, have, sem in calls:
                es = topo.engines(core, to) if m == "U2D" else near(topo, core, to, m)
                rid, pid = topo.addr(to, core)
                g.remote_dma(land, have, T.sem[sem], T.sem["l_" + m], pid, rid, bits(es))
                note("G", r, [], "l_" + m, len(es))
        k = sent[0] = node("G", run, r, [], 1.2 if m == "RQZ" else 0.15 * len(calls), 0.0, sent[0], 0)
        for x, lat in lats.items():
            far = T.cores[(rank - TO[x]) % len(T.cores)]
            by = [far] if x == "U2D" else helpers(T, topo, far)[1] * PARTS if x in TABLES else helpers(T, topo, far)[:1]
            arrives(x, sum(len(topo.engines(y, core)) for y in by[:PARTS]), lat, k)
        return k

    def arrives(x, n, lat, k):
        w = regions([b(x, 0, S) if x in ("F2", "F3") else b(x)])
        node("n" + x, lambda: note("net", [], w, "a_" + x, n), [], w, 0.0, lat, k)

    k = load("S", b("ZF", 80, 288), T.zf[:, 0:L], "zf0", None)
    j = load("A", b("EF", 96, 320), T.ef[:, 0:224], "ef0", None)
    j = load("A", b("EH", 96, 320), T.eh[:, 0:224], "eh0", j)
    j = load("A", b("HT", 0, S), T.tab[:, :], "tab", j)
    ms(b("EF", 80, 96), 0)
    ms(b("EH", 80, 96), 0)

    ms(b("ONB"), 1.0)
    iota(b("PI"), [[0, 1]], 0, 1)
    iota(b("C16"), [[16, 48]], 0, 0)
    iota(b("PC"), [[0, 8], [1, 2]], 0, 0)
    iota(b("KIO"), [[0, 13], [1, 16]], 0, 0)
    asel(b("ID"), b("ONB"), [[-1, 128]], OP.is_equal, 0, 1)
    z0 = b("ZF", 80, 288)
    first = send("RQZ", z0, {"RQZ": 2 * HOP + 1.5, "U2Z": 2 * HOP + 4.0})
    asel(b("BA"), b("ONB"), [[-16, 8], [0, 16]], OP.is_ge, 0, 1, first)
    asel(b("BO"), b("BA"), [[16, 8], [0, 16]], OP.is_ge, 15, -1)
    ts(b("PJ"), b("PI"), 15, OP.bitwise_and)
    ts(b("PK"), b("PI"), 4, OP.arith_shift_right, 1, OP.bitwise_and)
    cp(b("PM"), b("PJ"))
    cp(b("MH1"), b("PK"))
    ts(b("FW"), b("C16"), b("PM"), OP.add)

    def aff(out, a, scale, bias):
        if isinstance(bias, tuple):
            act(out, a, AF.Identity, scale, bias)
        else:
            act(out, a, AF.Copy, scale, float(bias))

    def fill(out, v, after):
        iota(out, [[0, out[4]]], v, 0, after)

    act(b("RKM"), b("KIO"), AF.Sigmoid, 400.0, -200.0)
    aff(b("MH0"), b("MH1"), -1.0, 1)
    ms(b("WMU"), 0.0)
    act(b("WMU", 15, 143, 16), b("BO", 0, 128, 16), scale=float(PEN))
    act(b("NBO"), b("BO"), scale=-1.0)
    act(b("IDF"), b("ID"))
    ts(b("PY"), b("PM"), -1.0, OP.add)
    act(b("IDN"), b("ID"), scale=b("PY"))
    act(b("WMH"), b("WMU"), scale=16.0)
    aff(b("KAD"), b("KIO"), -4096.0, OKB + 61440)
    ts(b("M16"), b("KIO"), b("PM"), OP.is_equal)

    tt(b("PX"), b("PJ"), b("PK"), OP.add)
    ts(b("PX"), b("PX"), 1, OP.bitwise_and)
    ts(b("PC"), b("PC"), b("MH1"), OP.not_equal)

    def places(x):
        nc, s = KINDS[x]
        off = 32.0 * ((nc + 1) // 2) + 16
        if s == 5:
            ts(b("RK", 0, s), b("FW", 0, s), 1.0 / s, OP.mult, 0.5 / s - 0.5, OP.add)
            ts(b("RX", 0, s), b("RK", 0, s), -float(s), OP.mult)
            tt(b("RC", 0, s), b("RX", 0, s), b("FW", 0, s), OP.add)
            ts(b("RP", 0, s), b("RC", 0, s), 1, OP.bitwise_and)
            ts(b("RX", 0, s), b("RP", 0, s), b("MH1"), OP.not_equal, off, OP.mult)
            ts(b("RY", 0, s), b("RK", 0, s), 1.0 - 16 * s, OP.mult)
            tt(b("RX", 0, s), b("RX", 0, s), b("RY", 0, s), OP.add)
            aff(b("RY", 0, s), b("FW", 0, s), 16.0, 0)
            tt(b("RX", 0, s), b("RX", 0, s), b("RY", 0, s), OP.add)
            cp(b("RO%d" % x, 0, s), b("RX", 0, s))
        else:
            r = b("RB", x, x + 1)
            if s == 16:
                ts(r, b("PM"), nc - 1.0, OP.min, 16.0, OP.mult)
            else:
                ts(r, b("PM"), 8.0, OP.is_ge, -127.0, OP.mult)
                aff(r, b("PM"), 16.0, r)
            ts(r, b("PX"), off, OP.mult, r, OP.add)
            ts(b("RO%d" % x, 0, s), b("C16", 0, s), 1.0 / s, OP.mult, r, OP.add)
        r = b("RZ%d" % x, 0, nc)
        if s == 8:
            iota(r, [[8, 2], [1, 2], [64, 2]], 0, 0)
            ts(b("RC", 8, 9), b("PJ"), 2, OP.arith_shift_right)
            tt(b("RC", 9, 10), b("RC", 8, 9), b("PK"), OP.add)
            ts(b("RC", 9, 10), b("RC", 9, 10), 1, OP.bitwise_and)
            ts(b("RY", 8, 9), b("RC", 8, 9), 8.0, OP.mult, b("PM"), OP.add)
            ts(b("RY", 8, 9), b("RY", 8, 9), b("PM"), OP.add)
            ts(b("RY", 8, 9), b("RC", 9, 10), off, OP.mult, b("RY", 8, 9), OP.add)
            return ts(b("RQ%d" % x, 0, nc), r, b("RY", 8, 9), OP.add)
        aff(r, b("PC", 0, nc), off, b("PM"))
        tt(r, r, b("C16", 0, nc), OP.add)
        cp(b("RQ%d" % x, 0, nc), r)

    def lists(x, src, lo, y, out, key=None, behind=None):
        nc, s = KINDS[x]
        n1, n2 = 32 * ((nc + 1) // 2), 32 * (nc // 2 + 1)
        tr(b(y, 0, n1), b(src, lo, lo + n1), behind)
        tr(b(y, n1, n1 + n2), b(src, lo - 16, lo - 16 + n2), behind)
        row[1] = cp(b(out, 0, 16 * s), ind(b(y, 0, n1 + n2), b("RO%d" % x, 0, s)))
        if key and x == 2:
            act(key, ind(b(y, 0, n1 + n2), b("RQ%d" % x, 0, nc)))
        elif key:
            tt(key, ind(b(y, 0, n1 + n2), b("RQ%d" % x, 0, nc)), b("KAD", 0, 16 * nc), OP.add)

    bank, row = [0, 0, 0], [None, None]

    def free_bank(n):
        bank[0] += 1
        bank[1 + (n == 6)] += 1
        return "T%d" % (bank[0] % 6 if NS == 4 else bank[2] % 2 if n == 6 else 2 + bank[1] % 4)

    def cols(t, n, lo=0, step=1):
        return b(t, lo, n, step) if t in PLACE else b3(t, 0, n // 16, lo, 16, step=step)

    def look(x, win, lst, z, cm, c0, chunks, k1, wide=None):
        nc, s = KINDS[x]
        for j in k1:
            lo, hi = 16 * c0, 16 * (c0 + nc)
            row[0] = tt((T[cm][:, lo:hi, j], cm, (lo, hi, j, j + 1), None, hi - lo), ind(win, b(lst, s * j, s * j + nc)), z, OP.is_le,
                        row[0] if j or x else None)
        for k0, k in chunks:
            n = k - k0
            ga, t = "GA%d" % (bank[0] % 6), free_bank(n)
            if s == nc:
                act(b(ga, 0, 16 * s * n), ind(win, b(lst, s * k0, s * k)), scale=-1.0)
            m = []
            for j in range(n):
                o, got = cols(t, 16 * nc * n, j, n), b(ga, 16 * nc * j, 16 * nc * (j + 1))
                if s != nc:
                    act(got, ind(win, b(lst, s * (k0 + j), s * (k0 + j) + nc)), scale=-1.0)
                m += [(o, b("ID"), got, False, j == n - 1)] if wide else [(o, b("ID"), z, True, False), (o, b("ID"), got, False, True)]
            if wide:
                mms((cols(t, 16 * nc * n), b("ID"), b3(wide, 0, 16 * nc, 0, n), True, False))
            mms(*m)
            act(b3(cm, 16 * c0, 16 * (c0 + nc), k0, k), cols(t, 16 * nc * n), AF.Sigmoid, 400.0, 200.0)

    def look2(win, lst, z, cm, na, j0=0, j1=8):
        for j in range(j0, j1):
            out = (T[cm][:, :, j], cm, (0, 256, j, j + 1), None, 256)
            got = ind(win, b(lst, 16 * j, 16 * j + 16))
            if j < 8 - na:
                row[0] = tt(out, got, z, OP.is_le, row[0])
                continue
            ga, t = b("GA%d" % (bank[0] % 6), 0, 256), cols(free_bank(1), 256)
            act(ga, got, scale=-1.0)
            mms((t, b("ID"), z, True, False))
            mms((t, b("ID"), ga, False, True))
            act(out, t, AF.Sigmoid, 400.0, 200.0)

    def sums2(key):
        out = b("PH", 80, L)
        mms((out, b("IDF"), key, True, False), (out, b("ID"), b("KAB"), False, False))
        mms(*[(b("PH", 80 + 64 * h, 144 + 64 * h), b("WMH", 15 - m, 143 - m), b3("CDH", m, 256, 4 * h, 4 * h + 4, cs=16), False, h + m == 16)
              for h in (0, 1) for m in range(16)])

    def far_sums(cm, r0, r1, k0, k1, bank, lo):
        out = b(bank, lo, lo + (r1 - r0) // 16 * (k1 - k0))
        mms(*[(out, b("WMU", 15 - m, 143 - m), b3(cm, r0 + m, r1, k0, k1, cs=16), m == 0, m == 15) for m in range(16)])

    def pairs(n, w):
        return [(k, min(16, k + w)) for k in range(16 - n, 16, w)], range(16 - n)

    def sums(cm, c0, c1, key):
        out = b("PH", 16 * c0, 16 * c1)
        mms((out, b("IDF"), key, True, False))
        if c0:
            mms((out, b("ID"), b("KAB"), False, False))
        mms(*[(out, b("WMH", 15 - m, 143 - m), b3(cm, 16 * c0 + m, 16 * c1, cs=16), False, m == 15) for m in range(16)])

    def far_max(c0, c1, k0, k1, bank, lo, out, other):
        n = k1 - k0
        hi = lo + n * (c1 - c0)
        mms(*[(b(bank, lo, hi), b("WMU", 15 - m, 143 - m), b3("CMF", 16 * c0 + m, 16 * c1, k0, k1, cs=16), m == 0, m == 15)
              for m in range(16)])
        scan(b("FS", lo, hi), b("RKM" if n == 16 else "RK8", 0, hi - lo), b(bank, lo, hi), OP.mult, OP.max)
        tt(out, b("FS", lo + n - 1, hi, n), other, OP.max)

    def home_max(t):
        scan(b("HS"), b("RK4" if t else "RKM"), b("PH", 0, L), OP.mult, OP.max)
        if t:
            tt(b("A1"), b("HS", 83, 144, 4), b("HS", 147, L, 4), OP.max)
            cp(b("HKI", 0, 5), b("HS", 15, 80, 16))
            tt(b("HKI", 5, 13), b("A1", 0, 8), b("A1", 8, 16), OP.max)
        else:
            cp(b("HKI", 0, 13), b("HS", 15, L, 16))
        ts(b("HSL", 0, 13), b("HKI", 0, 13), OKB + S - 1, OP.bitwise_and)
        ts(b("WI", 0, 13), b("HKI", 0, 13), 4, OP.arith_shift_right, 31 * PEN, OP.bitwise_and)
        tt(b("AP", 0, 13), b("HSL", 0, 13), b("WI", 0, 13), OP.max)

    CS = b("PF", 224, 237)

    def decide(t, yy, grown):
        ts(b("IX", 0, 13), yy, float(OKB + S), OP.min, float(OKB), OP.subtract)
        ts(b("B0"), ind(b("CT", 0, S + 16), b("IX", 0, 13)), b("MH0"), OP.mult)
        act(b("B1"), ind(b("CT", 0, S + 16), b("IX", 0, 13)), scale=b("MH1"))
        for a in (0, 2, 1, 3):
            pp = (32 * a, 32 * a + 32)
            mms((cols("T%d" % a, 2 * L), b("FJ", 0, NB, p=pp), b("FJ2" if a > NS - 5 else "FJ", 0, 2 * L, p=pp), True, False, a))
            for x in (0, 1):
                out = b3("T%d" % a, x, 26, cs=2) if a > NS - 5 else b("T%d" % a, L * x, L * x + L)
                mms((out, b("B%d" % x, 0, NB, p=pp), b("B%d" % x, p=pp), False, x == 1, a))
        for h in (0, 1):
            pp = (64 * h, 64 * h + 32)
            mms((b3("T%d" % (4 + h), 0, 20, p=(0, 80)), b("FJ", NB, L, p=pp), b("FJ4", p=pp), True, False, 2 * h))
        for a in (0, 2, 1, 3):
            pp = (32 * a, 32 * a + 32)
            mms(*[(b3("T%d" % (4 + a // 2), 2 * (a % 2) + x, 20, cs=4, p=(0, 80)), b("B%d" % x, NB, L, p=pp),
                   b("B%d" % x, NB, L, p=pp), False, a % 2 + x == 2, a) for x in (0, 1)])

        def over(a, c0, c1):
            if a < NS - 4:
                out, src, x, pp = b3("E0", 0, 13, 32 * a + 16 * c0, 32 * a + 16 * c1), b("T%d" % a, L * c0, L * c1), 0, (0, NB)
            elif a < 4:
                out, src, x, pp = b3("E0", c0, c1, 32 * a, 32 * a + 32), b3("T%d" % a, 2 * c0, 2 * c1), 0, (0, NB)
            else:
                pp = (0, L - NB)
                out, src, x = b3("E1", 0, 5, 64 * a - 256, 64 * a - 192, p=pp), b3("T%d" % a, 0, 20, p=pp), 1
            if a in EA:
                act(out, src, AF.Relu, 1024.0, b("TN", x, x + 1, p=pp))
            else:
                ts(out, src, b("TH", x, x + 1, p=pp), OP.is_gt)
        mms((CS, b("IDF"), yy, True, False))
        for a in range(4):
            for c0, c1 in ECA if a in EA else ((0, 1), (1, 2)) if NS == 6 else ECV:
                over(a, c0, c1)
        over(4, 0, 5)
        over(5, 0, 5)
        for c0, c1 in ECUT:
            mms(*[(b("PF", 224 + c, 225 + c), b2("E0", c, 0, 128), b("BW"), False, False) for c in range(c0, c1)])
        mms(*[(b("PF", 224 + c, 225 + c), b2("E1", c - 8, 0, 128, p=(0, 80)), b("BW", p=(0, 80)), False, c == 12) for c in range(8, 13)])
        ts(b("WU", 0, 13), yy, float(OKB + S), OP.max, 1.0 / PEN, OP.mult)
        act(grown, ind(b("TW"), b("WU", 0, 13)))
        tt(b("DS", 0, 13), CS, b("DU%d" % t, 0, 13), OP.min)
        ts(b("DT%d" % t, 0, 13), b("DS", 0, 13), float(OKB), OP.subtract)

    def lanes(t, n, fill, val):
        pls, lw, lu = "PL%d" % t, "LW%d" % t, "LU%d" % t
        scan(b("UC", 0, n), b("ON32", 0, n), b("UU", 0, n), OP.mult, OP.add)
        tt(b("NU", 0, n), b("UU", 0, n), b("CN", 0, n), OP.mult)
        out = b("PH", 224, 224 + n)
        mms((out, b("ID"), b("CF", 0, n), True, False))
        mms((out, b("NT"), b("UU", 0, n), False, False), (out, b("IDN"), b("UU", 0, n), False, False))
        mms((out, b("ID"), b("NU", 0, n), False, False), (out, b("BO"), b("UC", 0, n), False, True),
            (b("PH", 256, 257), b("BO"), b("UC", n - 1, n), True, True))
        ts(b(pls, 0, n), out, b("PM"), OP.subtract)
        aff(b("TS"), b("PH", 256, 257), -KQ, (fill - BIG) * KQ + 0.5)
        if t in LWA:
            act(ind(b(lw, 0, 1024), b(pls, 0, n)), val, AF.Sigmoid)
        else:
            scat(lw, 1024, pls, n, b("QW", 416 - 16 * n - (128 if t == 1 else 0), 288 if t == 1 else 416))
        aff(b("LD"), b("LM", 0, 128), KQ, b("TS"))
        scan(b("XS"), b("LD"), b(lw, 0, 128), OP.max, OP.min)
        ts(b(lu, 0, 8), b("XS", 15, 128, 16), 1.0 / KQ, OP.mult, 0.3 - 0.5 / KQ, OP.add)

    def wrap(x):
        act(b(x, S, S + PAD), b(x, 0, PAD))

    def step(t, ftab, update, later):
        lu, zl = b("LU%d" % t, 0, 8), "ZL%d" % t
        home, far = b("HT", 0, S + PAD), b(ftab, 0, S + PAD)
        look(1, b("HT", 0, S), "LSH%d" % t, b(zl, 0, 80), "CMH", 0, *pairs(16, NS), "ZX%d" % t)
        act(b("DQ"), ind(b("D"), lu))
        act(b(zl, 80, L), ind(b("ZF"), lu))
        act(b(zl, L, 336), b(zl, 80, L))
        tt(b("XH", 16, 144), ind(b("EH", 16, 16 + F), lu), b("DQ"), OP.add)
        lists(2, "XH", 16, "YH", "LDH", b("KA%d" % t, 80, L))
        tt(b("XF", 16, 144), ind(b("EF", 16, 16 + F), lu), b("DQ"), OP.add)
        lists(2, "XF", 16, "YF", "LDF")
        act(b("LF%d" % t, 80, L), ind(b("FQ"), lu))
        update()
        sums("CMH", 0, 5, b("KA%d" % t, 0, 80))
        look2(home, "LDH", b(zl, 80, 336), "CDH", KD[2 * t - 2], 0, MIX[0])
        look2(far, "LDF", b(zl, 80, 336), "CDF", KD[2 * t - 1], 0, MIX[1])
        look2(home, "LDH", b(zl, 80, 336), "CDH", KD[2 * t - 2], MIX[0])
        look(1, b(ftab, 0, S), "LSF%d" % t, b(zl, 0, 80), "CMF", 0, *pairs(16, NS), "ZX%d" % t)
        sums2(b("KA%d" % t, 80, L))
        look2(far, "LDF", b(zl, 80, 336), "CDF", KD[2 * t - 1], MIX[1])
        home_max(t)
        if SFIRST:
            far_sums("CMF", 0, 80, 0, 16, "PF", 0)
        far_sums("CDF", 0, 256, 0, 4, "PF", 80)
        if not SFIRST:
            far_sums("CMF", 0, 80, 0, 16, "PF", 0)
        far_sums("CDF", 0, 256, 4, 8, "PH", 320)
        scan(b("FS", 0, 144), b("RK4", 0, 144), b("PF", 0, 144), OP.mult, OP.max)
        scan(b("FS", 320, 384), b("RK4", 80, 144), b("PH", 320, 384), OP.mult, OP.max)
        tt(b("YY", 0, 5), b("FS", 15, 80, 16), b("AP", 0, 5), OP.max)
        tt(b("QQ", 0, 8), b("FS", 83, 112, 4), b("FS", 115, 144, 4), OP.max)
        tt(b("QQ", 8, 16), b("FS", 323, 352, 4), b("FS", 355, 384, 4), OP.max)
        tt(b("AP", 5, 13), b("QQ", 0, 8), b("AP", 5, 13), OP.max)
        tt(b("YY", 5, 13), b("QQ", 8, 16), b("AP", 5, 13), OP.max)
        later(b("YY", 0, 13))

    places(0)
    lists(0, "EF", 96, "YA", "LF0")
    asked = send("RQL", b("LF0"), {"RQL": 2 * HOP + RQX})
    lists(0, "EH", 96, "YB", "LH0", b("KA0"), row[1] - 1)
    k = load("S", b("ZF", 0, 80), T.zf[:, 544:F], "zf1", asked, b("LH0"))
    k = load("S", b("EH", 16, 96), T.eh[:, 544:F], "eh1", k)
    k = load("S", b("EF", 16, 96), T.ef[:, 544:F], "ef1", k)
    k = load("S", b("EH", 320, F + 16), T.eh[:, 224:544], "eh2", k)
    k = load("S", b("EF", 320, F + 16), T.ef[:, 224:544], "ef2", k)
    k = load("S", b("ZF", 288, F), T.zf[:, L:544], "zf2", k)
    send("F2", b("HT", 0, S), {"F2": 16.0})
    asel(b("NT"), b("NBO"), [[-1, 128]], OP.is_gt, 0, 1)
    iota(b("FJ"), [[0, 2], [1, L]], 48, 0, asked)
    iota(b("TH"), [[NB, 2]], 48, 1, asked)
    iota(b("TW"), [[1, 32]], 0, 0)
    for x in range(0, WT, 676):
        iota(b("OC", x, x + 676), [[0, 676]], -1, 0, asked)
    tab = b("HT", 0, S)
    look(0, tab, "LH0", z0, "CMH", 0, *pairs(KA0, 2))
    look(0, tab, "RQL", b("RQZ"), "CMF", 0, KR0, [k for k in range(16) if not any(x <= k < y for x, y in KR0)])
    ms(b("KFO"), 0.0)
    act(b("RK4", 0, 80), b("RKM", 0, 80))
    iota(b("RK4", 80, L), [[0, 32], [1, 4]], 0, 0, asked)
    act(b("RK4", 80, L), b("RK4", 80, L), AF.Sign)
    for h in (0, 1):
        iota(b("KAB", 64 * h, 64 * h + 64), [[-4096, 2], [0, 8], [-8192, 4]], OKB + 61440 - 32768 * h, 0, asked)
    if HFIRST:
        sums("CMH", 0, 13, b("KA0"))
    w = CUT0
    iota(b("RKA", 0, 13 * w), [[0, 13], [1, w]], 0, 0, asked)
    iota(b("RKA", 13 * w, L), [[0, 13], [1, 16 - w]], 0, 0, asked)
    act(b("RKA"), b("RKA"), AF.Sign)
    far_sums("CMF", 0, L, 0, w, "PF", 0)
    far_sums("CMF", 0, L, w, 16, "PF", 13 * w)
    scan(b("FS", 0, L), b("RKA"), b("PF", 0, L), OP.mult, OP.max)
    tt(b("KFO", 0, 13), b("FS", w - 1, 13 * w, w), b("FS", 12 * w + 15, L, 16 - w), OP.max)
    if not HFIRST:
        sums("CMH", 0, 13, b("KA0"))
    told = send("KFR", b("KFO"), {"KFR": 2 * HOP + KX})
    home_max(0)
    fill(b("ON32"), 1, asked)
    ts(b("CT", 0, 1), b("PM"), 11.0, OP.is_lt, -1.0, OP.mult)
    act(b("M2"), b("M16", 0, 16), scale=2.0)
    fill(b("CT", S, S + 16), 0, asked)
    for j in range(11):
        for lo in range(0, 1 << j, 512):
            hi = min(1 << j, lo + 512)
            ts(b("CT", (1 << j) + lo, (1 << j) + hi), b("CT", lo, hi), b("M2", j, j + 1), OP.add)
    ts(b("MC", 0, 1), b("M2", 11, 12), b("MH0"), OP.mult, 1.0 / 512, OP.mult)
    iota(b("FJ2"), [[16, 13], [0, 2], [1, 16]], 48, 0, asked)
    iota(b("FJ4"), [[16, 5], [0, 4], [1, 16]], NB + 48, 0, asked)
    for x in ("FJ", "FJ2", "FJ4"):
        act(b(x), b(x), scale=b("MC", 0, 1))
    aff(b("TN"), b("TH"), 1.0 / 65536, 0.5 / 65536)
    tt(b("TN"), b("TN"), b("TH"), OP.mult)
    aff(b("TH"), b("TN"), 1.0, 11)
    act(b("TN"), b("TH"), scale=-1024.0)
    fill(b("BW"), int(BIG), asked)
    act(b("T01"), b("TW", 0, 16))
    ts(b("NU"), b("TW"), 9.0, OP.is_ge)
    tt(b("TW"), b("TW"), b("NU"), OP.mult)
    iota(b("FQ", 80, F), [[1, F - 80]], 0, 0, told)
    iota(b("QV"), [[1, 416]], 0, 0, told)
    iota(b("FQ", 0, 80), [[1, 80]], 544, 0, told)
    iota(b("LF1", 0, 80), [[1, 80]], 544, 0, told)
    iota(b("LF2", 0, 80), [[1, 80]], 464, 0, told)
    if len(LWA) < 2:
        aff(b("QW"), b("QV"), KQ, 0.5)
    if LWA:
        act(b("QV"), b("QV"), scale=4 * KQ)
    iota(b("LM"), [[1, L]], int(BIG), 0, asked)
    tt(b("LM"), b("LM"), b("M16"), OP.mult)
    aff(b("FM"), b("LM"), 1.0, -BIG)
    for t in range(3):
        aff(b("DU%d" % t, 0, 13), b("FW", 0, 13), 1.0, OKB + S + PAD + L * t)
    aff(b("DUQ", 0, 13), b("FW", 0, 13), 1.0, OKB + S + F)
    aff(b("CF"), b("C16", 0, 32), -1.0, 1008)
    aff(b("CN"), b("C16", 0, 32), 1.0, -1008)
    for n_ in ("DT0", "DT1"):
        ms(b(n_), 0)
    for n_, lo, hi, v_ in (("EH", 0, 16, 0), ("EF", 0, 16, 0), ("EH", F + 16, F + 32, 0), ("EF", F + 16, F + 32, 0), ("LW1", 0, 128, int(BIG))):
        fill(b(n_, lo, hi), v_, asked)
    for n_, lo, hi, v_ in (("D", 288, F, 0), ("XH", 0, 160, 0), ("XF", 0, 160, 0), ("BP", L, 336, 0), ("BX", L, 336, 1), ("LVF", L, 592, 1),
                           ("LVF", 592, 1104, 0), ("LVW", L, 656, 0), ("LVW", 656, 1104, 0), ("LW2", 0, 128, int(BIG)), ("D", 0, 80, 0)):
        fill(b(n_, lo, hi), v_, told)
    places(1)
    places(2)
    for t, q0 in ((1, 0), (2, 544)):
        lists(1, "EH", 16 + q0, "YS", "LSH%d" % t, b("KA%d" % t, 0, 80))
        lists(1, "EF", 16 + q0, "YT", "LSF%d" % t)
        act(b("ZL%d" % t, 0, 80), b("ZF", q0, q0 + 80))
        for j in range(NS):
            act((T["ZX%d" % t][:, :, j], "ZX%d" % t, (0, 80, j, j + 1), None, 80, "ZX%d" % t), b("ZF", q0, q0 + 80))
    tt(b("YY", 0, 13), b("AP", 0, 13), b("KFR", 0, 13), OP.max)
    decide(0, b("YY", 0, 13), b("D", 80, 288))
    send("U2D", b("DT0"), {"U2D": HOP + UX})

    ts(b("UU", 0, 13), CS, float(OKB + S), OP.is_ge)
    scat("HT", WT, "DT0", 13, z0)
    wrap("HT")
    send("F3", b("HT", 0, S), {"F3": F3L})
    lanes(1, 13, 288, b("QV", 80, 288))
    aff(b("TB"), b("TS"), -1.0 / KQ, 80 - BIG + 0.5 / KQ)

    def update1():
        send("V3Z", b("ZL1", 0, L), {"V3Z": 2 * HOP + 1.0})
        scat("F2", WT, "U2D", 13, b("U2Z"))
        wrap("F2")

    def later1(yy):
        scat("OC", WT, "DT0", 13, b("FQ", 80, 288))
        ts(b("PL1", 13, 21), b("FW", 13, 21), b("TB"), OP.add)
        decide(1, yy, b("LVW", 0, L))
    step(1, "F2", update1, later1)
    send("V3D", b("DT1"), {"V3D": 2 * HOP + VX})

    ts(b("UL", 0, 13), CS, float(OKB + S), OP.is_ge)
    ts(b("UU", 0, 5), b("PF", 224, 229), float(OKB + S), OP.is_ge)
    act(b("LVF", 0, L), ind(b("T01"), b("UL", 0, 13)))
    act(b("UF", 0, 336), ind(b("LVF", 80, 1104), b("PL1", 0, 21)))
    scat("OC", WT, "DT1", 13, b("LF1"))
    tt(b("OQ"), ind(b("OC"), b("DT0", 0, 13)), b("FM"), OP.is_equal)
    scan(b("BX", 0, L), b("RKM"), b("OQ"), OP.mult, OP.add)
    scat("HT", WT, "DT1", 13, b("ZL1", 0, L))
    wrap("HT")
    mms(*[(b("PH", 288, 309), b("WMU", 15 - m, 143 - m), b("UF", m, 336, 16), m == 0, m == 15) for m in range(16)])
    tt(b("UU", 5, 26), b("PH", 288, 309), b("BX", 15, 336, 16), OP.is_ge)
    ts(b("BU", 0, 13), b("BX", 15, L, 16), 0.5, OP.is_lt)
    act(b("BP", 0, L), ind(b("T01"), b("BU", 0, 13)))
    lanes(2, 26, 416, b("QV"))
    act(b("GW", 0, 336), ind(b("LVW", 80, 1104), b("PL1", 0, 21)))
    act(b("D", 0, 80), b("LVW", 0, 80))
    mms(*[(b3("T5", 0, 21), b("ID"), x, i == 0, i == 2)
          for i, x in enumerate((b("D", 80, 416), b("GW", 0, 336), b("BP")))])
    act(b("D", 80, 416), b3("T5", 0, 21))

    def update2():
        scat("F3", WT, "V3D", 13, b("V3Z"))
        wrap("F3")
        aff(b("TB"), b("TS"), -1.0 / KQ, 0.5 / KQ - BIG)
        ts(b("PL2", 26, 34), b("FW", 26, 34), b("TB"), OP.add)

    def later2(yy):
        decide(2, yy, b("LVW", 0, L))
        tt(b("OQ"), ind(b("OC", 0, S + 16), b("IX", 0, 13)), b("M16"), OP.mult)
        scan(b("OX"), b("RKM"), b("OQ"), OP.mult, OP.add)
        occ = b("OX", 15, L, 16)
        ts(b("Q1", 0, 13), occ, 544.0, OP.is_ge, -float(F), OP.mult)
        ts(b("Q2", 0, 13), occ, 0.0, OP.is_lt, BIG, OP.mult)
        tt(b("Q1", 0, 13), b("Q1", 0, 13), occ, OP.add)
        ts(b("QI", 0, 13), b("Q1", 0, 13), 80.0, OP.add)
        tt(b("Q2", 0, 13), b("Q2", 0, 13), b("Q1", 0, 13), OP.add)
        ts(b("Q3", 0, 13), b("Q2", 0, 13), float(OKB + S + 80), OP.add)
        act(b("VB"), ind(b("D"), b("QI", 0, 13)), AF.Copy, 1.0, 1.0)
        act(b("GW"), ind(b("LVW", 80, 1104), b("PL2", 0, 34)))
        act(b("DF", 544, F), b("LVW", 0, 80))
        for x, lo, hi in (("T0", 0, 512), ("T1", 512, 544)):
            out = cols(x, hi - lo)
            mms((out, b("ID"), b("D", lo, hi), True, False), (out, b("ID"), b("GW", lo, hi), False, True))
            act(b("DF", lo, hi), out)
    step(2, "F3", update2, later2)

    scat("HT", WT, "DT2", 13, b("ZL2", 0, L))
    store("S", T.yt[:, :], b("HT", 0, S), "yt")
    tt(b("Q1", 0, 13), CS, b("Q3", 0, 13), OP.max)
    tt(b("Q2", 0, 13), b("Q1", 0, 13), b("DUQ", 0, 13), OP.min)
    ts(b("BL", 0, 13), b("Q2", 0, 13), float(OKB + S), OP.subtract)
    scat("OC", WT, "DT2", 13, b("LF2"))
    store("A", T.yo[:, :], (T.OC[0:128:16, 0:S], "OC", (0, 1, 0, S), None, S), "yo")
    scat("DF", F + L, "BL", 13, b("VB"))
    store("S", T.yd[:, 0:544], (T.DF[0:128:16, 80:F], "DF", (0, 1, 80, F), None, 544), "yd")
    store("A", T.yd[:, 544:F], (T.DF[0:128:16, 0:80], "DF", (0, 1, 0, 80), None, 80), "ye")
    issue()
    for s in sorted(SEMAPHORES, key=lambda x: (x[:2] == "o_", x[0] == "q")):
        if s in cnt and know["G"].get(s, 0) < cnt[s]:
            g.wait_ge(T.sem[s], cnt[s])
